import numpy as np
import ml_dtypes


def mxq(x, axis, fmt="e4m3"):
    dtype, down = {"e4m3": (ml_dtypes.float8_e4m3fn, 7), "e5m2": (ml_dtypes.float8_e5m2, 14)}[fmt]
    v = np.moveaxis(np.asarray(x, np.float32).astype(ml_dtypes.bfloat16).astype(np.float64), axis, -1)
    blocks = v.reshape(v.shape[:-1] + (-1, 32))
    amax = np.abs(blocks).max(-1, keepdims=True)
    byte = np.maximum(np.where(amax > 0, np.frexp(amax)[1] - 1 + 127, 0) - down, 1)
    scale = np.exp2(byte - 127.0)
    codes = (blocks / scale).astype(np.float32).astype(dtype).astype(np.float64)
    return np.moveaxis((codes * scale).reshape(v.shape), -1, axis)


WIDE = False


def mx_kscale(k):
    if not WIDE:
        return np.ones(k)
    levels = np.array([10, -10, 5, -5, 0])
    if k % 512:
        return np.exp2(np.random.permutation(np.resize(levels, k // 32))).repeat(32)
    a = np.empty((k // 512, 16))
    for p in range(k // 512):
        a[p, :8] = np.random.permutation(np.resize(levels, 8))
        for g in range(8):
            far = levels[np.abs(levels - a[p, g]) >= 10]
            a[p, g + 8] = far[np.random.randint(len(far))]
    return np.exp2(a.ravel()).repeat(32)


def f64(x):
    return np.asarray(x).astype(np.float64)


def striped(idx):
    return np.tile(idx.reshape(-1, 16).T, (8, 1)).astype(np.uint16)


def unstriped(offs):
    return offs[:16].T.reshape(-1).astype(np.int64)


E2M1 = np.array([0.0, 0.5, 1.0, 1.5, 2.0, 3.0, 4.0, 6.0, -0.0, -0.5, -1.0, -1.5, -2.0, -3.0, -4.0, -6.0])


def pack_weight(w, fmt):
    k, n = w.shape
    w = f64(np.asarray(w, np.float32).astype(ml_dtypes.bfloat16)).reshape(k // 32, 32, n)
    amax = np.abs(w).max(1)
    if fmt == "e4m3":
        byte = np.frexp(amax)[1] - 1 + 127 - 7
    else:
        mant, ex = np.frexp(amax / 6.0)
        byte = np.where(mant > 0.5, ex, ex - 1) + 127
    byte = np.clip(np.where(amax > 0, byte, 1), 1, 254)
    scaled = (w * np.exp2(127.0 - byte)[:, None, :]).reshape(k, n).astype(np.float32)
    by_word = np.ascontiguousarray(scaled.reshape(k // 512, 128, 4, n).transpose(0, 1, 3, 2))
    if fmt == "e4m3":
        words = by_word.astype(ml_dtypes.float8_e4m3fn).view(np.uint8)
    else:
        c = by_word.astype(ml_dtypes.float4_e2m1fn).view(np.uint8) & 0xF
        words = (c[..., 0::2] | (c[..., 1::2] << 4)).reshape(k // 512, 128, 2 * n)
    return np.ascontiguousarray(words), np.ascontiguousarray(byte.astype(np.uint8).reshape(k // 512, 16, n))


def unpack_weight(words, scales, fmt):
    g, _, n = scales.shape
    words = np.ascontiguousarray(words).reshape(g, 128, n, -1)
    if fmt == "e4m3":
        vals = words.view(ml_dtypes.float8_e4m3fn).astype(np.float64)
    else:
        nib = np.empty((g, 128, n, 4), np.uint8)
        nib[..., 0::2] = words & 0xF
        nib[..., 1::2] = words >> 4
        vals = E2M1[nib]
    vals = vals * np.repeat(np.exp2(scales.astype(np.float64) - 127.0), 8, axis=1)[..., None]
    return vals.transpose(0, 1, 3, 2).reshape(g * 512, n)


def gelu(v):
    return 0.5 * v * (1.0 + np.tanh(np.sqrt(2.0 / np.pi) * (v + 0.044715 * v**3)))


K, H, N, T, S = 1024, 512, 256, 2048, 1024

def setup_inputs():
    n = np.random.standard_normal
    s = mx_kscale(K)[:, None]
    u = mx_kscale(H)[:, None]
    tab_words, tab_scales = pack_weight(n((K, T)) * s, "e4m3")
    w1 = (n((K, H)) / np.sqrt(K) / s * u.T).astype(np.float32)
    w2_words, w2_scales = pack_weight(n((K, H)) / np.sqrt(K) / s * u.T, "e2m1")
    w3_words, w3_scales = pack_weight(n((K, H)) / np.sqrt(K) / s * u.T, "e4m3")
    w4 = (n((H, N)) / np.sqrt(H) / u).astype(np.float32)
    b = (0.5 * n(N)).astype(np.float32)
    return dict(tab_words=tab_words, tab_scales=tab_scales,
                offs=striped(np.random.permutation(T)[:S]),
                offs2=striped(np.random.permutation(T)[:S]),
                offs3=striped(np.random.permutation(T)[:S]),
                w1=w1, w2_words=w2_words, w2_scales=w2_scales,
                w3_words=w3_words, w3_scales=w3_scales, w4=w4, b=b)

def reference(tab_words, tab_scales, offs, offs2, offs3, w1, w2_words, w2_scales, w3_words, w3_scales, w4, b):
    v = unpack_weight(tab_words, tab_scales, "e4m3")[:, unstriped(offs)]
    v2 = unpack_weight(tab_words, tab_scales, "e4m3")[:, unstriped(offs2)]
    v3 = unpack_weight(tab_words, tab_scales, "e4m3")[:, unstriped(offs3)]
    w2 = unpack_weight(w2_words, w2_scales, "e2m1")
    w3 = unpack_weight(w3_words, w3_scales, "e4m3")
    p = mxq(f64(w1), 0, "e4m3").T @ v
    c = w2.T @ v2
    d = w3.T @ v3
    h = np.maximum(p + np.abs(c - d), 0.0)
    y = mxq(f64(w4), 0, "e4m3").T @ mxq(h, 0, "e4m3")
    return y + f64(b)[:, None]

@@ -1,0 +1,255 @@
+from contextlib import ExitStack
+
+import concourse.mybir as mybir
+
+K, H, N, T, S = 1024, 512, 256, 2048, 1024
+FLOPS = 2 * S * H * (3 * K + N)
+
+F32 = mybir.dt.float32
+BF16 = mybir.dt.bfloat16
+I32 = mybir.dt.int32
+U32 = mybir.dt.uint32
+U16 = mybir.dt.uint16
+U8 = mybir.dt.uint8
+FP8X4 = mybir.dt.float8_e4m3fn_x4
+FP4X4 = mybir.dt.float4_e2m1fn_x4
+ACT = mybir.ActivationFunctionType
+ALU = mybir.AluOpType
+
+P = 128
+SUB = 128
+
+
+def tile_list_citation_topic_scores_kernel(
+    tc, tab_words, tab_scales, offs, offs2, offs3, w1, w2_words, w2_scales, w3_words, w3_scales, w4, b, out
+):
+    nc = tc.nc
+    with ExitStack() as ctx:
+        lists = ctx.enter_context(tc.tile_pool(name="lists", bufs=1))
+        keep = ctx.enter_context(tc.tile_pool(name="keep", bufs=1))
+        ring = ctx.enter_context(tc.tile_pool(name="ring", bufs=3))
+        psum = ctx.enter_context(tc.psum_pool(name="psum", bufs=1))
+
+        o1 = lists.tile([P, S // 16], U16, name="o1")
+        o2 = lists.tile([P, S // 16], U16, name="o2")
+        o3 = lists.tile([P, S // 16], U16, name="o3")
+
+        def kt(shape, dtype, name):
+            return keep.tile(shape, dtype, name=name, align_bytes=64)
+
+        tabw = [kt([P, T], I32, "tabw%d" % a) for a in range(2)]
+        tabs_a = kt([P, T // 4], I32, "tabs_a")
+        wsc_raw = kt([P, 3, H // 4], I32, "wsc_raw")
+        wsc = kt([P, 3, H], U8, "wsc")
+        w2_raw = kt([P, 2, H // 2], I32, "w2_raw")
+        w2c = kt([P, 2, 2 * H], U8, "w2c")
+        w3_raw = kt([P, 2, H], I32, "w3_raw")
+        w3c = kt([P, 2, H], I32, "w3c")
+        w1_raw = [kt([P, 4, H], F32, "w1_raw%d" % a) for a in range(2)]
+        w1_bf = [kt([P, 4 * H], BF16, "w1_bf%d" % a) for a in range(2)]
+        w1c = kt([P, 2, H], U32, "w1c")
+        w1s = kt([P, 2, H], U8, "w1s")
+        w4_raw = kt([P, 4, N], F32, "w4_raw")
+        w4_bf = kt([P, 4 * N], BF16, "w4_bf")
+        w4c = kt([P, N], U32, "w4c")
+        w4s = kt([P, N], U8, "w4s")
+        bias = kt([P, 2], F32, "bias")
+        gw = {}
+        pair = ctx.enter_context(tc.tile_pool(name="pair", bufs=3))
+        gs = {l: kt([P, S], U8, "gs%d" % l) for l in (1, 2, 3)}
+        gs2b = kt([P, S // 4], I32, "gs2b")
+        dist = [kt([P, SUB, 4], F32, "dist%d" % u) for u in range(S // SUB)]
+        hsum = kt([P, 4 * S], BF16, "hsum")
+        hbf = kt([P, 4 * S], BF16, "hbf")
+        hc = kt([P, S], U32, "hc")
+        hs = kt([P, S], U8, "hs")
+        offt = {1: o1, 2: o2, 3: o3}
+
+        tsc = tab_scales.bitcast(I32)
+        w2sc = w2_scales.bitcast(I32)
+        w3sc = w3_scales.bitcast(I32)
+
+        def load_table(a):
+            nc.sync.dma_start(out=tabw[a][:], in_=tab_words[a].rearrange("p t i -> p (t i)").bitcast(I32))
+
+        def load_w1(a):
+            nc.sync.dma_start(out=w1_raw[a][:], in_=w1[512 * a : 512 * (a + 1), :].rearrange("(p j) r -> p j r", j=4))
+
+        nc.vector.memset(tabs_a[:], 0)
+        nc.vector.memset(wsc_raw[:], 0)
+        nc.vector.memset(gs2b[:], 0)
+        nc.sync.dma_start(o2[:], offs2)
+        for q in range(4):
+            nc.sync.dma_start(out=tabs_a[32 * q : 32 * q + 8, :], in_=tsc[:, 4 * q : 4 * q + 4, :])
+            nc.gpsimd.dma_start(out=wsc_raw[32 * q : 32 * q + 8, 2, :], in_=w3sc[:, 4 * q : 4 * q + 4, :])
+        nc.sync.dma_start(o3[:], offs3)
+        load_table(0)
+        nc.sync.dma_start(out=w3_raw[:], in_=w3_words.rearrange("a p e i -> p a (e i)").bitcast(I32))
+        for q in range(4):
+            nc.sync.dma_start(
+                out=wsc_raw[32 * q : 32 * q + 4, 0:2, :], in_=w2sc[:, 4 * q : 4 * q + 4, :].rearrange("a r e -> r a e")
+            )
+        nc.sync.dma_start(out=w2_raw[:], in_=w2_words.rearrange("a p e -> p a e").bitcast(I32))
+        load_w1(0)
+        load_table(1)
+        nc.sync.dma_start(o1[:], offs)
+        load_w1(1)
+        w4v = w4.rearrange("(g t i) n -> t g i n", t=4, i=8)
+        for t in range(4):
+            nc.sync.dma_start(out=w4_raw[:, t, :], in_=w4v[t])
+        nc.sync.dma_start(out=bias[:], in_=b.rearrange("(p c) -> p c", c=2))
+
+        def shift_scales():
+            nc.gpsimd.dma_start(out=gs2b[0:124, :], in_=gs[2][4:128, :].bitcast(I32))
+
+        def gather_words(l, a, j0, n):
+            gw[l, a, j0 // 256] = pair.tile([P, 256], U32, name="gw%d%d" % (l, a), align_bytes=64)
+            nc.vector.tensor_copy(
+                gw[l, a, j0 // 256][:], tabw[a][:].bitcast(U32).indirect(offt[l][:, j0 // 16 : (j0 + n) // 16])
+            )
+
+        def gather_scales(dst, src, l, j0, n):
+            nc.vector.tensor_copy(dst[:, j0 : j0 + n], src[:].bitcast(U8).indirect(offt[l][:, j0 // 16 : (j0 + n) // 16]))
+
+        def cast_w1(a):
+            src = w1_raw[a][:].rearrange("p j (g t i) -> p t g i j", t=4, i=8)
+            dst = w1_bf[a][:].rearrange("p (t g i j) -> p t g i j", t=4, i=8, j=4)
+            for t in range(4):
+                if a == 1 and t >= 2:
+                    nc.gpsimd.tensor_copy(out=dst[:, t], in_=src[:, t])
+                else:
+                    nc.scalar.activation(out=dst[:, t], in_=src[:, t], func=ACT.Copy)
+
+        def quant_w1(a):
+            nc.vector.quantize_mx(out=w1c[:, a, :].bitcast(FP8X4), scales=w1s[:, a, :], in_=w1_bf[a][:])
+
+        def permute_weights():
+            nc.vector.tensor_copy(
+                out=wsc[:].bitcast(I32).rearrange("p a (t g i) -> p a t g i", t=4, i=2),
+                in_=wsc_raw[:].rearrange("p a (g t i) -> p a t g i", t=4, i=2),
+            )
+            nc.vector.tensor_copy(
+                out=w3c[:].rearrange("p a (t g i) -> p a t g i", t=4, i=8),
+                in_=w3_raw[:].rearrange("p a (g t i) -> p a t g i", t=4, i=8),
+            )
+            nc.vector.tensor_copy(
+                out=w2c[:].bitcast(I32).rearrange("p a (t g i) -> p a t g i", t=4, i=4),
+                in_=w2_raw[:].rearrange("p a (g t i) -> p a t g i", t=4, i=4),
+            )
+
+        def product(l, u, bank):
+            tok = slice(u * SUB, (u + 1) * SUB)
+            for t in range(4):
+                col = slice(t * P, (t + 1) * P)
+                for a in range(2):
+                    if l == 1:
+                        lhs, lsc, rsc = w1c[:, a, col].bitcast(FP8X4), w1s[:, a, col], gs[1][4 * a :, tok]
+                    elif l == 2:
+                        lhs = w2c[:, a, 2 * t * P : 2 * (t + 1) * P].bitcast(FP4X4)
+                        lsc, rsc = wsc[:, a, col], (gs[2][:] if a == 0 else gs2b[:].bitcast(U8))[:, tok]
+                    else:
+                        lhs, lsc, rsc = w3c[:, a, col].bitcast(FP8X4), wsc[4 * a :, 2, col], gs[3][4 * a :, tok]
+                    nc.tensor.matmul_mx(
+                        out=bank[:, t, :], lhsT=lhs, lhsT_scale=lsc, rhs=gw[l, a, u // 2][:, (u % 2) * SUB : (u % 2 + 1) * SUB].bitcast(FP8X4), rhs_scale=rsc,
+                        start=(a == 0), stop=(a == 1),
+                    )
+
+        def woven(bank):
+            return bank[:].rearrange("p t n -> p n t")
+
+        def distance(u):
+            span = slice(4 * u * SUB, 4 * (u + 1) * SUB)
+            cb = psum.tile([P, 4, SUB], F32, name="cb", tag="cd", bufs=6)
+            db = psum.tile([P, 4, SUB], F32, name="db", tag="cd", bufs=6)
+            product(3, u, db)
+            product(2, u, cb)
+            dsb = ring.tile([P, SUB, 4], F32, name="dsb")
+            diff = ring.tile([P, SUB, 4], F32, name="diff")
+            nc.scalar.activation(out=dsb[:], in_=woven(db), func=ACT.Copy)
+            csb = ring.tile([P, SUB, 4], F32, name="csb")
+            nc.scalar.activation(out=csb[:], in_=woven(cb), func=ACT.Copy)
+            nc.gpsimd.tensor_tensor(out=diff[:], in0=csb[:], in1=dsb[:], op=ALU.subtract)
+            nc.scalar.activation(out=dist[u][:], in_=diff[:], func=ACT.Abs)
+
+        def hidden_sum(u):
+            span = slice(4 * u * SUB, 4 * (u + 1) * SUB)
+            pb = psum.tile([P, 4, SUB], F32, name="pb", bufs=2)
+            product(1, u, pb)
+            nc.vector.tensor_tensor(
+                out=hsum[:, span].rearrange("p (n t) -> p n t", t=4), in0=woven(pb),
+                in1=dist[u][:], op=ALU.add,
+            )
+
+        def relu(j0, n):
+            span = slice(4 * j0, 4 * (j0 + n))
+            nc.vector.tensor_scalar(out=hbf[:, span], in0=hsum[:, span], scalar1=0.0, scalar2=None, op0=ALU.max)
+
+        def quant_h(j0, n):
+            nc.vector.quantize_mx(
+                out=hc[:, j0 : j0 + n].bitcast(FP8X4), scales=hs[:, j0 : j0 + n], in_=hbf[:, 4 * j0 : 4 * (j0 + n)]
+            )
+
+        outv = out.rearrange("(p c) s -> p c s", c=2)
+
+        def classes(j0, n):
+            yb = psum.tile([P, 2, 256], F32, name="yb", tag="cd", bufs=6)
+            ysb = ring.tile([P, 2, 256], F32, name="ysb")
+            for c in range(2):
+                col = slice(c * P, (c + 1) * P)
+                nc.tensor.matmul_mx(
+                    out=yb[:, c, :n], lhsT=w4c[:, col].bitcast(FP8X4), lhsT_scale=w4s[:, col],
+                    rhs=hc[:, j0 : j0 + n].bitcast(FP8X4), rhs_scale=hs[:, j0 : j0 + n], start=True, stop=True,
+                )
+            for c in range(2):
+                nc.scalar.activation(out=ysb[:, c, :n], in_=yb[:, c, :n], func=ACT.Identity, bias=bias[:, c : c + 1])
+            nc.sync.dma_start(out=outv[:, :, j0 : j0 + n], in_=ysb[:, :, :n])
+
+        def cast_w4():
+            nc.gpsimd.tensor_copy(
+                out=w4_bf[:].rearrange("p (c m t) -> p c m t", c=2, t=4),
+                in_=w4_raw[:].rearrange("p t (m c) -> p c m t", c=2),
+            )
+
+        def quant_w4():
+            nc.vector.quantize_mx(out=w4c[:].bitcast(FP8X4), scales=w4s[:], in_=w4_bf[:])
+
+        gather_scales(gs[2], tabs_a, 2, 0, 1024)
+        shift_scales()
+        gather_scales(gs[3], tabs_a, 3, 0, 1024)
+        cast_w1(0)
+        for q in range(4):
+            for a in range(2):
+                for l in (3, 2):
+                    gather_words(l, a, 256 * q, 256)
+            if q == 0:
+                permute_weights()
+            distance(2 * q)
+            distance(2 * q + 1)
+            if q == 0:
+                cast_w1(1)
+                cast_w4()
+            if q == 1:
+                quant_w1(0)
+                gather_scales(gs[1], tabs_a, 1, 0, 1024)
+        quant_w1(1)
+        quant_w4()
+        for a in range(2):
+            gather_words(1, a, 0, 256)
+        for q in range(4):
+            if q < 3:
+                gather_words(1, 0, 256 * (q + 1), 256)
+            if q > 0:
+                relu(256 * (q - 1), 256)
+            if q < 3:
+                gather_words(1, 1, 256 * (q + 1), 256)
+            hidden_sum(2 * q)
+            if q > 0:
+                quant_h(256 * (q - 1), 256)
+                classes(256 * (q - 1), 256)
+            hidden_sum(2 * q + 1)
+        relu(768, 128)
+        relu(896, 128)
+        quant_h(768, 128)
+        quant_h(896, 128)
+        classes(768, 128)
+        classes(896, 128)

@@ -1,6 +1,7 @@
 from contextlib import ExitStack
 
 import concourse.mybir as mybir
+from concourse.masks import make_identity
 
 K, H, N, T, S = 1024, 512, 256, 2048, 1024
 FLOPS = 2 * S * H * (3 * K + N)
@@ -17,7 +18,22 @@ ACT = mybir.ActivationFunctionType
 ALU = mybir.AluOpType
 
 P = 128
-SUB = 128
+PACK = 4
+RUN = 8
+PASSES = K // (P * PACK)
+QUADS = 4
+TILE = 128
+TILES = S // TILE
+PAIR = 2 * TILE
+OWN, FIRST, LAST = "own", "first", "last"
+
+CITED_CUTS = ((0, 256), (256, 256), (512, 512))
+OWN_CUTS = ((0, 256), (256, 768))
+WORD_SLOTS = {(OWN, 0): 3, (OWN, 1): 3, (FIRST, 0): 2, (FIRST, 1): 3, (LAST, 0): 2, (LAST, 1): 3}
+STAGE_SLOTS = 4
+CITED_BANKS, DIFF_BANKS, OWN_BANKS = 3, 2, 3
+CITED_LEAD = 1
+OWN_LAG = 6
 
 
 def tile_list_citation_topic_scores_kernel(
@@ -27,229 +43,246 @@ def tile_list_citation_topic_scores_kernel(
     with ExitStack() as ctx:
         lists = ctx.enter_context(tc.tile_pool(name="lists", bufs=1))
         keep = ctx.enter_context(tc.tile_pool(name="keep", bufs=1))
-        ring = ctx.enter_context(tc.tile_pool(name="ring", bufs=3))
+        ring = ctx.enter_context(tc.tile_pool(name="ring", bufs=STAGE_SLOTS))
         psum = ctx.enter_context(tc.psum_pool(name="psum", bufs=1))
 
-        o1 = lists.tile([P, S // 16], U16, name="o1")
-        o2 = lists.tile([P, S // 16], U16, name="o2")
-        o3 = lists.tile([P, S // 16], U16, name="o3")
+        offsets = {name: lists.tile([P, S // 16], U16, name="offsets_" + name) for name in (OWN, FIRST, LAST)}
 
-        def kt(shape, dtype, name):
+        def kept(shape, dtype, name):
             return keep.tile(shape, dtype, name=name, align_bytes=64)
 
-        tabw = [kt([P, T], I32, "tabw%d" % a) for a in range(2)]
-        tabs_a = kt([P, T // 4], I32, "tabs_a")
-        wsc_raw = kt([P, 3, H // 4], I32, "wsc_raw")
-        wsc = kt([P, 3, H], U8, "wsc")
-        w2_raw = kt([P, 2, H // 2], I32, "w2_raw")
-        w2c = kt([P, 2, 2 * H], U8, "w2c")
-        w3_raw = kt([P, 2, H], I32, "w3_raw")
-        w3c = kt([P, 2, H], I32, "w3c")
-        w1_raw = [kt([P, 4, H], F32, "w1_raw%d" % a) for a in range(2)]
-        w1_bf = [kt([P, 4 * H], BF16, "w1_bf%d" % a) for a in range(2)]
-        w1c = kt([P, 2, H], U32, "w1c")
-        w1s = kt([P, 2, H], U8, "w1s")
-        w4_raw = kt([P, 4, N], F32, "w4_raw")
-        w4_bf = kt([P, 4 * N], BF16, "w4_bf")
-        w4c = kt([P, N], U32, "w4c")
-        w4s = kt([P, N], U8, "w4s")
-        bias = kt([P, 2], F32, "bias")
-        gw = {}
-        pair = ctx.enter_context(tc.tile_pool(name="pair", bufs=3))
-        gs = {l: kt([P, S], U8, "gs%d" % l) for l in (1, 2, 3)}
-        gs2b = kt([P, S // 4], I32, "gs2b")
-        dist = [kt([P, SUB, 4], F32, "dist%d" % u) for u in range(S // SUB)]
-        hsum = kt([P, 4 * S], BF16, "hsum")
-        hbf = kt([P, 4 * S], BF16, "hbf")
-        hc = kt([P, S], U32, "hc")
-        hs = kt([P, S], U8, "hs")
-        offt = {1: o1, 2: o2, 3: o3}
+        table_words = [kept([P, T], I32, "table_words%d" % a) for a in range(PASSES)]
+        table_scales = kept([P, T // 4], I32, "table_scales")
+        weight_scales = kept([P, 3, H // 4], I32, "weight_scales")
+        w2_codes = kept([P, PASSES, H // 2], I32, "w2_codes")
+        identity = kept([P, P], F32, "identity")
+        w3_codes = kept([P, PASSES, H], I32, "w3_codes")
+        w1_raw = [kept([P, PACK, H], F32, "w1_raw%d" % a) for a in range(PASSES)]
+        w1_bf16 = [kept([P, PACK * H], BF16, "w1_bf16_%d" % a) for a in range(PASSES)]
+        w1_codes = kept([P, PASSES, H], U32, "w1_codes")
+        w1_scales = kept([P, PASSES, H], U8, "w1_scales")
+        w4_raw = kept([P, PACK, N], F32, "w4_raw")
+        w4_bf16 = kept([P, PACK * N], BF16, "w4_bf16")
+        w4_codes = kept([P, N], U32, "w4_codes")
+        w4_scales = kept([P, N], U8, "w4_scales")
+        bias = kept([P, 2], F32, "bias")
+        picks = ctx.enter_context(tc.tile_pool(name="picks", bufs=2))
+        picked_scales = {name: kept([P, S], U8, "picked_scales_" + name) for name in (OWN, FIRST, LAST)}
+        first_scales_pass1 = kept([P, S // 4], I32, "first_scales_pass1")
+        distance = [kept([P, TILE, PACK], F32, "distance%d" % u) for u in range(TILES)]
+        h_sum = kept([P, PACK * S], BF16, "h_sum")
+        h_bf16 = kept([P, PACK * S], BF16, "h_bf16")
+        h_codes = kept([P, S], U32, "h_codes")
+        h_scales = kept([P, S], U8, "h_scales")
+        picked_words = {}
+        staged = {}
 
-        tsc = tab_scales.bitcast(I32)
-        w2sc = w2_scales.bitcast(I32)
-        w3sc = w3_scales.bitcast(I32)
 
-        def load_table(a):
-            nc.sync.dma_start(out=tabw[a][:], in_=tab_words[a].rearrange("p t i -> p (t i)").bitcast(I32))
+        def load_table_words(a):
+            nc.sync.dma_start(out=table_words[a][:], in_=tab_words[a].rearrange("p t i -> p (t i)").bitcast(I32))
 
-        def load_w1(a):
-            nc.sync.dma_start(out=w1_raw[a][:], in_=w1[512 * a : 512 * (a + 1), :].rearrange("(p j) r -> p j r", j=4))
+        def load_table_scales(q):
+            rows = tab_scales.bitcast(I32)[:, 4 * q : 4 * q + 4, :]
+            nc.sync.dma_start(out=table_scales[32 * q : 32 * q + 8, :], in_=rows)
 
-        nc.vector.memset(tabs_a[:], 0)
-        nc.vector.memset(wsc_raw[:], 0)
-        nc.vector.memset(gs2b[:], 0)
-        nc.sync.dma_start(o2[:], offs2)
-        for q in range(4):
-            nc.sync.dma_start(out=tabs_a[32 * q : 32 * q + 8, :], in_=tsc[:, 4 * q : 4 * q + 4, :])
-            nc.gpsimd.dma_start(out=wsc_raw[32 * q : 32 * q + 8, 2, :], in_=w3sc[:, 4 * q : 4 * q + 4, :])
-        nc.sync.dma_start(o3[:], offs3)
-        load_table(0)
-        nc.sync.dma_start(out=w3_raw[:], in_=w3_words.rearrange("a p e i -> p a (e i)").bitcast(I32))
-        for q in range(4):
-            nc.sync.dma_start(
-                out=wsc_raw[32 * q : 32 * q + 4, 0:2, :], in_=w2sc[:, 4 * q : 4 * q + 4, :].rearrange("a r e -> r a e")
+        def load_w3_scales(q):
+            rows = w3_scales.bitcast(I32)[:, 4 * q : 4 * q + 4, :]
+            nc.sync.dma_start(out=weight_scales[32 * q : 32 * q + 8, 2, :], in_=rows)
+
+        def load_w2_scales(q):
+            rows = w2_scales.bitcast(I32)[:, 4 * q : 4 * q + 4, :].rearrange("a r e -> r a e")
+            nc.sync.dma_start(out=weight_scales[32 * q : 32 * q + 4, 0:2, :], in_=rows)
+
+
+        def gather_scales(name):
+            window = table_scales[:].bitcast(U8)
+            nc.vector.tensor_copy(picked_scales[name][:, 0:S], window.indirect(offsets[name][:, 0 : S // 16]))
+
+        def gather_words(name, a, start, count):
+            words = picks.tile(
+                [P, count], U32, name="words_%s%d" % (name, a), align_bytes=64, bufs=WORD_SLOTS[name, a]
             )
-        nc.sync.dma_start(out=w2_raw[:], in_=w2_words.rearrange("a p e -> p a e").bitcast(I32))
-        load_w1(0)
-        load_table(1)
-        nc.sync.dma_start(o1[:], offs)
-        load_w1(1)
-        w4v = w4.rearrange("(g t i) n -> t g i n", t=4, i=8)
-        for t in range(4):
-            nc.sync.dma_start(out=w4_raw[:, t, :], in_=w4v[t])
-        nc.sync.dma_start(out=bias[:], in_=b.rearrange("(p c) -> p c", c=2))
+            window = table_words[a][:].bitcast(U32)
+            nc.vector.tensor_copy(words[:], window.indirect(offsets[name][:, start // 16 : (start + count) // 16]))
+            for k in range(count // TILE):
+                picked_words[name, a, start // TILE + k] = words[:, k * TILE : (k + 1) * TILE]
 
-        def shift_scales():
-            nc.gpsimd.dma_start(out=gs2b[0:124, :], in_=gs[2][4:128, :].bitcast(I32))
+        def gather_cited_words(start, count):
+            for a in range(PASSES):
+                for name in (LAST, FIRST):
+                    gather_words(name, a, start, count)
 
-        def gather_words(l, a, j0, n):
-            gw[l, a, j0 // 256] = pair.tile([P, 256], U32, name="gw%d%d" % (l, a), align_bytes=64)
-            nc.vector.tensor_copy(
-                gw[l, a, j0 // 256][:], tabw[a][:].bitcast(U32).indirect(offt[l][:, j0 // 16 : (j0 + n) // 16])
-            )
 
-        def gather_scales(dst, src, l, j0, n):
-            nc.vector.tensor_copy(dst[:, j0 : j0 + n], src[:].bitcast(U8).indirect(offt[l][:, j0 // 16 : (j0 + n) // 16]))
+        def round_w1(a):
+            src = w1_raw[a][:].rearrange("p j (g t u i) -> p t g u j i", t=PACK, u=2, i=4)
+            dst = w1_bf16[a][:].rearrange("p (t g u i j) -> p t g u j i", t=PACK, u=2, i=4, j=PACK)
+            for t in range(PACK):
+                nc.vector.tensor_copy(out=dst[:, t], in_=src[:, t])
 
-        def cast_w1(a):
-            src = w1_raw[a][:].rearrange("p j (g t i) -> p t g i j", t=4, i=8)
-            dst = w1_bf[a][:].rearrange("p (t g i j) -> p t g i j", t=4, i=8, j=4)
-            for t in range(4):
-                if a == 1 and t >= 2:
-                    nc.gpsimd.tensor_copy(out=dst[:, t], in_=src[:, t])
-                else:
-                    nc.scalar.activation(out=dst[:, t], in_=src[:, t], func=ACT.Copy)
+        def quantize_w1(a):
+            nc.vector.quantize_mx(out=w1_codes[:, a, :].bitcast(FP8X4), scales=w1_scales[:, a, :], in_=w1_bf16[a][:])
 
-        def quant_w1(a):
-            nc.vector.quantize_mx(out=w1c[:, a, :].bitcast(FP8X4), scales=w1s[:, a, :], in_=w1_bf[a][:])
-
-        def permute_weights():
-            nc.vector.tensor_copy(
-                out=wsc[:].bitcast(I32).rearrange("p a (t g i) -> p a t g i", t=4, i=2),
-                in_=wsc_raw[:].rearrange("p a (g t i) -> p a t g i", t=4, i=2),
-            )
-            nc.vector.tensor_copy(
-                out=w3c[:].rearrange("p a (t g i) -> p a t g i", t=4, i=8),
-                in_=w3_raw[:].rearrange("p a (g t i) -> p a t g i", t=4, i=8),
-            )
-            nc.vector.tensor_copy(
-                out=w2c[:].bitcast(I32).rearrange("p a (t g i) -> p a t g i", t=4, i=4),
-                in_=w2_raw[:].rearrange("p a (g t i) -> p a t g i", t=4, i=4),
+        def round_w4():
+            nc.scalar.activation(
+                out=w4_bf16[:].rearrange("p (e m t) -> p e m t", e=2, t=PACK),
+                in_=w4_raw[:].rearrange("p t (m e) -> p e m t", e=2),
+                func=ACT.Copy,
             )
 
-        def product(l, u, bank):
-            tok = slice(u * SUB, (u + 1) * SUB)
-            for t in range(4):
-                col = slice(t * P, (t + 1) * P)
-                for a in range(2):
-                    if l == 1:
-                        lhs, lsc, rsc = w1c[:, a, col].bitcast(FP8X4), w1s[:, a, col], gs[1][4 * a :, tok]
-                    elif l == 2:
-                        lhs = w2c[:, a, 2 * t * P : 2 * (t + 1) * P].bitcast(FP4X4)
-                        lsc, rsc = wsc[:, a, col], (gs[2][:] if a == 0 else gs2b[:].bitcast(U8))[:, tok]
-                    else:
-                        lhs, lsc, rsc = w3c[:, a, col].bitcast(FP8X4), wsc[4 * a :, 2, col], gs[3][4 * a :, tok]
-                    nc.tensor.matmul_mx(
-                        out=bank[:, t, :], lhsT=lhs, lhsT_scale=lsc, rhs=gw[l, a, u // 2][:, (u % 2) * SUB : (u % 2 + 1) * SUB].bitcast(FP8X4), rhs_scale=rsc,
-                        start=(a == 0), stop=(a == 1),
-                    )
+        def quantize_w4():
+            nc.vector.quantize_mx(out=w4_codes[:].bitcast(FP8X4), scales=w4_scales[:], in_=w4_bf16[:])
 
-        def woven(bank):
+
+        def by_token(bank):
             return bank[:].rearrange("p t n -> p n t")
 
-        def distance(u):
-            span = slice(4 * u * SUB, 4 * (u + 1) * SUB)
-            cb = psum.tile([P, 4, SUB], F32, name="cb", tag="cd", bufs=6)
-            db = psum.tile([P, 4, SUB], F32, name="db", tag="cd", bufs=6)
-            product(3, u, db)
-            product(2, u, cb)
-            dsb = ring.tile([P, SUB, 4], F32, name="dsb")
-            diff = ring.tile([P, SUB, 4], F32, name="diff")
-            nc.scalar.activation(out=dsb[:], in_=woven(db), func=ACT.Copy)
-            csb = ring.tile([P, SUB, 4], F32, name="csb")
-            nc.scalar.activation(out=csb[:], in_=woven(cb), func=ACT.Copy)
-            nc.gpsimd.tensor_tensor(out=diff[:], in0=csb[:], in1=dsb[:], op=ALU.subtract)
-            nc.scalar.activation(out=dist[u][:], in_=diff[:], func=ACT.Abs)
-
-        def hidden_sum(u):
-            span = slice(4 * u * SUB, 4 * (u + 1) * SUB)
-            pb = psum.tile([P, 4, SUB], F32, name="pb", bufs=2)
-            product(1, u, pb)
-            nc.vector.tensor_tensor(
-                out=hsum[:, span].rearrange("p (n t) -> p n t", t=4), in0=woven(pb),
-                in1=dist[u][:], op=ALU.add,
-            )
-
-        def relu(j0, n):
-            span = slice(4 * j0, 4 * (j0 + n))
-            nc.vector.tensor_scalar(out=hbf[:, span], in0=hsum[:, span], scalar1=0.0, scalar2=None, op0=ALU.max)
-
-        def quant_h(j0, n):
-            nc.vector.quantize_mx(
-                out=hc[:, j0 : j0 + n].bitcast(FP8X4), scales=hs[:, j0 : j0 + n], in_=hbf[:, 4 * j0 : 4 * (j0 + n)]
-            )
-
-        outv = out.rearrange("(p c) s -> p c s", c=2)
-
-        def classes(j0, n):
-            yb = psum.tile([P, 2, 256], F32, name="yb", tag="cd", bufs=6)
-            ysb = ring.tile([P, 2, 256], F32, name="ysb")
-            for c in range(2):
-                col = slice(c * P, (c + 1) * P)
-                nc.tensor.matmul_mx(
-                    out=yb[:, c, :n], lhsT=w4c[:, col].bitcast(FP8X4), lhsT_scale=w4s[:, col],
-                    rhs=hc[:, j0 : j0 + n].bitcast(FP8X4), rhs_scale=hs[:, j0 : j0 + n], start=True, stop=True,
+        def cited_products(u):
+            tokens = slice(u * TILE, (u + 1) * TILE)
+            planes = weight_scales[:].bitcast(U8)
+            for name, sign in ((LAST, -1.0), (FIRST, 1.0)):
+                bank = psum.tile([P, H], F32, name="cited_bank", tag="cited", bufs=CITED_BANKS)
+                for a in range(PASSES):
+                    if name == FIRST:
+                        weight, weight_plane = w2_codes[:, a, :].bitcast(U8).bitcast(FP4X4), planes[:, a, :]
+                        plane = picked_scales[FIRST][:] if a == 0 else first_scales_pass1[:].bitcast(U8)
+                        token_plane = plane[:, tokens]
+                    else:
+                        weight, weight_plane = w3_codes[:, a, :].bitcast(FP8X4), planes[4 * a :, 2, :]
+                        token_plane = picked_scales[LAST][4 * a :, tokens]
+                    nc.tensor.matmul_mx(
+                        out=bank[:], lhsT=picked_words[name, a, u].bitcast(FP8X4), lhsT_scale=token_plane,
+                        rhs=weight, rhs_scale=weight_plane, start=(a == 0), stop=(a == PASSES - 1),
+                    )
+                staged[name, u] = ring.tile([P, PACK, H // (PACK * RUN), RUN], F32, name="staged_" + name)
+                nc.scalar.activation(
+                    out=staged[name, u][:], in_=bank[:].rearrange("p (g t i) -> p t g i", t=PACK, i=RUN),
+                    func=ACT.Copy, scale=sign,
                 )
-            for c in range(2):
-                nc.scalar.activation(out=ysb[:, c, :n], in_=yb[:, c, :n], func=ACT.Identity, bias=bias[:, c : c + 1])
-            nc.sync.dma_start(out=outv[:, :, j0 : j0 + n], in_=ysb[:, :, :n])
 
-        def cast_w4():
-            nc.gpsimd.tensor_copy(
-                out=w4_bf[:].rearrange("p (c m t) -> p c m t", c=2, t=4),
-                in_=w4_raw[:].rearrange("p t (m c) -> p c m t", c=2),
+        def absolute_difference(u):
+            bank = psum.tile([P, PACK, TILE], F32, name="diff_bank", bufs=DIFF_BANKS)
+            for t in range(PACK):
+                for name in (LAST, FIRST):
+                    nc.tensor.matmul(
+                        out=bank[:, t, :], lhsT=staged[name, u][:, t].rearrange("p g i -> p (g i)"), rhs=identity[:],
+                        start=(name == LAST), stop=(name == FIRST), is_transpose=True,
+                    )
+            nc.scalar.activation(out=distance[u][:], in_=by_token(bank), func=ACT.Abs)
+
+        def own_product_and_sum(u):
+            tokens = slice(u * TILE, (u + 1) * TILE)
+            bank = psum.tile([P, PACK, TILE], F32, name="own_bank", bufs=OWN_BANKS)
+            for t in range(PACK):
+                channels = slice(t * P, (t + 1) * P)
+                for a in range(PASSES):
+                    nc.tensor.matmul_mx(
+                        out=bank[:, t, :], lhsT=w1_codes[:, a, channels].bitcast(FP8X4),
+                        lhsT_scale=w1_scales[:, a, channels], rhs=picked_words[OWN, a, u].bitcast(FP8X4),
+                        rhs_scale=picked_scales[OWN][4 * a :, tokens], start=(a == 0), stop=(a == PASSES - 1),
+                    )
+            values = slice(PACK * u * TILE, PACK * (u + 1) * TILE)
+            nc.vector.tensor_tensor(
+                out=h_sum[:, values].rearrange("p (n t) -> p n t", t=PACK), in0=by_token(bank), in1=distance[u][:],
+                op=ALU.add,
             )
 
-        def quant_w4():
-            nc.vector.quantize_mx(out=w4c[:].bitcast(FP8X4), scales=w4s[:], in_=w4_bf[:])
+        def relu(start, count):
+            values = slice(PACK * start, PACK * (start + count))
+            nc.vector.tensor_scalar(out=h_bf16[:, values], in0=h_sum[:, values], scalar1=0.0, scalar2=None, op0=ALU.max)
 
-        gather_scales(gs[2], tabs_a, 2, 0, 1024)
-        shift_scales()
-        gather_scales(gs[3], tabs_a, 3, 0, 1024)
-        cast_w1(0)
-        for q in range(4):
-            for a in range(2):
-                for l in (3, 2):
-                    gather_words(l, a, 256 * q, 256)
-            if q == 0:
-                permute_weights()
-            distance(2 * q)
-            distance(2 * q + 1)
-            if q == 0:
-                cast_w1(1)
-                cast_w4()
-            if q == 1:
-                quant_w1(0)
-                gather_scales(gs[1], tabs_a, 1, 0, 1024)
-        quant_w1(1)
-        quant_w4()
-        for a in range(2):
-            gather_words(1, a, 0, 256)
-        for q in range(4):
-            if q < 3:
-                gather_words(1, 0, 256 * (q + 1), 256)
-            if q > 0:
-                relu(256 * (q - 1), 256)
-            if q < 3:
-                gather_words(1, 1, 256 * (q + 1), 256)
-            hidden_sum(2 * q)
-            if q > 0:
-                quant_h(256 * (q - 1), 256)
-                classes(256 * (q - 1), 256)
-            hidden_sum(2 * q + 1)
-        relu(768, 128)
-        relu(896, 128)
-        quant_h(768, 128)
-        quant_h(896, 128)
-        classes(768, 128)
-        classes(896, 128)
+        def quantize_h(start, count):
+            nc.vector.quantize_mx(
+                out=h_codes[:, start : start + count].bitcast(FP8X4), scales=h_scales[:, start : start + count],
+                in_=h_bf16[:, PACK * start : PACK * (start + count)],
+            )
+
+        def scores(start, count):
+            tokens = slice(start, start + count)
+            bank = psum.tile([P, 2, PAIR], F32, name="score_bank", tag="cited", bufs=CITED_BANKS)
+            result = ring.tile([P, 2, PAIR], F32, name="result")
+            for e in range(2):
+                classes = slice(e * P, (e + 1) * P)
+                nc.tensor.matmul_mx(
+                    out=bank[:, e, :count], lhsT=w4_codes[:, classes].bitcast(FP8X4), lhsT_scale=w4_scales[:, classes],
+                    rhs=h_codes[:, tokens].bitcast(FP8X4), rhs_scale=h_scales[:, tokens], start=True, stop=True,
+                )
+            for e in range(2):
+                nc.scalar.activation(
+                    out=result[:, e, :count], in_=bank[:, e, :count], func=ACT.Identity, bias=bias[:, e : e + 1]
+                )
+            nc.sync.dma_start(out=out.rearrange("(m e) s -> m e s", e=2)[:, :, tokens], in_=result[:, :, :count])
+
+
+        nc.vector.memset(table_scales[:], 0)
+        nc.vector.memset(weight_scales[:], 0)
+        nc.vector.memset(first_scales_pass1[:], 0)
+        make_identity(nc, identity[:])
+
+        nc.sync.dma_start(offsets[FIRST][:], offs2)
+        for q in range(QUADS):
+            load_table_scales(q)
+        nc.sync.dma_start(offsets[LAST][:], offs3)
+        for q in range(QUADS // 2):
+            load_w3_scales(q)
+        load_table_words(0)
+        for q in range(QUADS // 2, QUADS):
+            load_w3_scales(q)
+        for q in range(QUADS):
+            load_w2_scales(q)
+        nc.sync.dma_start(out=w3_codes[:], in_=w3_words.rearrange("a p e i -> p a (e i)").bitcast(I32))
+        load_table_words(1)
+        nc.sync.dma_start(out=w2_codes[:], in_=w2_words.rearrange("a p e -> p a e").bitcast(I32))
+
+        gather_scales(FIRST)
+        nc.sync.dma_start(out=first_scales_pass1[0:112, :], in_=picked_scales[FIRST][4:116, :].bitcast(I32))
+
+        for a in range(PASSES):
+            rows = w1[P * PACK * a : P * PACK * (a + 1), :]
+            nc.sync.dma_start(out=w1_raw[a][:], in_=rows.rearrange("(p j) r -> p j r", j=PACK))
+        nc.sync.dma_start(offsets[OWN][:], offs)
+        for t in range(PACK):
+            nc.sync.dma_start(out=w4_raw[:, t, :], in_=w4.rearrange("(g t i) n -> t g i n", t=PACK, i=RUN)[t])
+        nc.sync.dma_start(out=bias[:], in_=b.rearrange("(m e) -> m e", e=2))
+
+        gather_scales(LAST)
+        gather_cited_words(*CITED_CUTS[0])
+
+        def gather_first_own():
+            gather_scales(OWN)
+            for a in range(PASSES):
+                gather_words(OWN, a, *OWN_CUTS[0])
+
+        preparation = {
+            0: (lambda: round_w1(0),),
+            1: (lambda: round_w1(1), gather_first_own, lambda: quantize_w1(0)),
+            2: (lambda: quantize_w1(1),),
+            6: (round_w4, quantize_w4),
+        }
+
+        for step in range(TILES + OWN_LAG):
+            for start, count in CITED_CUTS[1:]:
+                if step == start // TILE - CITED_LEAD:
+                    gather_cited_words(start, count)
+            if step < TILES:
+                cited_products(step)
+            if 1 <= step <= TILES:
+                absolute_difference(step - 1)
+            for job in preparation.get(step, ()):
+                job()
+            own = step - OWN_LAG
+            for start, count in OWN_CUTS[1:]:
+                for a in range(PASSES):
+                    if own == start // TILE - PASSES + a:
+                        gather_words(OWN, a, start, count)
+            pair_done = own >= 2 and own % 2 == 0
+            if pair_done:
+                relu((own - 2) * TILE, PAIR)
+            if own >= 0:
+                own_product_and_sum(own)
+            if pair_done:
+                quantize_h((own - 2) * TILE, PAIR)
+                scores((own - 2) * TILE, PAIR)
+
+        for stage in (relu, quantize_h, scores):
+            for u in (TILES - 2, TILES - 1):
+                stage(u * TILE, TILE)

@@ -25,15 +25,21 @@ QUADS = 4
 TILE = 128
 TILES = S // TILE
 PAIR = 2 * TILE
+VECTOR_PIECES = 2
+ROUND_STEPS = {0: (2,), 1: (3, 4), 2: (5, 6, 7)}
+PAIRS = TILES // 2
+EARLY_OWN = 2
+SCALAR_RELUS = ()
 OWN, FIRST, LAST = "own", "first", "last"
 
 CITED_CUTS = ((0, 256), (256, 256), (512, 512))
-OWN_CUTS = ((0, 256), (256, 768))
-WORD_SLOTS = {(OWN, 0): 3, (OWN, 1): 3, (FIRST, 0): 2, (FIRST, 1): 3, (LAST, 0): 2, (LAST, 1): 3}
+OWN_CUTS = ((0, 512), (512, 512))
+WORD_SLOTS = {(OWN, 0): 3, (OWN, 1): 3, (FIRST, 0): 4, (FIRST, 1): 4, (LAST, 0): 4, (LAST, 1): 4}
 STAGE_SLOTS = 4
-CITED_BANKS, DIFF_BANKS, OWN_BANKS = 3, 2, 3
+BANKS = 8
+VECTOR_TILES = 40
 CITED_LEAD = 1
-OWN_LAG = 6
+OWN_LAG = 7
 
 
 def tile_list_citation_topic_scores_kernel(
@@ -51,35 +57,39 @@ def tile_list_citation_topic_scores_kernel(
         def kept(shape, dtype, name):
             return keep.tile(shape, dtype, name=name, align_bytes=64)
 
-        table_words = [kept([P, T], I32, "table_words%d" % a) for a in range(PASSES)]
+        table_words = kept([P, PASSES, T], I32, "table_words")
         table_scales = kept([P, T // 4], I32, "table_scales")
         weight_scales = kept([P, 3, H // 4], I32, "weight_scales")
         w2_codes = kept([P, PASSES, H // 2], I32, "w2_codes")
         identity = kept([P, P], F32, "identity")
         w3_codes = kept([P, PASSES, H], I32, "w3_codes")
         w1_raw = [kept([P, PACK, H], F32, "w1_raw%d" % a) for a in range(PASSES)]
-        w1_bf16 = [kept([P, PACK * H], BF16, "w1_bf16_%d" % a) for a in range(PASSES)]
-        w1_codes = kept([P, PASSES, H], U32, "w1_codes")
-        w1_scales = kept([P, PASSES, H], U8, "w1_scales")
+        w1_bf16 = [keep.tile([P, PACK * H], BF16, name="w1_bf16_%d" % a, tag="w1_bf16_%d" % a, align_bytes=64) for a in range(PASSES)]
+        w1_codes = {}
+        w1_scales = kept([P, PASSES * H], U8, "w1_scales")
         w4_raw = kept([P, PACK, N], F32, "w4_raw")
         w4_bf16 = kept([P, PACK * N], BF16, "w4_bf16")
-        w4_codes = kept([P, N], U32, "w4_codes")
+        w4_codes = []
         w4_scales = kept([P, N], U8, "w4_scales")
+        warm = kept([P, 1], F32, "warm")
         bias = kept([P, 2], F32, "bias")
-        picks = ctx.enter_context(tc.tile_pool(name="picks", bufs=2))
-        picked_scales = {name: kept([P, S], U8, "picked_scales_" + name) for name in (OWN, FIRST, LAST)}
+        made = ctx.enter_context(tc.tile_pool(name="made", bufs=VECTOR_TILES))
+
+        def vector_tile(shape, dtype, name):
+            return made.tile(shape, dtype, name=name, tag="vector", align_bytes=64)
+
+        picked_scales = {}
         first_scales_pass1 = kept([P, S // 4], I32, "first_scales_pass1")
         distance = [kept([P, TILE, PACK], F32, "distance%d" % u) for u in range(TILES)]
-        h_sum = kept([P, PACK * S], BF16, "h_sum")
-        h_bf16 = kept([P, PACK * S], BF16, "h_bf16")
-        h_codes = kept([P, S], U32, "h_codes")
+        h_sum, h_bf16, h_codes = {}, {}, {}
         h_scales = kept([P, S], U8, "h_scales")
+        own_banks = {}
         picked_words = {}
         staged = {}
 
 
-        def load_table_words(a):
-            nc.sync.dma_start(out=table_words[a][:], in_=tab_words[a].rearrange("p t i -> p (t i)").bitcast(I32))
+        def load_table_words():
+            nc.sync.dma_start(out=table_words[:], in_=tab_words.rearrange("a p t i -> p a (t i)").bitcast(I32))
 
         def load_table_scales(q):
             rows = tab_scales.bitcast(I32)[:, 4 * q : 4 * q + 4, :]
@@ -96,31 +106,34 @@ def tile_list_citation_topic_scores_kernel(
 
         def gather_scales(name):
             window = table_scales[:].bitcast(U8)
+            picked_scales[name] = vector_tile([P, S], U8, "picked_scales_" + name)
             nc.vector.tensor_copy(picked_scales[name][:, 0:S], window.indirect(offsets[name][:, 0 : S // 16]))
 
         def gather_words(name, a, start, count):
-            words = picks.tile(
-                [P, count], U32, name="words_%s%d" % (name, a), align_bytes=64, bufs=WORD_SLOTS[name, a]
-            )
-            window = table_words[a][:].bitcast(U32)
+            words = vector_tile([P, count], U32, "words_%s%d" % (name, a))
+            window = table_words[:, a, :].bitcast(U32)
             nc.vector.tensor_copy(words[:], window.indirect(offsets[name][:, start // 16 : (start + count) // 16]))
             for k in range(count // TILE):
                 picked_words[name, a, start // TILE + k] = words[:, k * TILE : (k + 1) * TILE]
 
         def gather_cited_words(start, count):
-            for a in range(PASSES):
-                for name in (LAST, FIRST):
+            for name in (LAST, FIRST):
+                for a in range(PASSES):
                     gather_words(name, a, start, count)
 
 
-        def round_w1(a):
+        def round_w1(a, t):
             src = w1_raw[a][:].rearrange("p j (g t u i) -> p t g u j i", t=PACK, u=2, i=4)
             dst = w1_bf16[a][:].rearrange("p (t g u i j) -> p t g u j i", t=PACK, u=2, i=4, j=PACK)
-            for t in range(PACK):
+            if PACK * a + t < VECTOR_PIECES:
                 nc.vector.tensor_copy(out=dst[:, t], in_=src[:, t])
+            else:
+                nc.scalar.copy(out=dst[:, t], in_=src[:, t])
 
         def quantize_w1(a):
-            nc.vector.quantize_mx(out=w1_codes[:, a, :].bitcast(FP8X4), scales=w1_scales[:, a, :], in_=w1_bf16[a][:])
+            cols = slice(a * H, (a + 1) * H)
+            w1_codes[a] = vector_tile([P, H], U32, "w1_codes%d" % a)
+            nc.vector.quantize_mx(out=w1_codes[a][:].bitcast(FP8X4), scales=w1_scales[:, cols], in_=w1_bf16[a][:])
 
         def round_w4():
             nc.scalar.activation(
@@ -130,17 +143,18 @@ def tile_list_citation_topic_scores_kernel(
             )
 
         def quantize_w4():
-            nc.vector.quantize_mx(out=w4_codes[:].bitcast(FP8X4), scales=w4_scales[:], in_=w4_bf16[:])
+            w4_codes.append(vector_tile([P, N], U32, "w4_codes"))
+            nc.vector.quantize_mx(out=w4_codes[0][:].bitcast(FP8X4), scales=w4_scales[:], in_=w4_bf16[:])
 
 
         def by_token(bank):
             return bank[:].rearrange("p t n -> p n t")
 
-        def cited_products(u):
-            tokens = slice(u * TILE, (u + 1) * TILE)
+        def cited_products(pair):
             planes = weight_scales[:].bitcast(U8)
-            for name, sign in ((LAST, -1.0), (FIRST, 1.0)):
-                bank = psum.tile([P, H], F32, name="cited_bank", tag="cited", bufs=CITED_BANKS)
+            for name, sign, u in [(n, g, 2 * pair + k) for n, g in ((LAST, -1.0), (FIRST, 1.0)) for k in range(2)]:
+                tokens = slice(u * TILE, (u + 1) * TILE)
+                bank = psum.tile([P, H], F32, name="cited_bank", tag="bank", bufs=BANKS)
                 for a in range(PASSES):
                     if name == FIRST:
                         weight, weight_plane = w2_codes[:, a, :].bitcast(U8).bitcast(FP4X4), planes[:, a, :]
@@ -160,82 +174,104 @@ def tile_list_citation_topic_scores_kernel(
                 )
 
         def absolute_difference(u):
-            bank = psum.tile([P, PACK, TILE], F32, name="diff_bank", bufs=DIFF_BANKS)
+            bank = psum.tile([P, PACK, TILE], F32, name="diff_bank", tag="bank", bufs=BANKS)
             for t in range(PACK):
-                for name in (LAST, FIRST):
+                for name in (FIRST, LAST):
                     nc.tensor.matmul(
                         out=bank[:, t, :], lhsT=staged[name, u][:, t].rearrange("p g i -> p (g i)"), rhs=identity[:],
-                        start=(name == LAST), stop=(name == FIRST), is_transpose=True,
+                        start=(name == FIRST), stop=(name == LAST), is_transpose=True,
                     )
             nc.scalar.activation(out=distance[u][:], in_=by_token(bank), func=ACT.Abs)
 
-        def own_product_and_sum(u):
+        def own_product(u):
             tokens = slice(u * TILE, (u + 1) * TILE)
-            bank = psum.tile([P, PACK, TILE], F32, name="own_bank", bufs=OWN_BANKS)
+            bank = psum.tile([P, PACK, TILE], F32, name="own_bank", tag="bank", bufs=BANKS)
             for t in range(PACK):
-                channels = slice(t * P, (t + 1) * P)
                 for a in range(PASSES):
+                    channels = slice(a * H + t * P, a * H + (t + 1) * P)
                     nc.tensor.matmul_mx(
-                        out=bank[:, t, :], lhsT=w1_codes[:, a, channels].bitcast(FP8X4),
-                        lhsT_scale=w1_scales[:, a, channels], rhs=picked_words[OWN, a, u].bitcast(FP8X4),
+                        out=bank[:, t, :], lhsT=w1_codes[a][:, t * P : (t + 1) * P].bitcast(FP8X4),
+                        lhsT_scale=w1_scales[:, channels], rhs=picked_words[OWN, a, u].bitcast(FP8X4),
                         rhs_scale=picked_scales[OWN][4 * a :, tokens], start=(a == 0), stop=(a == PASSES - 1),
                     )
-            values = slice(PACK * u * TILE, PACK * (u + 1) * TILE)
+            own_banks[u] = bank
+
+        def add_distance(u):
+            if u % 2 == 0:
+                h_sum[u // 2] = vector_tile([P, 2, TILE, PACK], BF16, "h_sum")
             nc.vector.tensor_tensor(
-                out=h_sum[:, values].rearrange("p (n t) -> p n t", t=PACK), in0=by_token(bank), in1=distance[u][:],
-                op=ALU.add,
+                out=h_sum[u // 2][:, u % 2], in0=by_token(own_banks[u]), in1=distance[u][:], op=ALU.add
             )
 
         def relu(start, count):
-            values = slice(PACK * start, PACK * (start + count))
-            nc.vector.tensor_scalar(out=h_bf16[:, values], in0=h_sum[:, values], scalar1=0.0, scalar2=None, op0=ALU.max)
+            first = PACK * (start % PAIR)
+            values = h_sum[start // PAIR][:].rearrange("p u n t -> p (u n t)")[:, first : first + PACK * count]
+            if start // PAIR in SCALAR_RELUS:
+                h_bf16[start] = kept([P, PACK * count], BF16, "h_bf16_%d" % start)
+                nc.scalar.activation(out=h_bf16[start][:], in_=values, func=ACT.Relu)
+            else:
+                h_bf16[start] = vector_tile([P, PACK * count], BF16, "h_bf16")
+                nc.vector.tensor_scalar(out=h_bf16[start][:], in0=values, scalar1=0.0, scalar2=None, op0=ALU.max)
 
         def quantize_h(start, count):
+            h_codes[start] = vector_tile([P, count], U32, "h_codes")
             nc.vector.quantize_mx(
-                out=h_codes[:, start : start + count].bitcast(FP8X4), scales=h_scales[:, start : start + count],
-                in_=h_bf16[:, PACK * start : PACK * (start + count)],
+                out=h_codes[start][:].bitcast(FP8X4), scales=h_scales[:, start : start + count], in_=h_bf16[start][:]
             )
 
-        def scores(start, count):
+        def score_product(start, count):
             tokens = slice(start, start + count)
-            bank = psum.tile([P, 2, PAIR], F32, name="score_bank", tag="cited", bufs=CITED_BANKS)
-            result = ring.tile([P, 2, PAIR], F32, name="result")
+            bank = psum.tile([P, 2, count], F32, name="score_bank", tag="bank", bufs=BANKS)
             for e in range(2):
                 classes = slice(e * P, (e + 1) * P)
                 nc.tensor.matmul_mx(
-                    out=bank[:, e, :count], lhsT=w4_codes[:, classes].bitcast(FP8X4), lhsT_scale=w4_scales[:, classes],
-                    rhs=h_codes[:, tokens].bitcast(FP8X4), rhs_scale=h_scales[:, tokens], start=True, stop=True,
+                    out=bank[:, e, :], lhsT=w4_codes[0][:, classes].bitcast(FP8X4), lhsT_scale=w4_scales[:, classes],
+                    rhs=h_codes[start][:].bitcast(FP8X4), rhs_scale=h_scales[:, tokens], start=True, stop=True,
                 )
+            return bank
+
+        def add_bias_on_scalar(result, bank):
             for e in range(2):
-                nc.scalar.activation(
-                    out=result[:, e, :count], in_=bank[:, e, :count], func=ACT.Identity, bias=bias[:, e : e + 1]
+                nc.scalar.activation(out=result[:, e, :], in_=bank[:, e, :], func=ACT.Identity, bias=bias[:, e : e + 1])
+
+        def add_bias_on_vector(result, bank):
+            for e in range(2):
+                nc.vector.tensor_scalar(
+                    out=result[:, e, :], in0=bank[:, e, :], scalar1=bias[:, e : e + 1], scalar2=None, op0=ALU.add
                 )
-            nc.sync.dma_start(out=out.rearrange("(m e) s -> m e s", e=2)[:, :, tokens], in_=result[:, :, :count])
+
+        def store(start, result):
+            nc.sync.dma_start(out=out.rearrange("(m e) s -> m e s", e=2)[:, :, start : start + PAIR], in_=result[:])
+
+        def scores(start):
+            result = ring.tile([P, 2, PAIR], F32, name="result")
+            add_bias_on_scalar(result, score_product(start, PAIR))
+            store(start, result)
 
 
-        nc.vector.memset(table_scales[:], 0)
+        nc.gpsimd.memset(table_scales[:], 0)
         nc.vector.memset(weight_scales[:], 0)
         nc.vector.memset(first_scales_pass1[:], 0)
         make_identity(nc, identity[:])
+        nc.scalar.activation(out=warm[:], in_=identity[:, 0:1], func=ACT.Abs)
 
         nc.sync.dma_start(offsets[FIRST][:], offs2)
         for q in range(QUADS):
             load_table_scales(q)
         nc.sync.dma_start(offsets[LAST][:], offs3)
-        for q in range(QUADS // 2):
-            load_w3_scales(q)
-        load_table_words(0)
-        for q in range(QUADS // 2, QUADS):
-            load_w3_scales(q)
-        for q in range(QUADS):
-            load_w2_scales(q)
+        load_table_words()
+        load_w3_scales(0)
+        load_w3_scales(1)
+        load_w3_scales(2)
+        load_w3_scales(3)
         nc.sync.dma_start(out=w3_codes[:], in_=w3_words.rearrange("a p e i -> p a (e i)").bitcast(I32))
-        load_table_words(1)
         nc.sync.dma_start(out=w2_codes[:], in_=w2_words.rearrange("a p e -> p a e").bitcast(I32))
-
+        load_w2_scales(0)
+        load_w2_scales(1)
+        load_w2_scales(2)
         gather_scales(FIRST)
         nc.sync.dma_start(out=first_scales_pass1[0:112, :], in_=picked_scales[FIRST][4:116, :].bitcast(I32))
-
+        load_w2_scales(3)
         for a in range(PASSES):
             rows = w1[P * PACK * a : P * PACK * (a + 1), :]
             nc.sync.dma_start(out=w1_raw[a][:], in_=rows.rearrange("(p j) r -> p j r", j=PACK))
@@ -247,42 +283,58 @@ def tile_list_citation_topic_scores_kernel(
         gather_scales(LAST)
         gather_cited_words(*CITED_CUTS[0])
 
-        def gather_first_own():
-            gather_scales(OWN)
-            for a in range(PASSES):
-                gather_words(OWN, a, *OWN_CUTS[0])
-
-        preparation = {
-            0: (lambda: round_w1(0),),
-            1: (lambda: round_w1(1), gather_first_own, lambda: quantize_w1(0)),
-            2: (lambda: quantize_w1(1),),
-            6: (round_w4, quantize_w4),
-        }
-
-        for step in range(TILES + OWN_LAG):
-            for start, count in CITED_CUTS[1:]:
-                if step == start // TILE - CITED_LEAD:
-                    gather_cited_words(start, count)
-            if step < TILES:
-                cited_products(step)
-            if 1 <= step <= TILES:
-                absolute_difference(step - 1)
-            for job in preparation.get(step, ()):
-                job()
-            own = step - OWN_LAG
-            for start, count in OWN_CUTS[1:]:
+        gather_cited_words(*CITED_CUTS[1])
+        for pair in range(PAIRS + 1):
+            if pair < PAIRS:
+                cited_products(pair)
+            if pair == 0:
+                gather_cited_words(*CITED_CUTS[2])
+                for piece in range(VECTOR_PIECES):
+                    round_w1(0, piece)
+            for piece in ROUND_STEPS.get(pair, ()):
+                round_w1(piece // PACK, piece % PACK)
+            if pair == PAIRS - 1:
+                gather_scales(OWN)
+                quantize_w1(0)
                 for a in range(PASSES):
-                    if own == start // TILE - PASSES + a:
+                    gather_words(OWN, a, *OWN_CUTS[0])
+                quantize_w1(1)
+                for start, count in OWN_CUTS[1:]:
+                    for a in range(PASSES):
                         gather_words(OWN, a, start, count)
-            pair_done = own >= 2 and own % 2 == 0
-            if pair_done:
-                relu((own - 2) * TILE, PAIR)
-            if own >= 0:
-                own_product_and_sum(own)
-            if pair_done:
-                quantize_h((own - 2) * TILE, PAIR)
-                scores((own - 2) * TILE, PAIR)
+            if pair == 3:
+                round_w4()
+            if pair == PAIRS:
+                for u in range(EARLY_OWN):
+                    own_product(u)
+            if pair >= 1:
+                for u in (2 * pair - 2, 2 * pair - 1):
+                    absolute_difference(u)
+        for u in range(EARLY_OWN, 6):
+            own_product(u)
+        for u in range(TILES):
+            add_distance(u)
+            if u == 1:
+                quantize_w4()
+            if u in (2, 4):
+                relu((u - 2) * TILE, PAIR)
+            if u in (3, 5):
+                quantize_h((u - 3) * TILE, PAIR)
+                scores((u - 3) * TILE)
+            if u == 3:
+                for late_tile in range(6, TILES):
+                    own_product(late_tile)
+            if u == 5:
+                relu((u - 1) * TILE, PAIR)
+            if u == 6:
+                quantize_h((u - 2) * TILE, PAIR)
+                scores((u - 2) * TILE)
 
-        for stage in (relu, quantize_h, scores):
-            for u in (TILES - 2, TILES - 1):
-                stage(u * TILE, TILE)
+        for u in (TILES - 2, TILES - 1):
+            relu(u * TILE, TILE)
+        for u in (TILES - 2, TILES - 1):
+            quantize_h(u * TILE, TILE)
+        last = ring.tile([P, 2, PAIR], F32, name="result")
+        add_bias_on_scalar(last[:, :, :TILE], score_product(S - PAIR, TILE))
+        add_bias_on_vector(last[:, :, TILE:], score_product(S - TILE, TILE))
+        store(S - PAIR, last)

@@ -25,10 +25,10 @@ QUADS = 4
 TILE = 128
 TILES = S // TILE
 PAIR = 2 * TILE
-VECTOR_PIECES = 2
-ROUND_STEPS = {0: (2,), 1: (3, 4), 2: (5, 6, 7)}
+VECTOR_PIECES = 4
+ROUND_STEPS = {1: (4, 5), 2: (6, 7)}
 PAIRS = TILES // 2
-EARLY_OWN = 2
+EARLY_OWN = 4
 SCALAR_RELUS = ()
 OWN, FIRST, LAST = "own", "first", "last"
 
@@ -57,7 +57,7 @@ def tile_list_citation_topic_scores_kernel(
         def kept(shape, dtype, name):
             return keep.tile(shape, dtype, name=name, align_bytes=64)
 
-        table_words = kept([P, PASSES, T], I32, "table_words")
+        table_words = [kept([P, T], I32, "table_words%d" % a) for a in range(PASSES)]
         table_scales = kept([P, T // 4], I32, "table_scales")
         weight_scales = kept([P, 3, H // 4], I32, "weight_scales")
         w2_codes = kept([P, PASSES, H // 2], I32, "w2_codes")
@@ -80,7 +80,7 @@ def tile_list_citation_topic_scores_kernel(
 
         picked_scales = {}
         first_scales_pass1 = kept([P, S // 4], I32, "first_scales_pass1")
-        distance = [kept([P, TILE, PACK], F32, "distance%d" % u) for u in range(TILES)]
+        distance = [kept([P, TILE // 2, PACK, 2], F32, "distance%d" % u) for u in range(TILES)]
         h_sum, h_bf16, h_codes = {}, {}, {}
         h_scales = kept([P, S], U8, "h_scales")
         own_banks = {}
@@ -88,8 +88,8 @@ def tile_list_citation_topic_scores_kernel(
         staged = {}
 
 
-        def load_table_words():
-            nc.sync.dma_start(out=table_words[:], in_=tab_words.rearrange("a p t i -> p a (t i)").bitcast(I32))
+        def load_table_words(a):
+            nc.sync.dma_start(out=table_words[a][:], in_=tab_words[a].rearrange("p t i -> p (t i)").bitcast(I32))
 
         def load_table_scales(q):
             rows = tab_scales.bitcast(I32)[:, 4 * q : 4 * q + 4, :]
@@ -111,7 +111,7 @@ def tile_list_citation_topic_scores_kernel(
 
         def gather_words(name, a, start, count):
             words = vector_tile([P, count], U32, "words_%s%d" % (name, a))
-            window = table_words[:, a, :].bitcast(U32)
+            window = table_words[a][:].bitcast(U32)
             nc.vector.tensor_copy(words[:], window.indirect(offsets[name][:, start // 16 : (start + count) // 16]))
             for k in range(count // TILE):
                 picked_words[name, a, start // TILE + k] = words[:, k * TILE : (k + 1) * TILE]
@@ -126,7 +126,11 @@ def tile_list_citation_topic_scores_kernel(
             src = w1_raw[a][:].rearrange("p j (g t u i) -> p t g u j i", t=PACK, u=2, i=4)
             dst = w1_bf16[a][:].rearrange("p (t g u i j) -> p t g u j i", t=PACK, u=2, i=4, j=PACK)
             if PACK * a + t < VECTOR_PIECES:
-                nc.vector.tensor_copy(out=dst[:, t], in_=src[:, t])
+                nc.gpsimd.tensor_scalar(
+                    out=w1_bf16[a][:].rearrange("p (t g i j) -> p t g i j", t=PACK, i=RUN, j=PACK)[:, t],
+                    in0=w1_raw[a][:].rearrange("p j (g t i) -> p t g i j", t=PACK, i=RUN)[:, t],
+                    scalar1=1.0, scalar2=0.0, op0=ALU.mult, op1=ALU.add,
+                )
             else:
                 nc.scalar.copy(out=dst[:, t], in_=src[:, t])
 
@@ -136,10 +140,10 @@ def tile_list_citation_topic_scores_kernel(
             nc.vector.quantize_mx(out=w1_codes[a][:].bitcast(FP8X4), scales=w1_scales[:, cols], in_=w1_bf16[a][:])
 
         def round_w4():
-            nc.scalar.activation(
+            nc.gpsimd.tensor_scalar(
                 out=w4_bf16[:].rearrange("p (e m t) -> p e m t", e=2, t=PACK),
-                in_=w4_raw[:].rearrange("p t (m e) -> p e m t", e=2),
-                func=ACT.Copy,
+                in0=w4_raw[:].rearrange("p t (m e) -> p e m t", e=2),
+                scalar1=1.0, scalar2=0.0, op0=ALU.mult, op1=ALU.add,
             )
 
         def quantize_w4():
@@ -148,7 +152,7 @@ def tile_list_citation_topic_scores_kernel(
 
 
         def by_token(bank):
-            return bank[:].rearrange("p t n -> p n t")
+            return bank[:].rearrange("p t (m i) -> p m t i", i=2)
 
         def cited_products(pair):
             planes = weight_scales[:].bitcast(U8)
@@ -200,7 +204,8 @@ def tile_list_citation_topic_scores_kernel(
             if u % 2 == 0:
                 h_sum[u // 2] = vector_tile([P, 2, TILE, PACK], BF16, "h_sum")
             nc.vector.tensor_tensor(
-                out=h_sum[u // 2][:, u % 2], in0=by_token(own_banks[u]), in1=distance[u][:], op=ALU.add
+                out=h_sum[u // 2][:, u % 2].rearrange("p (m i) t -> p m t i", i=2), in0=by_token(own_banks[u]),
+                in1=distance[u][:], op=ALU.add,
             )
 
         def relu(start, count):
@@ -259,7 +264,8 @@ def tile_list_citation_topic_scores_kernel(
         for q in range(QUADS):
             load_table_scales(q)
         nc.sync.dma_start(offsets[LAST][:], offs3)
-        load_table_words()
+        for a in range(PASSES):
+            load_table_words(a)
         load_w3_scales(0)
         load_w3_scales(1)
         load_w3_scales(2)
@@ -281,7 +287,9 @@ def tile_list_citation_topic_scores_kernel(
         nc.sync.dma_start(out=bias[:], in_=b.rearrange("(m e) -> m e", e=2))
 
         gather_scales(LAST)
-        gather_cited_words(*CITED_CUTS[0])
+        for a in range(PASSES):
+            for name in (LAST, FIRST):
+                gather_words(name, a, *CITED_CUTS[0])
 
         gather_cited_words(*CITED_CUTS[1])
         for pair in range(PAIRS + 1):
@@ -295,10 +303,10 @@ def tile_list_citation_topic_scores_kernel(
                 round_w1(piece // PACK, piece % PACK)
             if pair == PAIRS - 1:
                 gather_scales(OWN)
-                quantize_w1(0)
                 for a in range(PASSES):
                     gather_words(OWN, a, *OWN_CUTS[0])
-                quantize_w1(1)
+                for a in range(PASSES):
+                    quantize_w1(a)
                 for start, count in OWN_CUTS[1:]:
                     for a in range(PASSES):
                         gather_words(OWN, a, start, count)

@@ -25,19 +25,22 @@ QUADS = 4
 TILE = 128
 TILES = S // TILE
 PAIR = 2 * TILE
-VECTOR_PIECES = 4
-ROUND_STEPS = {1: (4, 5), 2: (6, 7)}
+VECTOR_PIECES = 6
+ROUND_STEPS = {1: (6, 7)}
 PAIRS = TILES // 2
 EARLY_OWN = 4
 SCALAR_RELUS = ()
 OWN, FIRST, LAST = "own", "first", "last"
 
-CITED_CUTS = ((0, 256), (256, 256), (512, 512))
-OWN_CUTS = ((0, 512), (512, 512))
+CITED_CUTS = ((0, 256), (256, 256), (512, 256), (768, 256))
+OWN_CUTS = ((0, 256), (256, 256), (512, 512))
 WORD_SLOTS = {(OWN, 0): 3, (OWN, 1): 3, (FIRST, 0): 4, (FIRST, 1): 4, (LAST, 0): 4, (LAST, 1): 4}
 STAGE_SLOTS = 4
 BANKS = 8
-VECTOR_TILES = 40
+GPSIMD_TILES = 2
+WARM_PASSES = 4
+VECTOR_TILES = 47
+SCALAR_TILES = 20
 CITED_LEAD = 1
 OWN_LAG = 7
 
@@ -62,14 +65,13 @@ def tile_list_citation_topic_scores_kernel(
         weight_scales = kept([P, 3, H // 4], I32, "weight_scales")
         w2_codes = kept([P, PASSES, H // 2], I32, "w2_codes")
         identity = kept([P, P], F32, "identity")
-        w3_codes = kept([P, PASSES, H], I32, "w3_codes")
+        w3_codes = [kept([P, H], I32, "w3_codes%d" % a) for a in range(PASSES)]
         w1_raw = [kept([P, PACK, H], F32, "w1_raw%d" % a) for a in range(PASSES)]
         w1_bf16 = [keep.tile([P, PACK * H], BF16, name="w1_bf16_%d" % a, tag="w1_bf16_%d" % a, align_bytes=64) for a in range(PASSES)]
         w1_codes = {}
         w1_scales = kept([P, PASSES * H], U8, "w1_scales")
         w4_raw = kept([P, PACK, N], F32, "w4_raw")
-        w4_bf16 = kept([P, PACK * N], BF16, "w4_bf16")
-        w4_codes = []
+        w4_bf16, w4_codes = [], []
         w4_scales = kept([P, N], U8, "w4_scales")
         warm = kept([P, 1], F32, "warm")
         bias = kept([P, 2], F32, "bias")
@@ -78,9 +80,12 @@ def tile_list_citation_topic_scores_kernel(
         def vector_tile(shape, dtype, name):
             return made.tile(shape, dtype, name=name, tag="vector", align_bytes=64)
 
+        def scalar_tile(shape, dtype, name):
+            return made.tile(shape, dtype, name=name, tag="scalar", bufs=SCALAR_TILES, align_bytes=64)
+
         picked_scales = {}
         first_scales_pass1 = kept([P, S // 4], I32, "first_scales_pass1")
-        distance = [kept([P, TILE // 2, PACK, 2], F32, "distance%d" % u) for u in range(TILES)]
+        distance = {}
         h_sum, h_bf16, h_codes = {}, {}, {}
         h_scales = kept([P, S], U8, "h_scales")
         own_banks = {}
@@ -90,6 +95,9 @@ def tile_list_citation_topic_scores_kernel(
 
         def load_table_words(a):
             nc.sync.dma_start(out=table_words[a][:], in_=tab_words[a].rearrange("p t i -> p (t i)").bitcast(I32))
+
+        def load_w3_words(a):
+            nc.sync.dma_start(out=w3_codes[a][:], in_=w3_words[a].rearrange("p e i -> p (e i)").bitcast(I32))
 
         def load_table_scales(q):
             rows = tab_scales.bitcast(I32)[:, 4 * q : 4 * q + 4, :]
@@ -104,10 +112,13 @@ def tile_list_citation_topic_scores_kernel(
             nc.sync.dma_start(out=weight_scales[32 * q : 32 * q + 4, 0:2, :], in_=rows)
 
 
-        def gather_scales(name):
+        def gather_scales(name, start=0, count=S):
             window = table_scales[:].bitcast(U8)
-            picked_scales[name] = vector_tile([P, S], U8, "picked_scales_" + name)
-            nc.vector.tensor_copy(picked_scales[name][:, 0:S], window.indirect(offsets[name][:, 0 : S // 16]))
+            plane = vector_tile([P, count], U8, "picked_scales_" + name)
+            nc.vector.tensor_copy(plane[:], window.indirect(offsets[name][:, start // 16 : (start + count) // 16]))
+            for k in range(count // TILE):
+                picked_scales[name, start // TILE + k] = plane[:, k * TILE : (k + 1) * TILE]
+            return plane
 
         def gather_words(name, a, start, count):
             words = vector_tile([P, count], U32, "words_%s%d" % (name, a))
@@ -140,33 +151,34 @@ def tile_list_citation_topic_scores_kernel(
             nc.vector.quantize_mx(out=w1_codes[a][:].bitcast(FP8X4), scales=w1_scales[:, cols], in_=w1_bf16[a][:])
 
         def round_w4():
+            w4_bf16.append(keep.tile([P, PACK * N], BF16, name="w4_bf16", tag="w1_bf16_1", align_bytes=64))
             nc.gpsimd.tensor_scalar(
-                out=w4_bf16[:].rearrange("p (e m t) -> p e m t", e=2, t=PACK),
+                out=w4_bf16[0][:].rearrange("p (e m t) -> p e m t", e=2, t=PACK),
                 in0=w4_raw[:].rearrange("p t (m e) -> p e m t", e=2),
                 scalar1=1.0, scalar2=0.0, op0=ALU.mult, op1=ALU.add,
             )
 
         def quantize_w4():
             w4_codes.append(vector_tile([P, N], U32, "w4_codes"))
-            nc.vector.quantize_mx(out=w4_codes[0][:].bitcast(FP8X4), scales=w4_scales[:], in_=w4_bf16[:])
+            nc.vector.quantize_mx(out=w4_codes[0][:].bitcast(FP8X4), scales=w4_scales[:], in_=w4_bf16[0][:])
 
 
         def by_token(bank):
             return bank[:].rearrange("p t (m i) -> p m t i", i=2)
 
-        def cited_products(pair):
+        def cited_products(name, pair):
             planes = weight_scales[:].bitcast(U8)
-            for name, sign, u in [(n, g, 2 * pair + k) for n, g in ((LAST, -1.0), (FIRST, 1.0)) for k in range(2)]:
+            sign = -1.0 if name == LAST else 1.0
+            for u in (2 * pair, 2 * pair + 1):
                 tokens = slice(u * TILE, (u + 1) * TILE)
                 bank = psum.tile([P, H], F32, name="cited_bank", tag="bank", bufs=BANKS)
                 for a in range(PASSES):
                     if name == FIRST:
                         weight, weight_plane = w2_codes[:, a, :].bitcast(U8).bitcast(FP4X4), planes[:, a, :]
-                        plane = picked_scales[FIRST][:] if a == 0 else first_scales_pass1[:].bitcast(U8)
-                        token_plane = plane[:, tokens]
+                        token_plane = picked_scales[FIRST, u] if a == 0 else first_scales_pass1[:].bitcast(U8)[:, tokens]
                     else:
-                        weight, weight_plane = w3_codes[:, a, :].bitcast(FP8X4), planes[4 * a :, 2, :]
-                        token_plane = picked_scales[LAST][4 * a :, tokens]
+                        weight, weight_plane = w3_codes[a][:].bitcast(FP8X4), planes[4 * a :, 2, :]
+                        token_plane = picked_scales[LAST, u][4 * a :, :]
                     nc.tensor.matmul_mx(
                         out=bank[:], lhsT=picked_words[name, a, u].bitcast(FP8X4), lhsT_scale=token_plane,
                         rhs=weight, rhs_scale=weight_plane, start=(a == 0), stop=(a == PASSES - 1),
@@ -185,10 +197,14 @@ def tile_list_citation_topic_scores_kernel(
                         out=bank[:, t, :], lhsT=staged[name, u][:, t].rearrange("p g i -> p (g i)"), rhs=identity[:],
                         start=(name == FIRST), stop=(name == LAST), is_transpose=True,
                     )
-            nc.scalar.activation(out=distance[u][:], in_=by_token(bank), func=ACT.Abs)
+            if u < GPSIMD_TILES:
+                distance[u] = scalar_tile([P, TILE, PACK], F32, "distance")
+                nc.scalar.activation(out=distance[u][:], in_=bank[:].rearrange("p t n -> p n t"), func=ACT.Abs)
+            else:
+                distance[u] = scalar_tile([P, TILE // 2, PACK, 2], F32, "distance")
+                nc.scalar.activation(out=distance[u][:], in_=by_token(bank), func=ACT.Abs)
 
         def own_product(u):
-            tokens = slice(u * TILE, (u + 1) * TILE)
             bank = psum.tile([P, PACK, TILE], F32, name="own_bank", tag="bank", bufs=BANKS)
             for t in range(PACK):
                 for a in range(PASSES):
@@ -196,9 +212,15 @@ def tile_list_citation_topic_scores_kernel(
                     nc.tensor.matmul_mx(
                         out=bank[:, t, :], lhsT=w1_codes[a][:, t * P : (t + 1) * P].bitcast(FP8X4),
                         lhsT_scale=w1_scales[:, channels], rhs=picked_words[OWN, a, u].bitcast(FP8X4),
-                        rhs_scale=picked_scales[OWN][4 * a :, tokens], start=(a == 0), stop=(a == PASSES - 1),
+                        rhs_scale=picked_scales[OWN, u][4 * a :, :], start=(a == 0), stop=(a == PASSES - 1),
                     )
             own_banks[u] = bank
+            if u < GPSIMD_TILES:
+                own = scalar_tile([P, TILE, PACK], F32, "own")
+                nc.scalar.activation(out=own[:], in_=bank[:].rearrange("p t n -> p n t"), func=ACT.Copy)
+                if u % 2 == 0:
+                    h_sum[u // 2] = kept([P, 2, TILE, PACK], BF16, "h_sum_early%d" % u)
+                nc.gpsimd.tensor_tensor(out=h_sum[u // 2][:, u % 2], in0=own[:], in1=distance[u][:], op=ALU.add)
 
         def add_distance(u):
             if u % 2 == 0:
@@ -212,7 +234,7 @@ def tile_list_citation_topic_scores_kernel(
             first = PACK * (start % PAIR)
             values = h_sum[start // PAIR][:].rearrange("p u n t -> p (u n t)")[:, first : first + PACK * count]
             if start // PAIR in SCALAR_RELUS:
-                h_bf16[start] = kept([P, PACK * count], BF16, "h_bf16_%d" % start)
+                h_bf16[start] = scalar_tile([P, PACK * count], BF16, "h_relu")
                 nc.scalar.activation(out=h_bf16[start][:], in_=values, func=ACT.Relu)
             else:
                 h_bf16[start] = vector_tile([P, PACK * count], BF16, "h_bf16")
@@ -224,34 +246,31 @@ def tile_list_citation_topic_scores_kernel(
                 out=h_codes[start][:].bitcast(FP8X4), scales=h_scales[:, start : start + count], in_=h_bf16[start][:]
             )
 
-        def score_product(start, count):
-            tokens = slice(start, start + count)
-            bank = psum.tile([P, 2, count], F32, name="score_bank", tag="bank", bufs=BANKS)
-            for e in range(2):
-                classes = slice(e * P, (e + 1) * P)
-                nc.tensor.matmul_mx(
-                    out=bank[:, e, :], lhsT=w4_codes[0][:, classes].bitcast(FP8X4), lhsT_scale=w4_scales[:, classes],
-                    rhs=h_codes[start][:].bitcast(FP8X4), rhs_scale=h_scales[:, tokens], start=True, stop=True,
-                )
-            return bank
+        def score_product(sums, e, start, count):
+            classes = slice(e * P, (e + 1) * P)
+            nc.tensor.matmul_mx(
+                out=sums, lhsT=w4_codes[0][:, classes].bitcast(FP8X4), lhsT_scale=w4_scales[:, classes],
+                rhs=h_codes[start][:].bitcast(FP8X4), rhs_scale=h_scales[:, start : start + count],
+                start=True, stop=True,
+            )
 
-        def add_bias_on_scalar(result, bank):
-            for e in range(2):
-                nc.scalar.activation(out=result[:, e, :], in_=bank[:, e, :], func=ACT.Identity, bias=bias[:, e : e + 1])
+        def add_bias_on_scalar(result, sums, e):
+            nc.scalar.activation(out=result, in_=sums, func=ACT.Identity, bias=bias[:, e : e + 1])
 
-        def add_bias_on_vector(result, bank):
-            for e in range(2):
-                nc.vector.tensor_scalar(
-                    out=result[:, e, :], in0=bank[:, e, :], scalar1=bias[:, e : e + 1], scalar2=None, op0=ALU.add
-                )
+        def add_bias_on_vector(result, sums, e):
+            nc.vector.tensor_scalar(out=result, in0=sums, scalar1=bias[:, e : e + 1], scalar2=None, op0=ALU.add)
 
-        def store(start, result):
-            nc.sync.dma_start(out=out.rearrange("(m e) s -> m e s", e=2)[:, :, start : start + PAIR], in_=result[:])
+        def store(start, count, result):
+            nc.sync.dma_start(out=out.rearrange("(m e) s -> m e s", e=2)[:, :, start : start + count], in_=result[:])
 
         def scores(start):
-            result = ring.tile([P, 2, PAIR], F32, name="result")
-            add_bias_on_scalar(result, score_product(start, PAIR))
-            store(start, result)
+            bank = psum.tile([P, 2, PAIR], F32, name="score_bank", tag="bank", bufs=BANKS)
+            result = scalar_tile([P, 2, PAIR], F32, "result")
+            for e in range(2):
+                score_product(bank[:, e, :], e, start, PAIR)
+            for e in range(2):
+                add_bias_on_scalar(result[:, e, :], bank[:, e, :], e)
+            store(start, PAIR, result)
 
 
         nc.gpsimd.memset(table_scales[:], 0)
@@ -264,85 +283,114 @@ def tile_list_citation_topic_scores_kernel(
         for q in range(QUADS):
             load_table_scales(q)
         nc.sync.dma_start(offsets[LAST][:], offs3)
-        for a in range(PASSES):
-            load_table_words(a)
+        load_table_words(0)
+        load_w3_words(0)
         load_w3_scales(0)
         load_w3_scales(1)
         load_w3_scales(2)
         load_w3_scales(3)
-        nc.sync.dma_start(out=w3_codes[:], in_=w3_words.rearrange("a p e i -> p a (e i)").bitcast(I32))
+        load_table_words(1)
+        load_w3_words(1)
         nc.sync.dma_start(out=w2_codes[:], in_=w2_words.rearrange("a p e -> p a e").bitcast(I32))
+        first_scales = gather_scales(FIRST)
+        nc.sync.dma_start(out=first_scales_pass1[0:112, :], in_=first_scales[4:116, :].bitcast(I32))
         load_w2_scales(0)
         load_w2_scales(1)
         load_w2_scales(2)
-        gather_scales(FIRST)
-        nc.sync.dma_start(out=first_scales_pass1[0:112, :], in_=picked_scales[FIRST][4:116, :].bitcast(I32))
         load_w2_scales(3)
         for a in range(PASSES):
             rows = w1[P * PACK * a : P * PACK * (a + 1), :]
             nc.sync.dma_start(out=w1_raw[a][:], in_=rows.rearrange("(p j) r -> p j r", j=PACK))
-        nc.sync.dma_start(offsets[OWN][:], offs)
+            if a == 0:
+                nc.sync.dma_start(offsets[OWN][:], offs)
         for t in range(PACK):
             nc.sync.dma_start(out=w4_raw[:, t, :], in_=w4.rearrange("(g t i) n -> t g i n", t=PACK, i=RUN)[t])
         nc.sync.dma_start(out=bias[:], in_=b.rearrange("(m e) -> m e", e=2))
 
-        gather_scales(LAST)
-        for a in range(PASSES):
+        gather_scales(LAST, 0, S // 2)
+        idle_bank = psum.tile([P, H], F32, name="idle_bank", tag="bank", bufs=BANKS)
+        for k in range(WARM_PASSES):
+            w3_plane = weight_scales[:].bitcast(U8)[:, 2, :]
+            nc.tensor.matmul_mx(
+                out=idle_bank[:], lhsT=w3_codes[0][:, :P].bitcast(FP8X4), lhsT_scale=w3_plane[:, :P],
+                rhs=w3_codes[0][:].bitcast(FP8X4), rhs_scale=w3_plane, start=True, stop=True,
+            )
+        for name, a, cut in (
+            (LAST, 0, 0), (FIRST, 0, 0), (LAST, 0, 1), (LAST, 1, 0), (FIRST, 1, 0), (LAST, 1, 1), (FIRST, 0, 1), (FIRST, 1, 1)
+        ):
+            gather_words(name, a, *CITED_CUTS[cut])
+        def both_products(pair):
             for name in (LAST, FIRST):
-                gather_words(name, a, *CITED_CUTS[0])
+                cited_products(name, pair)
 
-        gather_cited_words(*CITED_CUTS[1])
-        for pair in range(PAIRS + 1):
-            if pair < PAIRS:
-                cited_products(pair)
-            if pair == 0:
-                gather_cited_words(*CITED_CUTS[2])
-                for piece in range(VECTOR_PIECES):
-                    round_w1(0, piece)
-            for piece in ROUND_STEPS.get(pair, ()):
-                round_w1(piece // PACK, piece % PACK)
-            if pair == PAIRS - 1:
-                gather_scales(OWN)
-                for a in range(PASSES):
-                    gather_words(OWN, a, *OWN_CUTS[0])
-                for a in range(PASSES):
-                    quantize_w1(a)
-                for start, count in OWN_CUTS[1:]:
-                    for a in range(PASSES):
-                        gather_words(OWN, a, start, count)
-            if pair == 3:
-                round_w4()
-            if pair == PAIRS:
-                for u in range(EARLY_OWN):
-                    own_product(u)
-            if pair >= 1:
-                for u in (2 * pair - 2, 2 * pair - 1):
-                    absolute_difference(u)
-        for u in range(EARLY_OWN, 6):
+        def differences(pair):
+            for u in (2 * pair, 2 * pair + 1):
+                absolute_difference(u)
+
+        def gather_passes(name, cut):
+            for a in range(PASSES):
+                gather_words(name, a, *cut)
+
+        both_products(0)
+        gather_scales(LAST, S // 2, S // 2)
+        gather_cited_words(*CITED_CUTS[2])
+        for piece in range(VECTOR_PIECES):
+            round_w1(piece // PACK, piece % PACK)
+        both_products(1)
+        for piece in range(VECTOR_PIECES, PASSES * PACK):
+            round_w1(piece // PACK, piece % PACK)
+        differences(0)
+        gather_scales(OWN, 0, S // 2)
+        gather_passes(OWN, OWN_CUTS[0])
+        gather_passes(LAST, CITED_CUTS[3])
+        for a in range(PASSES):
+            quantize_w1(a)
+        round_w4()
+        gather_passes(FIRST, CITED_CUTS[3])
+        gather_passes(OWN, OWN_CUTS[1])
+        gather_scales(OWN, S // 2, S // 2)
+        gather_passes(OWN, OWN_CUTS[2])
+        both_products(2)
+        differences(1)
+        cited_products(LAST, 3)
+        for u in range(2):
             own_product(u)
-        for u in range(TILES):
-            add_distance(u)
-            if u == 1:
-                quantize_w4()
-            if u in (2, 4):
-                relu((u - 2) * TILE, PAIR)
-            if u in (3, 5):
-                quantize_h((u - 3) * TILE, PAIR)
-                scores((u - 3) * TILE)
-            if u == 3:
-                for late_tile in range(6, TILES):
-                    own_product(late_tile)
-            if u == 5:
-                relu((u - 1) * TILE, PAIR)
-            if u == 6:
-                quantize_h((u - 2) * TILE, PAIR)
-                scores((u - 2) * TILE)
-
+        cited_products(FIRST, 3)
+        differences(2)
+        for u in range(2, EARLY_OWN):
+            own_product(u)
+        differences(3)
+        for u in range(EARLY_OWN, 8):
+            own_product(u)
+        add_distance(2)
+        add_distance(3)
+        quantize_w4()
+        relu(0 * PAIR, PAIR)
+        add_distance(4)
+        relu(1 * PAIR, PAIR)
+        quantize_h(0 * PAIR, PAIR)
+        scores(0 * PAIR)
+        add_distance(5)
+        quantize_h(1 * PAIR, PAIR)
+        scores(1 * PAIR)
+        relu(2 * PAIR, PAIR)
+        add_distance(6)
+        quantize_h(2 * PAIR, PAIR)
+        scores(2 * PAIR)
+        add_distance(7)
         for u in (TILES - 2, TILES - 1):
             relu(u * TILE, TILE)
+
+        tail, stores = [], []
         for u in (TILES - 2, TILES - 1):
             quantize_h(u * TILE, TILE)
-        last = ring.tile([P, 2, PAIR], F32, name="result")
-        add_bias_on_scalar(last[:, :, :TILE], score_product(S - PAIR, TILE))
-        add_bias_on_vector(last[:, :, TILE:], score_product(S - TILE, TILE))
-        store(S - PAIR, last)
+            result = scalar_tile([P, 2, TILE], F32, "result")
+            for e, add_bias in enumerate((add_bias_on_scalar, add_bias_on_vector)):
+                bank = psum.tile([P, TILE], F32, name="score_bank", tag="bank", bufs=BANKS)
+                score_product(bank[:], e, u * TILE, TILE)
+                tail.append((add_bias, result, bank, e))
+            stores.append((u * TILE, TILE, result))
+        for add_bias, result, bank, e in tail:
+            add_bias(result[:, e, :], bank[:], e)
+        for args in stores:
+            store(*args)

@@ -25,21 +25,22 @@ QUADS = 4
 TILE = 128
 TILES = S // TILE
 PAIR = 2 * TILE
-VECTOR_PIECES = 6
+VECTOR_PIECES = 5
 ROUND_STEPS = {1: (6, 7)}
 PAIRS = TILES // 2
-EARLY_OWN = 4
-SCALAR_RELUS = ()
+EARLY_OWN = 6
+SCALAR_RELUS = (0, 1)
 OWN, FIRST, LAST = "own", "first", "last"
 
 CITED_CUTS = ((0, 256), (256, 256), (512, 256), (768, 256))
-OWN_CUTS = ((0, 256), (256, 256), (512, 512))
+OWN_CUTS = ((0, 256), (256, 256), (512, 256), (768, 256))
 WORD_SLOTS = {(OWN, 0): 3, (OWN, 1): 3, (FIRST, 0): 4, (FIRST, 1): 4, (LAST, 0): 4, (LAST, 1): 4}
 STAGE_SLOTS = 4
 BANKS = 8
+GPSIMD_DIFFERENCES = (3, 4, 5)
 GPSIMD_TILES = 2
-WARM_PASSES = 4
-VECTOR_TILES = 47
+WARM_PASSES = 3
+VECTOR_TILES = 49
 SCALAR_TILES = 20
 CITED_LEAD = 1
 OWN_LAG = 7
@@ -83,12 +84,15 @@ def tile_list_citation_topic_scores_kernel(
         def scalar_tile(shape, dtype, name):
             return made.tile(shape, dtype, name=name, tag="scalar", bufs=SCALAR_TILES, align_bytes=64)
 
+        def gpsimd_tile(shape, dtype, name):
+            return made.tile(shape, dtype, name=name, tag="gpsimd", bufs=6, align_bytes=64)
+
         picked_scales = {}
         first_scales_pass1 = kept([P, S // 4], I32, "first_scales_pass1")
         distance = {}
         h_sum, h_bf16, h_codes = {}, {}, {}
         h_scales = kept([P, S], U8, "h_scales")
-        own_banks = {}
+        own_banks, difference = {}, {}
         picked_words = {}
         staged = {}
 
@@ -151,7 +155,7 @@ def tile_list_citation_topic_scores_kernel(
             nc.vector.quantize_mx(out=w1_codes[a][:].bitcast(FP8X4), scales=w1_scales[:, cols], in_=w1_bf16[a][:])
 
         def round_w4():
-            w4_bf16.append(keep.tile([P, PACK * N], BF16, name="w4_bf16", tag="w1_bf16_1", align_bytes=64))
+            w4_bf16.append(gpsimd_tile([P, PACK * N], BF16, "w4_bf16"))
             nc.gpsimd.tensor_scalar(
                 out=w4_bf16[0][:].rearrange("p (e m t) -> p e m t", e=2, t=PACK),
                 in0=w4_raw[:].rearrange("p t (m e) -> p e m t", e=2),
@@ -189,13 +193,22 @@ def tile_list_citation_topic_scores_kernel(
                     func=ACT.Copy, scale=sign,
                 )
 
+        def subtract_on_gpsimd(u):
+            shape = [P, PACK, H // (PACK * RUN), RUN]
+            if u == 4:
+                difference[u] = keep.tile(shape, F32, name="difference", tag="w1_bf16_1", align_bytes=64)
+            else:
+                difference[u] = gpsimd_tile(shape, F32, "difference")
+            nc.gpsimd.tensor_tensor(out=difference[u][:], in0=staged[FIRST, u][:], in1=staged[LAST, u][:], op=ALU.add)
+
         def absolute_difference(u):
             bank = psum.tile([P, PACK, TILE], F32, name="diff_bank", tag="bank", bufs=BANKS)
+            terms = (difference[u],) if u in GPSIMD_DIFFERENCES else (staged[FIRST, u], staged[LAST, u])
             for t in range(PACK):
-                for name in (FIRST, LAST):
+                for k, term in enumerate(terms):
                     nc.tensor.matmul(
-                        out=bank[:, t, :], lhsT=staged[name, u][:, t].rearrange("p g i -> p (g i)"), rhs=identity[:],
-                        start=(name == FIRST), stop=(name == LAST), is_transpose=True,
+                        out=bank[:, t, :], lhsT=term[:, t].rearrange("p g i -> p (g i)"), rhs=identity[:],
+                        start=(k == 0), stop=(k == len(terms) - 1), is_transpose=True,
                     )
             if u < GPSIMD_TILES:
                 distance[u] = scalar_tile([P, TILE, PACK], F32, "distance")
@@ -219,7 +232,7 @@ def tile_list_citation_topic_scores_kernel(
                 own = scalar_tile([P, TILE, PACK], F32, "own")
                 nc.scalar.activation(out=own[:], in_=bank[:].rearrange("p t n -> p n t"), func=ACT.Copy)
                 if u % 2 == 0:
-                    h_sum[u // 2] = kept([P, 2, TILE, PACK], BF16, "h_sum_early%d" % u)
+                    h_sum[u // 2] = gpsimd_tile([P, 2, TILE, PACK], BF16, "h_sum_early")
                 nc.gpsimd.tensor_tensor(out=h_sum[u // 2][:, u % 2], in0=own[:], in1=distance[u][:], op=ALU.add)
 
         def add_distance(u):
@@ -323,6 +336,11 @@ def tile_list_citation_topic_scores_kernel(
             for name in (LAST, FIRST):
                 cited_products(name, pair)
 
+        def subtractions(pair):
+            for u in (2 * pair, 2 * pair + 1):
+                if u in GPSIMD_DIFFERENCES:
+                    subtract_on_gpsimd(u)
+
         def differences(pair):
             for u in (2 * pair, 2 * pair + 1):
                 absolute_difference(u)
@@ -337,6 +355,7 @@ def tile_list_citation_topic_scores_kernel(
         for piece in range(VECTOR_PIECES):
             round_w1(piece // PACK, piece % PACK)
         both_products(1)
+        subtractions(1)
         for piece in range(VECTOR_PIECES, PASSES * PACK):
             round_w1(piece // PACK, piece % PACK)
         differences(0)
@@ -345,31 +364,36 @@ def tile_list_citation_topic_scores_kernel(
         gather_passes(LAST, CITED_CUTS[3])
         for a in range(PASSES):
             quantize_w1(a)
-        round_w4()
         gather_passes(FIRST, CITED_CUTS[3])
         gather_passes(OWN, OWN_CUTS[1])
         gather_scales(OWN, S // 2, S // 2)
-        gather_passes(OWN, OWN_CUTS[2])
+        for cut in OWN_CUTS[2:]:
+            gather_passes(OWN, cut)
         both_products(2)
+        subtractions(2)
         differences(1)
         cited_products(LAST, 3)
         for u in range(2):
             own_product(u)
+        round_w4()
         cited_products(FIRST, 3)
+        subtractions(3)
         differences(2)
         for u in range(2, EARLY_OWN):
             own_product(u)
-        differences(3)
-        for u in range(EARLY_OWN, 8):
-            own_product(u)
+        relu(0, PAIR)
         add_distance(2)
         add_distance(3)
-        quantize_w4()
-        relu(0 * PAIR, PAIR)
-        add_distance(4)
         relu(1 * PAIR, PAIR)
+        differences(3)
+        for u in range(EARLY_OWN, 7):
+            own_product(u)
+        add_distance(4)
+        quantize_w4()
         quantize_h(0 * PAIR, PAIR)
         scores(0 * PAIR)
+        for u in range(7, TILES):
+            own_product(u)
         add_distance(5)
         quantize_h(1 * PAIR, PAIR)
         scores(1 * PAIR)

@@ -25,25 +25,13 @@ QUADS = 4
 TILE = 128
 TILES = S // TILE
 PAIR = 2 * TILE
-VECTOR_PIECES = 5
-ROUND_STEPS = {1: (6, 7)}
-PAIRS = TILES // 2
-EARLY_OWN = 6
-SCALAR_RELUS = (0, 1)
+PAIRS = S // PAIR
+HALF = S // 2
 OWN, FIRST, LAST = "own", "first", "last"
 
-CITED_CUTS = ((0, 256), (256, 256), (512, 256), (768, 256))
-OWN_CUTS = ((0, 256), (256, 256), (512, 256), (768, 256))
-WORD_SLOTS = {(OWN, 0): 3, (OWN, 1): 3, (FIRST, 0): 4, (FIRST, 1): 4, (LAST, 0): 4, (LAST, 1): 4}
-STAGE_SLOTS = 4
 BANKS = 8
-GPSIMD_DIFFERENCES = (3, 4, 5)
-GPSIMD_TILES = 2
-WARM_PASSES = 3
-VECTOR_TILES = 49
-SCALAR_TILES = 20
-CITED_LEAD = 1
-OWN_LAG = 7
+VECTOR_TILES = 43
+SCALAR_TILES = 33
 
 
 def tile_list_citation_topic_scores_kernel(
@@ -53,205 +41,211 @@ def tile_list_citation_topic_scores_kernel(
     with ExitStack() as ctx:
         lists = ctx.enter_context(tc.tile_pool(name="lists", bufs=1))
         keep = ctx.enter_context(tc.tile_pool(name="keep", bufs=1))
-        ring = ctx.enter_context(tc.tile_pool(name="ring", bufs=STAGE_SLOTS))
-        psum = ctx.enter_context(tc.psum_pool(name="psum", bufs=1))
+        made = ctx.enter_context(tc.tile_pool(name="made", bufs=1))
+        psum = ctx.enter_context(tc.psum_pool(name="psum", bufs=BANKS))
 
-        offsets = {name: lists.tile([P, S // 16], U16, name="offsets_" + name) for name in (OWN, FIRST, LAST)}
-
-        def kept(shape, dtype, name):
-            return keep.tile(shape, dtype, name=name, align_bytes=64)
-
-        table_words = [kept([P, T], I32, "table_words%d" % a) for a in range(PASSES)]
-        table_scales = kept([P, T // 4], I32, "table_scales")
-        weight_scales = kept([P, 3, H // 4], I32, "weight_scales")
-        w2_codes = kept([P, PASSES, H // 2], I32, "w2_codes")
-        identity = kept([P, P], F32, "identity")
-        w3_codes = [kept([P, H], I32, "w3_codes%d" % a) for a in range(PASSES)]
-        w1_raw = [kept([P, PACK, H], F32, "w1_raw%d" % a) for a in range(PASSES)]
-        w1_bf16 = [keep.tile([P, PACK * H], BF16, name="w1_bf16_%d" % a, tag="w1_bf16_%d" % a, align_bytes=64) for a in range(PASSES)]
-        w1_codes = {}
-        w1_scales = kept([P, PASSES * H], U8, "w1_scales")
-        w4_raw = kept([P, PACK, N], F32, "w4_raw")
-        w4_bf16, w4_codes = [], []
-        w4_scales = kept([P, N], U8, "w4_scales")
-        warm = kept([P, 1], F32, "warm")
-        bias = kept([P, 2], F32, "bias")
-        made = ctx.enter_context(tc.tile_pool(name="made", bufs=VECTOR_TILES))
+        def kept(shape, dtype, name, tag=None):
+            return keep.tile(shape, dtype, name=name, tag=tag or name, align_bytes=64)
 
         def vector_tile(shape, dtype, name):
-            return made.tile(shape, dtype, name=name, tag="vector", align_bytes=64)
+            return made.tile(shape, dtype, name=name, tag="vector", bufs=VECTOR_TILES, align_bytes=64)
 
         def scalar_tile(shape, dtype, name):
             return made.tile(shape, dtype, name=name, tag="scalar", bufs=SCALAR_TILES, align_bytes=64)
 
-        def gpsimd_tile(shape, dtype, name):
-            return made.tile(shape, dtype, name=name, tag="gpsimd", bufs=6, align_bytes=64)
+        def next_bank(shape, name):
+            return psum.tile(shape, F32, name=name, tag="bank")
 
-        picked_scales = {}
-        first_scales_pass1 = kept([P, S // 4], I32, "first_scales_pass1")
-        distance = {}
-        h_sum, h_bf16, h_codes = {}, {}, {}
+        offsets = {name: lists.tile([P, S // 16], U16, name="offsets_" + name) for name in (OWN, FIRST, LAST)}
+        table_words = [kept([P, T], I32, "table_words%d" % a) for a in range(PASSES)]
+        table_scales = kept([P, T // 4], I32, "table_scales")
+        weight_scales = kept([P, 3, H // 4], I32, "weight_scales")
+        w2_codes = kept([P, PASSES, H // 2], I32, "w2_codes")
+        w3_codes = [kept([P, H], I32, "w3_codes%d" % a) for a in range(PASSES)]
+        w1_raw = [kept([P, PACK, H], F32, "w1_raw%d" % a) for a in range(PASSES)]
+        w1_bf16 = [kept([P, PACK * H], BF16, "w1_bf16_%d" % a) for a in range(PASSES)]
+        w1_scales = kept([P, PASSES, H], U8, "w1_scales")
+        w4_raw = kept([P, PACK, N], F32, "w4_raw")
+        w4_scales = kept([P, N], U8, "w4_scales")
         h_scales = kept([P, S], U8, "h_scales")
-        own_banks, difference = {}, {}
+        first_scales_pass1 = kept([P, S // 4], I32, "first_scales_pass1")
+        identity = kept([P, P], F32, "identity")
+        bias = kept([P, 2], F32, "bias")
         picked_words = {}
+        picked_scales = {}
         staged = {}
+        distance = {}
+        cited_bank = {}
+        own_bank = {}
+        h_sum = {}
+        h_bf16, h_codes = {}, {}
+        w1_codes = {}
+        w4_tiles = {}
+
+        def tiles_of(pair):
+            return (2 * pair, 2 * pair + 1)
 
 
-        def load_table_words(a):
-            nc.sync.dma_start(out=table_words[a][:], in_=tab_words[a].rearrange("p t i -> p (t i)").bitcast(I32))
+        def load_words(tile, words):
+            nc.sync.dma_start(out=tile[:], in_=words.rearrange("p n i -> p (n i)").bitcast(I32))
 
-        def load_w3_words(a):
-            nc.sync.dma_start(out=w3_codes[a][:], in_=w3_words[a].rearrange("p e i -> p (e i)").bitcast(I32))
+        def load_both_planes(tile, scales):
+            for q in range(QUADS):
+                nc.sync.dma_start(out=tile[32 * q : 32 * q + 8, :], in_=scales.bitcast(I32)[:, 4 * q : 4 * q + 4, :])
 
-        def load_table_scales(q):
-            rows = tab_scales.bitcast(I32)[:, 4 * q : 4 * q + 4, :]
-            nc.sync.dma_start(out=table_scales[32 * q : 32 * q + 8, :], in_=rows)
+        def load_w2_planes():
+            for q in range(QUADS):
+                rows = w2_scales.bitcast(I32)[:, 4 * q : 4 * q + 4, :].rearrange("a r e -> r a e")
+                nc.sync.dma_start(out=weight_scales[32 * q : 32 * q + 4, 0:PASSES, :], in_=rows)
 
-        def load_w3_scales(q):
-            rows = w3_scales.bitcast(I32)[:, 4 * q : 4 * q + 4, :]
-            nc.sync.dma_start(out=weight_scales[32 * q : 32 * q + 8, 2, :], in_=rows)
-
-        def load_w2_scales(q):
-            rows = w2_scales.bitcast(I32)[:, 4 * q : 4 * q + 4, :].rearrange("a r e -> r a e")
-            nc.sync.dma_start(out=weight_scales[32 * q : 32 * q + 4, 0:2, :], in_=rows)
+        def load_w1(a):
+            rows = w1[P * PACK * a : P * PACK * (a + 1), :]
+            nc.sync.dma_start(out=w1_raw[a][:], in_=rows.rearrange("(p j) r -> p j r", j=PACK))
 
 
-        def gather_scales(name, start=0, count=S):
+        def gather_scales(name, start, count):
+            plane = vector_tile([P, count], U8, "scales_" + name)
             window = table_scales[:].bitcast(U8)
-            plane = vector_tile([P, count], U8, "picked_scales_" + name)
             nc.vector.tensor_copy(plane[:], window.indirect(offsets[name][:, start // 16 : (start + count) // 16]))
             for k in range(count // TILE):
                 picked_scales[name, start // TILE + k] = plane[:, k * TILE : (k + 1) * TILE]
             return plane
 
-        def gather_words(name, a, start, count):
-            words = vector_tile([P, count], U32, "words_%s%d" % (name, a))
+        def gather_words(name, a, pair):
+            words = vector_tile([P, PAIR], U32, "words_%s%d" % (name, a))
             window = table_words[a][:].bitcast(U32)
-            nc.vector.tensor_copy(words[:], window.indirect(offsets[name][:, start // 16 : (start + count) // 16]))
-            for k in range(count // TILE):
-                picked_words[name, a, start // TILE + k] = words[:, k * TILE : (k + 1) * TILE]
+            columns = slice(pair * PAIR // 16, (pair + 1) * PAIR // 16)
+            nc.vector.tensor_copy(words[:], window.indirect(offsets[name][:, columns]))
+            for k, u in enumerate(tiles_of(pair)):
+                picked_words[name, a, u] = words[:, k * TILE : (k + 1) * TILE]
 
-        def gather_cited_words(start, count):
-            for name in (LAST, FIRST):
-                for a in range(PASSES):
-                    gather_words(name, a, start, count)
+        def gather_passes(name, pair):
+            for a in range(PASSES):
+                gather_words(name, a, pair)
 
 
-        def round_w1(a, t):
+        def round_on_gpsimd(dst, src):
+            nc.gpsimd.tensor_scalar(out=dst, in0=src, scalar1=1.0, scalar2=0.0, op0=ALU.mult, op1=ALU.add)
+
+        def round_w1_on_gpsimd(a):
+            src = w1_raw[a][:].rearrange("p j (g t i) -> p t g i j", t=PACK, i=RUN)
+            dst = w1_bf16[a][:].rearrange("p (t g i j) -> p t g i j", t=PACK, i=RUN, j=PACK)
+            for t in range(PACK):
+                round_on_gpsimd(dst[:, t], src[:, t])
+
+        def round_w1_on_scalar(a):
             src = w1_raw[a][:].rearrange("p j (g t u i) -> p t g u j i", t=PACK, u=2, i=4)
             dst = w1_bf16[a][:].rearrange("p (t g u i j) -> p t g u j i", t=PACK, u=2, i=4, j=PACK)
-            if PACK * a + t < VECTOR_PIECES:
-                nc.gpsimd.tensor_scalar(
-                    out=w1_bf16[a][:].rearrange("p (t g i j) -> p t g i j", t=PACK, i=RUN, j=PACK)[:, t],
-                    in0=w1_raw[a][:].rearrange("p j (g t i) -> p t g i j", t=PACK, i=RUN)[:, t],
-                    scalar1=1.0, scalar2=0.0, op0=ALU.mult, op1=ALU.add,
-                )
-            else:
+            for t in range(PACK):
                 nc.scalar.copy(out=dst[:, t], in_=src[:, t])
 
         def quantize_w1(a):
-            cols = slice(a * H, (a + 1) * H)
             w1_codes[a] = vector_tile([P, H], U32, "w1_codes%d" % a)
-            nc.vector.quantize_mx(out=w1_codes[a][:].bitcast(FP8X4), scales=w1_scales[:, cols], in_=w1_bf16[a][:])
+            nc.vector.quantize_mx(out=w1_codes[a][:].bitcast(FP8X4), scales=w1_scales[:, a, :], in_=w1_bf16[a][:])
 
         def round_w4():
-            w4_bf16.append(gpsimd_tile([P, PACK * N], BF16, "w4_bf16"))
-            nc.gpsimd.tensor_scalar(
-                out=w4_bf16[0][:].rearrange("p (e m t) -> p e m t", e=2, t=PACK),
-                in0=w4_raw[:].rearrange("p t (m e) -> p e m t", e=2),
-                scalar1=1.0, scalar2=0.0, op0=ALU.mult, op1=ALU.add,
+            w4_tiles["bf16"] = kept([P, PACK * N], BF16, "w4_bf16", tag="w1_bf16_%d" % (PASSES - 1))
+            round_on_gpsimd(
+                w4_tiles["bf16"][:].rearrange("p (e m t) -> p e m t", e=2, t=PACK),
+                w4_raw[:].rearrange("p t (m e) -> p e m t", e=2),
             )
 
         def quantize_w4():
-            w4_codes.append(vector_tile([P, N], U32, "w4_codes"))
-            nc.vector.quantize_mx(out=w4_codes[0][:].bitcast(FP8X4), scales=w4_scales[:], in_=w4_bf16[0][:])
+            w4_tiles["codes"] = vector_tile([P, N], U32, "w4_codes")
+            nc.vector.quantize_mx(
+                out=w4_tiles["codes"][:].bitcast(FP8X4), scales=w4_scales[:], in_=w4_tiles["bf16"][:]
+            )
 
 
         def by_token(bank):
+            return bank[:].rearrange("p t n -> p n t")
+
+        def by_two_tokens(bank):
             return bank[:].rearrange("p t (m i) -> p m t i", i=2)
 
         def cited_products(name, pair):
             planes = weight_scales[:].bitcast(U8)
-            sign = -1.0 if name == LAST else 1.0
-            for u in (2 * pair, 2 * pair + 1):
-                tokens = slice(u * TILE, (u + 1) * TILE)
-                bank = psum.tile([P, H], F32, name="cited_bank", tag="bank", bufs=BANKS)
+            for u in tiles_of(pair):
+                bank = next_bank([P, H], "cited_bank")
                 for a in range(PASSES):
-                    if name == FIRST:
-                        weight, weight_plane = w2_codes[:, a, :].bitcast(U8).bitcast(FP4X4), planes[:, a, :]
-                        token_plane = picked_scales[FIRST, u] if a == 0 else first_scales_pass1[:].bitcast(U8)[:, tokens]
-                    else:
-                        weight, weight_plane = w3_codes[a][:].bitcast(FP8X4), planes[4 * a :, 2, :]
+                    if name == LAST:
+                        weight, weight_plane = w3_codes[a][:].bitcast(FP8X4), planes[4 * a :, PASSES, :]
                         token_plane = picked_scales[LAST, u][4 * a :, :]
+                    else:
+                        weight, weight_plane = w2_codes[:, a, :].bitcast(U8).bitcast(FP4X4), planes[:, a, :]
+                        moved_plane = first_scales_pass1[:].bitcast(U8)[:, u * TILE : (u + 1) * TILE]
+                        token_plane = moved_plane if a else picked_scales[FIRST, u]
                     nc.tensor.matmul_mx(
                         out=bank[:], lhsT=picked_words[name, a, u].bitcast(FP8X4), lhsT_scale=token_plane,
                         rhs=weight, rhs_scale=weight_plane, start=(a == 0), stop=(a == PASSES - 1),
                     )
-                staged[name, u] = ring.tile([P, PACK, H // (PACK * RUN), RUN], F32, name="staged_" + name)
+                cited_bank[name, u] = bank
+
+        def stage(name, pair):
+            for u in tiles_of(pair):
+                staged[name, u] = scalar_tile([P, PACK, H // (PACK * RUN), RUN], F32, "staged_" + name)
+                sums = cited_bank[name, u][:].rearrange("p (g t i) -> p t g i", t=PACK, i=RUN)
                 nc.scalar.activation(
-                    out=staged[name, u][:], in_=bank[:].rearrange("p (g t i) -> p t g i", t=PACK, i=RUN),
-                    func=ACT.Copy, scale=sign,
+                    out=staged[name, u][:], in_=sums, func=ACT.Copy, scale=-1.0 if name == LAST else 1.0
                 )
 
-        def subtract_on_gpsimd(u):
-            shape = [P, PACK, H // (PACK * RUN), RUN]
-            if u == 4:
-                difference[u] = keep.tile(shape, F32, name="difference", tag="w1_bf16_1", align_bytes=64)
-            else:
-                difference[u] = gpsimd_tile(shape, F32, "difference")
-            nc.gpsimd.tensor_tensor(out=difference[u][:], in0=staged[FIRST, u][:], in1=staged[LAST, u][:], op=ALU.add)
+        def both_products(pair):
+            for name in (LAST, FIRST):
+                cited_products(name, pair)
+                stage(name, pair)
 
-        def absolute_difference(u):
-            bank = psum.tile([P, PACK, TILE], F32, name="diff_bank", tag="bank", bufs=BANKS)
-            terms = (difference[u],) if u in GPSIMD_DIFFERENCES else (staged[FIRST, u], staged[LAST, u])
-            for t in range(PACK):
-                for k, term in enumerate(terms):
-                    nc.tensor.matmul(
-                        out=bank[:, t, :], lhsT=term[:, t].rearrange("p g i -> p (g i)"), rhs=identity[:],
-                        start=(k == 0), stop=(k == len(terms) - 1), is_transpose=True,
-                    )
-            if u < GPSIMD_TILES:
-                distance[u] = scalar_tile([P, TILE, PACK], F32, "distance")
-                nc.scalar.activation(out=distance[u][:], in_=bank[:].rearrange("p t n -> p n t"), func=ACT.Abs)
-            else:
-                distance[u] = scalar_tile([P, TILE // 2, PACK, 2], F32, "distance")
-                nc.scalar.activation(out=distance[u][:], in_=by_token(bank), func=ACT.Abs)
+        def absolute_differences(pair):
+            for u in tiles_of(pair):
+                bank = next_bank([P, PACK, TILE], "diff_bank")
+                for t in range(PACK):
+                    for name in (FIRST, LAST):
+                        nc.tensor.matmul(
+                            out=bank[:, t, :], lhsT=staged[name, u][:, t].rearrange("p g i -> p (g i)"),
+                            rhs=identity[:], start=(name == FIRST), stop=(name == LAST), is_transpose=True,
+                        )
+                walk = by_two_tokens(bank) if pair else by_token(bank)
+                distance[u] = scalar_tile(list(walk.shape), F32, "distance")
+                nc.scalar.activation(out=distance[u][:], in_=walk, func=ACT.Abs)
 
         def own_product(u):
-            bank = psum.tile([P, PACK, TILE], F32, name="own_bank", tag="bank", bufs=BANKS)
+            own_bank[u] = next_bank([P, PACK, TILE], "own_bank")
             for t in range(PACK):
+                channels = slice(t * P, (t + 1) * P)
                 for a in range(PASSES):
-                    channels = slice(a * H + t * P, a * H + (t + 1) * P)
                     nc.tensor.matmul_mx(
-                        out=bank[:, t, :], lhsT=w1_codes[a][:, t * P : (t + 1) * P].bitcast(FP8X4),
-                        lhsT_scale=w1_scales[:, channels], rhs=picked_words[OWN, a, u].bitcast(FP8X4),
+                        out=own_bank[u][:, t, :], lhsT=w1_codes[a][:, channels].bitcast(FP8X4),
+                        lhsT_scale=w1_scales[:, a, channels], rhs=picked_words[OWN, a, u].bitcast(FP8X4),
                         rhs_scale=picked_scales[OWN, u][4 * a :, :], start=(a == 0), stop=(a == PASSES - 1),
                     )
-            own_banks[u] = bank
-            if u < GPSIMD_TILES:
-                own = scalar_tile([P, TILE, PACK], F32, "own")
-                nc.scalar.activation(out=own[:], in_=bank[:].rearrange("p t n -> p n t"), func=ACT.Copy)
-                if u % 2 == 0:
-                    h_sum[u // 2] = gpsimd_tile([P, 2, TILE, PACK], BF16, "h_sum_early")
-                nc.gpsimd.tensor_tensor(out=h_sum[u // 2][:, u % 2], in0=own[:], in1=distance[u][:], op=ALU.add)
 
-        def add_distance(u):
+        def add_on_gpsimd(u):
+            own = scalar_tile([P, TILE, PACK], F32, "own")
+            nc.scalar.activation(out=own[:], in_=by_token(own_bank[u]), func=ACT.Copy)
+            if u % 2 == 0:
+                h_sum[u // 2] = kept([P, 2, TILE, PACK], BF16, "h_sum_first")
+            nc.gpsimd.tensor_tensor(out=h_sum[u // 2][:, u % 2], in0=own[:], in1=distance[u][:], op=ALU.add)
+
+        def add_on_vector(u):
             if u % 2 == 0:
                 h_sum[u // 2] = vector_tile([P, 2, TILE, PACK], BF16, "h_sum")
             nc.vector.tensor_tensor(
-                out=h_sum[u // 2][:, u % 2].rearrange("p (m i) t -> p m t i", i=2), in0=by_token(own_banks[u]),
+                out=h_sum[u // 2][:, u % 2].rearrange("p (m i) t -> p m t i", i=2), in0=by_two_tokens(own_bank[u]),
                 in1=distance[u][:], op=ALU.add,
             )
 
-        def relu(start, count):
+        def sums_of(start, count):
             first = PACK * (start % PAIR)
-            values = h_sum[start // PAIR][:].rearrange("p u n t -> p (u n t)")[:, first : first + PACK * count]
-            if start // PAIR in SCALAR_RELUS:
-                h_bf16[start] = scalar_tile([P, PACK * count], BF16, "h_relu")
-                nc.scalar.activation(out=h_bf16[start][:], in_=values, func=ACT.Relu)
-            else:
-                h_bf16[start] = vector_tile([P, PACK * count], BF16, "h_bf16")
-                nc.vector.tensor_scalar(out=h_bf16[start][:], in0=values, scalar1=0.0, scalar2=None, op0=ALU.max)
+            return h_sum[start // PAIR][:].rearrange("p u n t -> p (u n t)")[:, first : first + PACK * count]
+
+        def relu_on_scalar(pair):
+            h_bf16[pair * PAIR] = scalar_tile([P, PACK * PAIR], BF16, "h_relu")
+            nc.scalar.activation(out=h_bf16[pair * PAIR][:], in_=sums_of(pair * PAIR, PAIR), func=ACT.Relu)
+
+        def relu_on_vector(start, count):
+            h_bf16[start] = vector_tile([P, PACK * count], BF16, "h_bf16")
+            nc.vector.tensor_scalar(
+                out=h_bf16[start][:], in0=sums_of(start, count), scalar1=0.0, scalar2=None, op0=ALU.max
+            )
 
         def quantize_h(start, count):
             h_codes[start] = vector_tile([P, count], U32, "h_codes")
@@ -262,7 +256,7 @@ def tile_list_citation_topic_scores_kernel(
         def score_product(sums, e, start, count):
             classes = slice(e * P, (e + 1) * P)
             nc.tensor.matmul_mx(
-                out=sums, lhsT=w4_codes[0][:, classes].bitcast(FP8X4), lhsT_scale=w4_scales[:, classes],
+                out=sums, lhsT=w4_tiles["codes"][:, classes].bitcast(FP8X4), lhsT_scale=w4_scales[:, classes],
                 rhs=h_codes[start][:].bitcast(FP8X4), rhs_scale=h_scales[:, start : start + count],
                 start=True, stop=True,
             )
@@ -276,145 +270,115 @@ def tile_list_citation_topic_scores_kernel(
         def store(start, count, result):
             nc.sync.dma_start(out=out.rearrange("(m e) s -> m e s", e=2)[:, :, start : start + count], in_=result[:])
 
-        def scores(start):
-            bank = psum.tile([P, 2, PAIR], F32, name="score_bank", tag="bank", bufs=BANKS)
+        def finish_pair(pair):
+            quantize_h(pair * PAIR, PAIR)
+            bank = next_bank([P, 2, PAIR], "score_bank")
             result = scalar_tile([P, 2, PAIR], F32, "result")
             for e in range(2):
-                score_product(bank[:, e, :], e, start, PAIR)
+                score_product(bank[:, e, :], e, pair * PAIR, PAIR)
             for e in range(2):
                 add_bias_on_scalar(result[:, e, :], bank[:, e, :], e)
-            store(start, PAIR, result)
+            store(pair * PAIR, PAIR, result)
 
 
         nc.gpsimd.memset(table_scales[:], 0)
         nc.vector.memset(weight_scales[:], 0)
         nc.vector.memset(first_scales_pass1[:], 0)
         make_identity(nc, identity[:])
-        nc.scalar.activation(out=warm[:], in_=identity[:, 0:1], func=ACT.Abs)
 
         nc.sync.dma_start(offsets[FIRST][:], offs2)
-        for q in range(QUADS):
-            load_table_scales(q)
+        load_both_planes(table_scales, tab_scales)
         nc.sync.dma_start(offsets[LAST][:], offs3)
-        load_table_words(0)
-        load_w3_words(0)
-        load_w3_scales(0)
-        load_w3_scales(1)
-        load_w3_scales(2)
-        load_w3_scales(3)
-        load_table_words(1)
-        load_w3_words(1)
+        load_words(table_words[0], tab_words[0])
+        load_words(w3_codes[0], w3_words[0])
+        load_both_planes(weight_scales[:, PASSES, :], w3_scales)
+        load_words(table_words[1], tab_words[1])
+        load_words(w3_codes[1], w3_words[1])
         nc.sync.dma_start(out=w2_codes[:], in_=w2_words.rearrange("a p e -> p a e").bitcast(I32))
-        first_scales = gather_scales(FIRST)
+        first_scales = gather_scales(FIRST, 0, S)
         nc.sync.dma_start(out=first_scales_pass1[0:112, :], in_=first_scales[4:116, :].bitcast(I32))
-        load_w2_scales(0)
-        load_w2_scales(1)
-        load_w2_scales(2)
-        load_w2_scales(3)
-        for a in range(PASSES):
-            rows = w1[P * PACK * a : P * PACK * (a + 1), :]
-            nc.sync.dma_start(out=w1_raw[a][:], in_=rows.rearrange("(p j) r -> p j r", j=PACK))
-            if a == 0:
-                nc.sync.dma_start(offsets[OWN][:], offs)
+        load_w2_planes()
+        load_w1(0)
+        nc.sync.dma_start(offsets[OWN][:], offs)
+        load_w1(1)
         for t in range(PACK):
             nc.sync.dma_start(out=w4_raw[:, t, :], in_=w4.rearrange("(g t i) n -> t g i n", t=PACK, i=RUN)[t])
         nc.sync.dma_start(out=bias[:], in_=b.rearrange("(m e) -> m e", e=2))
 
-        gather_scales(LAST, 0, S // 2)
-        idle_bank = psum.tile([P, H], F32, name="idle_bank", tag="bank", bufs=BANKS)
-        for k in range(WARM_PASSES):
-            w3_plane = weight_scales[:].bitcast(U8)[:, 2, :]
-            nc.tensor.matmul_mx(
-                out=idle_bank[:], lhsT=w3_codes[0][:, :P].bitcast(FP8X4), lhsT_scale=w3_plane[:, :P],
-                rhs=w3_codes[0][:].bitcast(FP8X4), rhs_scale=w3_plane, start=True, stop=True,
-            )
-        for name, a, cut in (
-            (LAST, 0, 0), (FIRST, 0, 0), (LAST, 0, 1), (LAST, 1, 0), (FIRST, 1, 0), (LAST, 1, 1), (FIRST, 0, 1), (FIRST, 1, 1)
-        ):
-            gather_words(name, a, *CITED_CUTS[cut])
-        def both_products(pair):
-            for name in (LAST, FIRST):
-                cited_products(name, pair)
-
-        def subtractions(pair):
-            for u in (2 * pair, 2 * pair + 1):
-                if u in GPSIMD_DIFFERENCES:
-                    subtract_on_gpsimd(u)
-
-        def differences(pair):
-            for u in (2 * pair, 2 * pair + 1):
-                absolute_difference(u)
-
-        def gather_passes(name, cut):
-            for a in range(PASSES):
-                gather_words(name, a, *cut)
+        gather_scales(LAST, 0, HALF)
+        gather_words(LAST, 0, 0)
+        gather_words(FIRST, 0, 0)
+        gather_words(LAST, 0, 1)
+        gather_words(LAST, 1, 0)
+        gather_words(FIRST, 1, 0)
+        gather_words(LAST, 1, 1)
+        gather_passes(FIRST, 1)
 
         both_products(0)
-        gather_scales(LAST, S // 2, S // 2)
-        gather_cited_words(*CITED_CUTS[2])
-        for piece in range(VECTOR_PIECES):
-            round_w1(piece // PACK, piece % PACK)
+        gather_scales(LAST, HALF, HALF)
+        gather_passes(LAST, 2)
+        gather_passes(FIRST, 2)
+        round_w1_on_gpsimd(0)
         both_products(1)
-        subtractions(1)
-        for piece in range(VECTOR_PIECES, PASSES * PACK):
-            round_w1(piece // PACK, piece % PACK)
-        differences(0)
-        gather_scales(OWN, 0, S // 2)
-        gather_passes(OWN, OWN_CUTS[0])
-        gather_passes(LAST, CITED_CUTS[3])
+        round_w1_on_scalar(1)
+        absolute_differences(0)
+
+        gather_scales(OWN, 0, HALF)
+        gather_passes(OWN, 0)
+        gather_passes(LAST, 3)
         for a in range(PASSES):
             quantize_w1(a)
-        gather_passes(FIRST, CITED_CUTS[3])
-        gather_passes(OWN, OWN_CUTS[1])
-        gather_scales(OWN, S // 2, S // 2)
-        for cut in OWN_CUTS[2:]:
-            gather_passes(OWN, cut)
-        both_products(2)
-        subtractions(2)
-        differences(1)
-        cited_products(LAST, 3)
-        for u in range(2):
-            own_product(u)
         round_w4()
-        cited_products(FIRST, 3)
-        subtractions(3)
-        differences(2)
-        for u in range(2, EARLY_OWN):
-            own_product(u)
-        relu(0, PAIR)
-        add_distance(2)
-        add_distance(3)
-        relu(1 * PAIR, PAIR)
-        differences(3)
-        for u in range(EARLY_OWN, 7):
-            own_product(u)
-        add_distance(4)
-        quantize_w4()
-        quantize_h(0 * PAIR, PAIR)
-        scores(0 * PAIR)
-        for u in range(7, TILES):
-            own_product(u)
-        add_distance(5)
-        quantize_h(1 * PAIR, PAIR)
-        scores(1 * PAIR)
-        relu(2 * PAIR, PAIR)
-        add_distance(6)
-        quantize_h(2 * PAIR, PAIR)
-        scores(2 * PAIR)
-        add_distance(7)
-        for u in (TILES - 2, TILES - 1):
-            relu(u * TILE, TILE)
+        gather_passes(FIRST, 3)
+        gather_passes(OWN, 1)
+        gather_scales(OWN, HALF, HALF)
+        gather_passes(OWN, 2)
+        gather_passes(OWN, 3)
 
-        tail, stores = [], []
-        for u in (TILES - 2, TILES - 1):
-            quantize_h(u * TILE, TILE)
-            result = scalar_tile([P, 2, TILE], F32, "result")
-            for e, add_bias in enumerate((add_bias_on_scalar, add_bias_on_vector)):
-                bank = psum.tile([P, TILE], F32, name="score_bank", tag="bank", bufs=BANKS)
-                score_product(bank[:], e, u * TILE, TILE)
-                tail.append((add_bias, result, bank, e))
-            stores.append((u * TILE, TILE, result))
-        for add_bias, result, bank, e in tail:
-            add_bias(result[:, e, :], bank[:], e)
-        for args in stores:
-            store(*args)
+        both_products(2)
+        absolute_differences(1)
+        cited_products(LAST, 3)
+        for u in tiles_of(0):
+            own_product(u)
+            add_on_gpsimd(u)
+        stage(LAST, 3)
+        cited_products(FIRST, 3)
+        stage(FIRST, 3)
+        absolute_differences(2)
+
+        for u in tiles_of(1) + tiles_of(2):
+            own_product(u)
+        relu_on_scalar(0)
+        for u in tiles_of(1):
+            add_on_vector(u)
+        relu_on_scalar(1)
+        absolute_differences(3)
+
+        own_product(TILES - 2)
+        for pair in range(PAIRS - 1):
+            u = HALF // TILE + pair
+            add_on_vector(u)
+            if pair == 0:
+                quantize_w4()
+            finish_pair(pair)
+            if pair == 0:
+                own_product(TILES - 1)
+            if u % 2 == 1:
+                relu_on_vector(u // 2 * PAIR, PAIR)
+        add_on_vector(TILES - 1)
+
+        last_starts = [u * TILE for u in tiles_of(PAIRS - 1)]
+        for start in last_starts:
+            relu_on_vector(start, TILE)
+        results, banks = {}, {}
+        for start in last_starts:
+            quantize_h(start, TILE)
+            results[start] = scalar_tile([P, 2, TILE], F32, "result")
+            for e in range(2):
+                banks[start, e] = next_bank([P, TILE], "score_bank")
+                score_product(banks[start, e][:], e, start, TILE)
+        for start in last_starts:
+            add_bias_on_scalar(results[start][:, 0, :], banks[start, 0][:], 0)
+            add_bias_on_vector(results[start][:, 1, :], banks[start, 1][:], 1)
+        for start in last_starts:
+            store(start, TILE, results[start])

@@ -29,9 +29,10 @@ PAIRS = S // PAIR
 HALF = S // 2
 OWN, FIRST, LAST = "own", "first", "last"
 
+GPSIMD_TILES = 2
 BANKS = 8
 VECTOR_TILES = 43
-SCALAR_TILES = 33
+SCALAR_TILES = 35
 
 
 def tile_list_citation_topic_scores_kernel(
@@ -76,6 +77,9 @@ def tile_list_citation_topic_scores_kernel(
         staged = {}
         distance = {}
         cited_bank = {}
+        diff_bank = {}
+        own_staged = {}
+        score_bank = {}
         own_bank = {}
         h_sum = {}
         h_bf16, h_codes = {}, {}
@@ -89,9 +93,9 @@ def tile_list_citation_topic_scores_kernel(
         def load_words(tile, words):
             nc.sync.dma_start(out=tile[:], in_=words.rearrange("p n i -> p (n i)").bitcast(I32))
 
-        def load_both_planes(tile, scales):
+        def load_both_planes(queue, tile, scales):
             for q in range(QUADS):
-                nc.sync.dma_start(out=tile[32 * q : 32 * q + 8, :], in_=scales.bitcast(I32)[:, 4 * q : 4 * q + 4, :])
+                queue.dma_start(out=tile[32 * q : 32 * q + 8, :], in_=scales.bitcast(I32)[:, 4 * q : 4 * q + 4, :])
 
         def load_w2_planes():
             for q in range(QUADS):
@@ -111,32 +115,37 @@ def tile_list_citation_topic_scores_kernel(
                 picked_scales[name, start // TILE + k] = plane[:, k * TILE : (k + 1) * TILE]
             return plane
 
-        def gather_words(name, a, pair):
-            words = vector_tile([P, PAIR], U32, "words_%s%d" % (name, a))
+        def gather_words(name, a, pair, pairs=1):
+            words = vector_tile([P, pairs * PAIR], U32, "words_%s%d" % (name, a))
             window = table_words[a][:].bitcast(U32)
-            columns = slice(pair * PAIR // 16, (pair + 1) * PAIR // 16)
+            columns = slice(pair * PAIR // 16, (pair + pairs) * PAIR // 16)
             nc.vector.tensor_copy(words[:], window.indirect(offsets[name][:, columns]))
-            for k, u in enumerate(tiles_of(pair)):
-                picked_words[name, a, u] = words[:, k * TILE : (k + 1) * TILE]
+            for k in range(2 * pairs):
+                picked_words[name, a, 2 * pair + k] = words[:, k * TILE : (k + 1) * TILE]
 
-        def gather_passes(name, pair):
+        def gather_passes(name, pair, pairs=1):
             for a in range(PASSES):
-                gather_words(name, a, pair)
+                gather_words(name, a, pair, pairs)
+
+        def gather_first_scales(start):
+            plane = gather_scales(FIRST, start, HALF)
+            moved = first_scales_pass1[0:112, start // 4 : (start + HALF) // 4]
+            nc.sync.dma_start(out=moved, in_=plane[4:116, :].bitcast(I32))
 
 
         def round_on_gpsimd(dst, src):
             nc.gpsimd.tensor_scalar(out=dst, in0=src, scalar1=1.0, scalar2=0.0, op0=ALU.mult, op1=ALU.add)
 
-        def round_w1_on_gpsimd(a):
+        def round_w1_on_gpsimd(a, pieces=range(PACK)):
             src = w1_raw[a][:].rearrange("p j (g t i) -> p t g i j", t=PACK, i=RUN)
             dst = w1_bf16[a][:].rearrange("p (t g i j) -> p t g i j", t=PACK, i=RUN, j=PACK)
-            for t in range(PACK):
+            for t in pieces:
                 round_on_gpsimd(dst[:, t], src[:, t])
 
-        def round_w1_on_scalar(a):
+        def round_w1_on_scalar(a, pieces=range(PACK)):
             src = w1_raw[a][:].rearrange("p j (g t u i) -> p t g u j i", t=PACK, u=2, i=4)
             dst = w1_bf16[a][:].rearrange("p (t g u i j) -> p t g u j i", t=PACK, u=2, i=4, j=PACK)
-            for t in range(PACK):
+            for t in pieces:
                 nc.scalar.copy(out=dst[:, t], in_=src[:, t])
 
         def quantize_w1(a):
@@ -163,11 +172,13 @@ def tile_list_citation_topic_scores_kernel(
         def by_two_tokens(bank):
             return bank[:].rearrange("p t (m i) -> p m t i", i=2)
 
-        def cited_products(name, pair):
+        def cited_products(name, pair, passes=range(PASSES)):
             planes = weight_scales[:].bitcast(U8)
             for u in tiles_of(pair):
-                bank = next_bank([P, H], "cited_bank")
-                for a in range(PASSES):
+                if (name, u) not in cited_bank:
+                    cited_bank[name, u] = next_bank([P, H], "cited_bank")
+                bank = cited_bank[name, u]
+                for a in passes:
                     if name == LAST:
                         weight, weight_plane = w3_codes[a][:].bitcast(FP8X4), planes[4 * a :, PASSES, :]
                         token_plane = picked_scales[LAST, u][4 * a :, :]
@@ -179,7 +190,6 @@ def tile_list_citation_topic_scores_kernel(
                         out=bank[:], lhsT=picked_words[name, a, u].bitcast(FP8X4), lhsT_scale=token_plane,
                         rhs=weight, rhs_scale=weight_plane, start=(a == 0), stop=(a == PASSES - 1),
                     )
-                cited_bank[name, u] = bank
 
         def stage(name, pair):
             for u in tiles_of(pair):
@@ -194,18 +204,24 @@ def tile_list_citation_topic_scores_kernel(
                 cited_products(name, pair)
                 stage(name, pair)
 
+        def transposes(u):
+            diff_bank[u] = next_bank([P, PACK, TILE], "diff_bank")
+            for t in range(PACK):
+                for name in (FIRST, LAST):
+                    nc.tensor.matmul(
+                        out=diff_bank[u][:, t, :], lhsT=staged[name, u][:, t].rearrange("p g i -> p (g i)"),
+                        rhs=identity[:], start=(name == FIRST), stop=(name == LAST), is_transpose=True,
+                    )
+
+        def absolute(u):
+            walk = by_two_tokens(diff_bank[u]) if u >= GPSIMD_TILES else by_token(diff_bank[u])
+            distance[u] = scalar_tile(list(walk.shape), F32, "distance")
+            nc.scalar.activation(out=distance[u][:], in_=walk, func=ACT.Abs)
+
         def absolute_differences(pair):
             for u in tiles_of(pair):
-                bank = next_bank([P, PACK, TILE], "diff_bank")
-                for t in range(PACK):
-                    for name in (FIRST, LAST):
-                        nc.tensor.matmul(
-                            out=bank[:, t, :], lhsT=staged[name, u][:, t].rearrange("p g i -> p (g i)"),
-                            rhs=identity[:], start=(name == FIRST), stop=(name == LAST), is_transpose=True,
-                        )
-                walk = by_two_tokens(bank) if pair else by_token(bank)
-                distance[u] = scalar_tile(list(walk.shape), F32, "distance")
-                nc.scalar.activation(out=distance[u][:], in_=walk, func=ACT.Abs)
+                transposes(u)
+                absolute(u)
 
         def own_product(u):
             own_bank[u] = next_bank([P, PACK, TILE], "own_bank")
@@ -218,12 +234,18 @@ def tile_list_citation_topic_scores_kernel(
                         rhs_scale=picked_scales[OWN, u][4 * a :, :], start=(a == 0), stop=(a == PASSES - 1),
                     )
 
-        def add_on_gpsimd(u):
-            own = scalar_tile([P, TILE, PACK], F32, "own")
-            nc.scalar.activation(out=own[:], in_=by_token(own_bank[u]), func=ACT.Copy)
+        def copy_own(u):
+            own_staged[u] = scalar_tile([P, TILE, PACK], F32, "own")
+            nc.scalar.activation(out=own_staged[u][:], in_=by_token(own_bank[u]), func=ACT.Copy)
+
+        def sum_on_gpsimd(u):
             if u % 2 == 0:
-                h_sum[u // 2] = kept([P, 2, TILE, PACK], BF16, "h_sum_first")
-            nc.gpsimd.tensor_tensor(out=h_sum[u // 2][:, u % 2], in0=own[:], in1=distance[u][:], op=ALU.add)
+                h_sum[u // 2] = kept([P, 2, TILE, PACK], BF16, "h_sum_early%d" % (u // 2))
+            nc.gpsimd.tensor_tensor(out=h_sum[u // 2][:, u % 2], in0=own_staged[u][:], in1=distance[u][:], op=ALU.add)
+
+        def add_on_gpsimd(u):
+            copy_own(u)
+            sum_on_gpsimd(u)
 
         def add_on_vector(u):
             if u % 2 == 0:
@@ -270,15 +292,21 @@ def tile_list_citation_topic_scores_kernel(
         def store(start, count, result):
             nc.sync.dma_start(out=out.rearrange("(m e) s -> m e s", e=2)[:, :, start : start + count], in_=result[:])
 
-        def finish_pair(pair):
+        def scores(pair):
             quantize_h(pair * PAIR, PAIR)
-            bank = next_bank([P, 2, PAIR], "score_bank")
+            score_bank[pair] = next_bank([P, 2, PAIR], "score_bank")
+            for e in range(2):
+                score_product(score_bank[pair][:, e, :], e, pair * PAIR, PAIR)
+
+        def bias_and_store(pair):
             result = scalar_tile([P, 2, PAIR], F32, "result")
             for e in range(2):
-                score_product(bank[:, e, :], e, pair * PAIR, PAIR)
-            for e in range(2):
-                add_bias_on_scalar(result[:, e, :], bank[:, e, :], e)
+                add_bias_on_scalar(result[:, e, :], score_bank[pair][:, e, :], e)
             store(pair * PAIR, PAIR, result)
+
+        def finish_pair(pair):
+            scores(pair)
+            bias_and_store(pair)
 
 
         nc.gpsimd.memset(table_scales[:], 0)
@@ -286,46 +314,48 @@ def tile_list_citation_topic_scores_kernel(
         nc.vector.memset(first_scales_pass1[:], 0)
         make_identity(nc, identity[:])
 
-        nc.sync.dma_start(offsets[FIRST][:], offs2)
-        load_both_planes(table_scales, tab_scales)
         nc.sync.dma_start(offsets[LAST][:], offs3)
-        load_words(table_words[0], tab_words[0])
         load_words(w3_codes[0], w3_words[0])
-        load_both_planes(weight_scales[:, PASSES, :], w3_scales)
+        load_both_planes(nc.sync, table_scales, tab_scales)
+        nc.sync.dma_start(offsets[FIRST][:], offs2)
+        load_words(table_words[0], tab_words[0])
+        load_both_planes(nc.sync, weight_scales[:, PASSES, :], w3_scales)
         load_words(table_words[1], tab_words[1])
         load_words(w3_codes[1], w3_words[1])
         nc.sync.dma_start(out=w2_codes[:], in_=w2_words.rearrange("a p e -> p a e").bitcast(I32))
-        first_scales = gather_scales(FIRST, 0, S)
-        nc.sync.dma_start(out=first_scales_pass1[0:112, :], in_=first_scales[4:116, :].bitcast(I32))
+        gather_scales(LAST, 0, HALF)
+        gather_first_scales(0)
         load_w2_planes()
         load_w1(0)
         nc.sync.dma_start(offsets[OWN][:], offs)
         load_w1(1)
+        gather_words(LAST, 0, 0, 2)
+        gather_words(FIRST, 0, 0, 2)
+        for pair in range(2):
+            gather_words(LAST, 1, pair)
+            gather_words(FIRST, 1, pair)
+        gather_first_scales(HALF)
         for t in range(PACK):
             nc.sync.dma_start(out=w4_raw[:, t, :], in_=w4.rearrange("(g t i) n -> t g i n", t=PACK, i=RUN)[t])
         nc.sync.dma_start(out=bias[:], in_=b.rearrange("(m e) -> m e", e=2))
 
-        gather_scales(LAST, 0, HALF)
-        gather_words(LAST, 0, 0)
-        gather_words(FIRST, 0, 0)
-        gather_words(LAST, 0, 1)
-        gather_words(LAST, 1, 0)
-        gather_words(FIRST, 1, 0)
-        gather_words(LAST, 1, 1)
-        gather_passes(FIRST, 1)
-
-        both_products(0)
+        cited_products(LAST, 0, [0])
+        cited_products(LAST, 1, [0])
+        for pair in range(2):
+            cited_products(LAST, pair, [1])
+            stage(LAST, pair)
+            cited_products(FIRST, pair)
+            stage(FIRST, pair)
         gather_scales(LAST, HALF, HALF)
-        gather_passes(LAST, 2)
+        gather_passes(LAST, 2, 2)
         gather_passes(FIRST, 2)
         round_w1_on_gpsimd(0)
-        both_products(1)
-        round_w1_on_scalar(1)
+        round_w1_on_gpsimd(1, [0])
+        round_w1_on_scalar(1, [1, 2, 3])
         absolute_differences(0)
 
         gather_scales(OWN, 0, HALF)
         gather_passes(OWN, 0)
-        gather_passes(LAST, 3)
         for a in range(PASSES):
             quantize_w1(a)
         round_w4()
@@ -335,16 +365,19 @@ def tile_list_citation_topic_scores_kernel(
         gather_passes(OWN, 2)
         gather_passes(OWN, 3)
 
-        both_products(2)
+        cited_products(LAST, 2)
+        stage(LAST, 2)
         absolute_differences(1)
+        cited_products(FIRST, 2)
+        stage(FIRST, 2)
         cited_products(LAST, 3)
         for u in tiles_of(0):
             own_product(u)
             add_on_gpsimd(u)
         stage(LAST, 3)
+        absolute_differences(2)
         cited_products(FIRST, 3)
         stage(FIRST, 3)
-        absolute_differences(2)
 
         for u in tiles_of(1) + tiles_of(2):
             own_product(u)

@@ -153,7 +153,7 @@ def tile_list_citation_topic_scores_kernel(
             nc.vector.quantize_mx(out=w1_codes[a][:].bitcast(FP8X4), scales=w1_scales[:, a, :], in_=w1_bf16[a][:])
 
         def round_w4():
-            w4_tiles["bf16"] = kept([P, PACK * N], BF16, "w4_bf16", tag="w1_bf16_%d" % (PASSES - 1))
+            w4_tiles["bf16"] = kept([P, PACK * N], BF16, "w4_bf16", tag="last_own")
             round_on_gpsimd(
                 w4_tiles["bf16"][:].rearrange("p (e m t) -> p e m t", e=2, t=PACK),
                 w4_raw[:].rearrange("p t (m e) -> p e m t", e=2),
@@ -235,7 +235,10 @@ def tile_list_citation_topic_scores_kernel(
                     )
 
         def copy_own(u):
-            own_staged[u] = scalar_tile([P, TILE, PACK], F32, "own")
+            if u == GPSIMD_TILES - 1:
+                own_staged[u] = kept([P, TILE, PACK], F32, "own", tag="last_own")
+            else:
+                own_staged[u] = scalar_tile([P, TILE, PACK], F32, "own")
             nc.scalar.activation(out=own_staged[u][:], in_=by_token(own_bank[u]), func=ACT.Copy)
 
         def sum_on_gpsimd(u):
@@ -350,15 +353,13 @@ def tile_list_citation_topic_scores_kernel(
         gather_passes(LAST, 2, 2)
         gather_passes(FIRST, 2)
         round_w1_on_gpsimd(0)
-        round_w1_on_gpsimd(1, [0])
-        round_w1_on_scalar(1, [1, 2, 3])
+        round_w1_on_scalar(1)
         absolute_differences(0)
 
         gather_scales(OWN, 0, HALF)
         gather_passes(OWN, 0)
         for a in range(PASSES):
             quantize_w1(a)
-        round_w4()
         gather_passes(FIRST, 3)
         gather_passes(OWN, 1)
         gather_scales(OWN, HALF, HALF)
@@ -374,6 +375,7 @@ def tile_list_citation_topic_scores_kernel(
         for u in tiles_of(0):
             own_product(u)
             add_on_gpsimd(u)
+        round_w4()
         stage(LAST, 3)
         absolute_differences(2)
         cited_products(FIRST, 3)
@@ -386,19 +388,17 @@ def tile_list_citation_topic_scores_kernel(
             add_on_vector(u)
         relu_on_scalar(1)
         absolute_differences(3)
-
-        own_product(TILES - 2)
-        for pair in range(PAIRS - 1):
-            u = HALF // TILE + pair
+        own_product(6)
+        for u in tiles_of(2):
             add_on_vector(u)
-            if pair == 0:
-                quantize_w4()
-            finish_pair(pair)
-            if pair == 0:
-                own_product(TILES - 1)
-            if u % 2 == 1:
-                relu_on_vector(u // 2 * PAIR, PAIR)
-        add_on_vector(TILES - 1)
+        quantize_w4()
+        finish_pair(0)
+        own_product(7)
+        relu_on_vector(2 * PAIR, PAIR)
+        finish_pair(1)
+        add_on_vector(6)
+        finish_pair(2)
+        add_on_vector(7)
 
         last_starts = [u * TILE for u in tiles_of(PAIRS - 1)]
         for start in last_starts:

@@ -317,38 +317,34 @@ def tile_list_citation_topic_scores_kernel(
         nc.vector.memset(first_scales_pass1[:], 0)
         make_identity(nc, identity[:])
 
-        nc.sync.dma_start(offsets[LAST][:], offs3)
-        load_words(w3_codes[0], w3_words[0])
-        load_both_planes(nc.sync, table_scales, tab_scales)
         nc.sync.dma_start(offsets[FIRST][:], offs2)
+        load_both_planes(nc.sync, table_scales, tab_scales)
+        nc.sync.dma_start(offsets[LAST][:], offs3)
         load_words(table_words[0], tab_words[0])
+        load_words(w3_codes[0], w3_words[0])
         load_both_planes(nc.sync, weight_scales[:, PASSES, :], w3_scales)
         load_words(table_words[1], tab_words[1])
         load_words(w3_codes[1], w3_words[1])
         nc.sync.dma_start(out=w2_codes[:], in_=w2_words.rearrange("a p e -> p a e").bitcast(I32))
-        gather_scales(LAST, 0, HALF)
-        gather_first_scales(0)
+        first_scales = gather_scales(FIRST, 0, S)
+        nc.sync.dma_start(out=first_scales_pass1[0:112, :], in_=first_scales[4:116, :].bitcast(I32))
         load_w2_planes()
         load_w1(0)
         nc.sync.dma_start(offsets[OWN][:], offs)
         load_w1(1)
-        gather_words(LAST, 0, 0, 2)
-        gather_words(FIRST, 0, 0, 2)
-        for pair in range(2):
-            gather_words(LAST, 1, pair)
-            gather_words(FIRST, 1, pair)
-        gather_first_scales(HALF)
         for t in range(PACK):
             nc.sync.dma_start(out=w4_raw[:, t, :], in_=w4.rearrange("(g t i) n -> t g i n", t=PACK, i=RUN)[t])
         nc.sync.dma_start(out=bias[:], in_=b.rearrange("(m e) -> m e", e=2))
 
-        cited_products(LAST, 0, [0])
-        cited_products(LAST, 1, [0])
-        for pair in range(2):
-            cited_products(LAST, pair, [1])
-            stage(LAST, pair)
-            cited_products(FIRST, pair)
-            stage(FIRST, pair)
+        gather_scales(LAST, 0, HALF)
+        gather_words(LAST, 0, 0, 2)
+        gather_words(FIRST, 0, 0)
+        gather_words(LAST, 1, 0)
+        gather_words(FIRST, 1, 0)
+        gather_words(LAST, 1, 1)
+        gather_passes(FIRST, 1)
+        both_products(0)
+        both_products(1)
         gather_scales(LAST, HALF, HALF)
         gather_passes(LAST, 2, 2)
         gather_passes(FIRST, 2)

@@ -29,10 +29,11 @@ PAIRS = S // PAIR
 HALF = S // 2
 OWN, FIRST, LAST = "own", "first", "last"
 
-GPSIMD_TILES = 2
+MOVED_ROWS = 32 * (QUADS - 1) + 4
+
 BANKS = 8
-VECTOR_TILES = 43
-SCALAR_TILES = 35
+VECTOR_TILES = 40
+SCALAR_TILES = 32
 
 
 def tile_list_citation_topic_scores_kernel(
@@ -77,9 +78,6 @@ def tile_list_citation_topic_scores_kernel(
         staged = {}
         distance = {}
         cited_bank = {}
-        diff_bank = {}
-        own_staged = {}
-        score_bank = {}
         own_bank = {}
         h_sum = {}
         h_bf16, h_codes = {}, {}
@@ -93,9 +91,9 @@ def tile_list_citation_topic_scores_kernel(
         def load_words(tile, words):
             nc.sync.dma_start(out=tile[:], in_=words.rearrange("p n i -> p (n i)").bitcast(I32))
 
-        def load_both_planes(queue, tile, scales):
+        def load_both_planes(tile, scales):
             for q in range(QUADS):
-                queue.dma_start(out=tile[32 * q : 32 * q + 8, :], in_=scales.bitcast(I32)[:, 4 * q : 4 * q + 4, :])
+                nc.sync.dma_start(out=tile[32 * q : 32 * q + 8, :], in_=scales.bitcast(I32)[:, 4 * q : 4 * q + 4, :])
 
         def load_w2_planes():
             for q in range(QUADS):
@@ -127,25 +125,20 @@ def tile_list_citation_topic_scores_kernel(
             for a in range(PASSES):
                 gather_words(name, a, pair, pairs)
 
-        def gather_first_scales(start):
-            plane = gather_scales(FIRST, start, HALF)
-            moved = first_scales_pass1[0:112, start // 4 : (start + HALF) // 4]
-            nc.sync.dma_start(out=moved, in_=plane[4:116, :].bitcast(I32))
-
 
         def round_on_gpsimd(dst, src):
             nc.gpsimd.tensor_scalar(out=dst, in0=src, scalar1=1.0, scalar2=0.0, op0=ALU.mult, op1=ALU.add)
 
-        def round_w1_on_gpsimd(a, pieces=range(PACK)):
+        def round_w1_on_gpsimd(a):
             src = w1_raw[a][:].rearrange("p j (g t i) -> p t g i j", t=PACK, i=RUN)
             dst = w1_bf16[a][:].rearrange("p (t g i j) -> p t g i j", t=PACK, i=RUN, j=PACK)
-            for t in pieces:
+            for t in range(PACK):
                 round_on_gpsimd(dst[:, t], src[:, t])
 
-        def round_w1_on_scalar(a, pieces=range(PACK)):
+        def round_w1_on_scalar(a):
             src = w1_raw[a][:].rearrange("p j (g t u i) -> p t g u j i", t=PACK, u=2, i=4)
             dst = w1_bf16[a][:].rearrange("p (t g u i j) -> p t g u j i", t=PACK, u=2, i=4, j=PACK)
-            for t in pieces:
+            for t in range(PACK):
                 nc.scalar.copy(out=dst[:, t], in_=src[:, t])
 
         def quantize_w1(a):
@@ -153,7 +146,7 @@ def tile_list_citation_topic_scores_kernel(
             nc.vector.quantize_mx(out=w1_codes[a][:].bitcast(FP8X4), scales=w1_scales[:, a, :], in_=w1_bf16[a][:])
 
         def round_w4():
-            w4_tiles["bf16"] = kept([P, PACK * N], BF16, "w4_bf16", tag="last_own")
+            w4_tiles["bf16"] = kept([P, PACK * N], BF16, "w4_bf16", tag="own_then_w4")
             round_on_gpsimd(
                 w4_tiles["bf16"][:].rearrange("p (e m t) -> p e m t", e=2, t=PACK),
                 w4_raw[:].rearrange("p t (m e) -> p e m t", e=2),
@@ -172,13 +165,11 @@ def tile_list_citation_topic_scores_kernel(
         def by_two_tokens(bank):
             return bank[:].rearrange("p t (m i) -> p m t i", i=2)
 
-        def cited_products(name, pair, passes=range(PASSES)):
+        def cited_products(name, pair):
             planes = weight_scales[:].bitcast(U8)
             for u in tiles_of(pair):
-                if (name, u) not in cited_bank:
-                    cited_bank[name, u] = next_bank([P, H], "cited_bank")
-                bank = cited_bank[name, u]
-                for a in passes:
+                bank = cited_bank[name, u] = next_bank([P, H], "cited_bank")
+                for a in range(PASSES):
                     if name == LAST:
                         weight, weight_plane = w3_codes[a][:].bitcast(FP8X4), planes[4 * a :, PASSES, :]
                         token_plane = picked_scales[LAST, u][4 * a :, :]
@@ -204,24 +195,18 @@ def tile_list_citation_topic_scores_kernel(
                 cited_products(name, pair)
                 stage(name, pair)
 
-        def transposes(u):
-            diff_bank[u] = next_bank([P, PACK, TILE], "diff_bank")
-            for t in range(PACK):
-                for name in (FIRST, LAST):
-                    nc.tensor.matmul(
-                        out=diff_bank[u][:, t, :], lhsT=staged[name, u][:, t].rearrange("p g i -> p (g i)"),
-                        rhs=identity[:], start=(name == FIRST), stop=(name == LAST), is_transpose=True,
-                    )
-
-        def absolute(u):
-            walk = by_two_tokens(diff_bank[u]) if u >= GPSIMD_TILES else by_token(diff_bank[u])
-            distance[u] = scalar_tile(list(walk.shape), F32, "distance")
-            nc.scalar.activation(out=distance[u][:], in_=walk, func=ACT.Abs)
-
         def absolute_differences(pair):
             for u in tiles_of(pair):
-                transposes(u)
-                absolute(u)
+                bank = next_bank([P, PACK, TILE], "diff_bank")
+                for t in range(PACK):
+                    for name in (FIRST, LAST):
+                        nc.tensor.matmul(
+                            out=bank[:, t, :], lhsT=staged[name, u][:, t].rearrange("p g i -> p (g i)"),
+                            rhs=identity[:], start=(name == FIRST), stop=(name == LAST), is_transpose=True,
+                        )
+                walk = by_two_tokens(bank) if pair else by_token(bank)
+                distance[u] = scalar_tile(list(walk.shape), F32, "distance")
+                nc.scalar.activation(out=distance[u][:], in_=walk, func=ACT.Abs)
 
         def own_product(u):
             own_bank[u] = next_bank([P, PACK, TILE], "own_bank")
@@ -234,21 +219,15 @@ def tile_list_citation_topic_scores_kernel(
                         rhs_scale=picked_scales[OWN, u][4 * a :, :], start=(a == 0), stop=(a == PASSES - 1),
                     )
 
-        def copy_own(u):
-            if u == GPSIMD_TILES - 1:
-                own_staged[u] = kept([P, TILE, PACK], F32, "own", tag="last_own")
-            else:
-                own_staged[u] = scalar_tile([P, TILE, PACK], F32, "own")
-            nc.scalar.activation(out=own_staged[u][:], in_=by_token(own_bank[u]), func=ACT.Copy)
-
-        def sum_on_gpsimd(u):
-            if u % 2 == 0:
-                h_sum[u // 2] = kept([P, 2, TILE, PACK], BF16, "h_sum_early%d" % (u // 2))
-            nc.gpsimd.tensor_tensor(out=h_sum[u // 2][:, u % 2], in0=own_staged[u][:], in1=distance[u][:], op=ALU.add)
-
         def add_on_gpsimd(u):
-            copy_own(u)
-            sum_on_gpsimd(u)
+            if u % 2 == 0:
+                own = scalar_tile([P, TILE, PACK], F32, "own")
+            else:
+                own = kept([P, TILE, PACK], F32, "own_second", tag="own_then_w4")
+            nc.scalar.activation(out=own[:], in_=by_token(own_bank[u]), func=ACT.Copy)
+            if u % 2 == 0:
+                h_sum[u // 2] = kept([P, 2, TILE, PACK], BF16, "h_sum_first")
+            nc.gpsimd.tensor_tensor(out=h_sum[u // 2][:, u % 2], in0=own[:], in1=distance[u][:], op=ALU.add)
 
         def add_on_vector(u):
             if u % 2 == 0:
@@ -295,21 +274,15 @@ def tile_list_citation_topic_scores_kernel(
         def store(start, count, result):
             nc.sync.dma_start(out=out.rearrange("(m e) s -> m e s", e=2)[:, :, start : start + count], in_=result[:])
 
-        def scores(pair):
+        def finish_pair(pair):
             quantize_h(pair * PAIR, PAIR)
-            score_bank[pair] = next_bank([P, 2, PAIR], "score_bank")
+            bank = next_bank([P, 2, PAIR], "score_bank")
             for e in range(2):
-                score_product(score_bank[pair][:, e, :], e, pair * PAIR, PAIR)
-
-        def bias_and_store(pair):
+                score_product(bank[:, e, :], e, pair * PAIR, PAIR)
             result = scalar_tile([P, 2, PAIR], F32, "result")
             for e in range(2):
-                add_bias_on_scalar(result[:, e, :], score_bank[pair][:, e, :], e)
+                add_bias_on_scalar(result[:, e, :], bank[:, e, :], e)
             store(pair * PAIR, PAIR, result)
-
-        def finish_pair(pair):
-            scores(pair)
-            bias_and_store(pair)
 
 
         nc.gpsimd.memset(table_scales[:], 0)
@@ -318,16 +291,16 @@ def tile_list_citation_topic_scores_kernel(
         make_identity(nc, identity[:])
 
         nc.sync.dma_start(offsets[FIRST][:], offs2)
-        load_both_planes(nc.sync, table_scales, tab_scales)
+        load_both_planes(table_scales, tab_scales)
         nc.sync.dma_start(offsets[LAST][:], offs3)
         load_words(table_words[0], tab_words[0])
         load_words(w3_codes[0], w3_words[0])
-        load_both_planes(nc.sync, weight_scales[:, PASSES, :], w3_scales)
+        load_both_planes(weight_scales[:, PASSES, :], w3_scales)
         load_words(table_words[1], tab_words[1])
         load_words(w3_codes[1], w3_words[1])
         nc.sync.dma_start(out=w2_codes[:], in_=w2_words.rearrange("a p e -> p a e").bitcast(I32))
         first_scales = gather_scales(FIRST, 0, S)
-        nc.sync.dma_start(out=first_scales_pass1[0:112, :], in_=first_scales[4:116, :].bitcast(I32))
+        nc.sync.dma_start(out=first_scales_pass1[0:MOVED_ROWS, :], in_=first_scales[4 : 4 + MOVED_ROWS, :].bitcast(I32))
         load_w2_planes()
         load_w1(0)
         nc.sync.dma_start(offsets[OWN][:], offs)
@@ -337,7 +310,7 @@ def tile_list_citation_topic_scores_kernel(
         nc.sync.dma_start(out=bias[:], in_=b.rearrange("(m e) -> m e", e=2))
 
         gather_scales(LAST, 0, HALF)
-        gather_words(LAST, 0, 0, 2)
+        gather_words(LAST, 0, 0, pairs=2)
         gather_words(FIRST, 0, 0)
         gather_words(LAST, 1, 0)
         gather_words(FIRST, 1, 0)
@@ -345,8 +318,9 @@ def tile_list_citation_topic_scores_kernel(
         gather_passes(FIRST, 1)
         both_products(0)
         both_products(1)
+
         gather_scales(LAST, HALF, HALF)
-        gather_passes(LAST, 2, 2)
+        gather_passes(LAST, 2, pairs=2)
         gather_passes(FIRST, 2)
         round_w1_on_gpsimd(0)
         round_w1_on_scalar(1)
@@ -377,6 +351,7 @@ def tile_list_citation_topic_scores_kernel(
         cited_products(FIRST, 3)
         stage(FIRST, 3)
 
+        second_last, last = tiles_of(PAIRS - 1)
         for u in tiles_of(1) + tiles_of(2):
             own_product(u)
         relu_on_scalar(0)
@@ -384,17 +359,18 @@ def tile_list_citation_topic_scores_kernel(
             add_on_vector(u)
         relu_on_scalar(1)
         absolute_differences(3)
-        own_product(6)
+        own_product(second_last)
         for u in tiles_of(2):
             add_on_vector(u)
         quantize_w4()
+
         finish_pair(0)
-        own_product(7)
+        own_product(last)
         relu_on_vector(2 * PAIR, PAIR)
         finish_pair(1)
-        add_on_vector(6)
+        add_on_vector(second_last)
         finish_pair(2)
-        add_on_vector(7)
+        add_on_vector(last)
 
         last_starts = [u * TILE for u in tiles_of(PAIRS - 1)]
         for start in last_starts:

@@ -29,11 +29,12 @@ PAIRS = S // PAIR
 HALF = S // 2
 OWN, FIRST, LAST = "own", "first", "last"
 
+ROWS_AT = P - 32
 MOVED_ROWS = 32 * (QUADS - 1) + 4
 
 BANKS = 8
-VECTOR_TILES = 40
-SCALAR_TILES = 32
+VECTOR_TILES = 46
+SCALAR_TILES = 33
 
 
 def tile_list_citation_topic_scores_kernel(
@@ -61,7 +62,8 @@ def tile_list_citation_topic_scores_kernel(
         offsets = {name: lists.tile([P, S // 16], U16, name="offsets_" + name) for name in (OWN, FIRST, LAST)}
         table_words = [kept([P, T], I32, "table_words%d" % a) for a in range(PASSES)]
         table_scales = kept([P, T // 4], I32, "table_scales")
-        weight_scales = kept([P, 3, H // 4], I32, "weight_scales")
+        w2_planes = kept([P, PASSES, H // 4], I32, "w2_planes")
+        w3_planes = kept([P, PASSES, H // 4], I32, "w3_planes")
         w2_codes = kept([P, PASSES, H // 2], I32, "w2_codes")
         w3_codes = [kept([P, H], I32, "w3_codes%d" % a) for a in range(PASSES)]
         w1_raw = [kept([P, PACK, H], F32, "w1_raw%d" % a) for a in range(PASSES)]
@@ -71,7 +73,8 @@ def tile_list_citation_topic_scores_kernel(
         w4_scales = kept([P, N], U8, "w4_scales")
         h_scales = kept([P, S], U8, "h_scales")
         first_scales_pass1 = kept([P, S // 4], I32, "first_scales_pass1")
-        identity = kept([P, P], F32, "identity")
+        scale_rows = kept([P, T // 4], I32, "scale_rows")
+        own_plane = kept([P, S // 4], I32, "own_plane")
         bias = kept([P, 2], F32, "bias")
         picked_words = {}
         picked_scales = {}
@@ -91,14 +94,14 @@ def tile_list_citation_topic_scores_kernel(
         def load_words(tile, words):
             nc.sync.dma_start(out=tile[:], in_=words.rearrange("p n i -> p (n i)").bitcast(I32))
 
-        def load_both_planes(tile, scales):
-            for q in range(QUADS):
-                nc.sync.dma_start(out=tile[32 * q : 32 * q + 8, :], in_=scales.bitcast(I32)[:, 4 * q : 4 * q + 4, :])
+        def load_table_planes(queue, q):
+            rows = tab_scales.bitcast(I32)[:, 4 * q : 4 * q + 4, :]
+            queue.dma_start(out=table_scales[32 * q : 32 * q + 8, :], in_=rows)
 
-        def load_w2_planes():
+        def load_weight_planes(planes, scales):
             for q in range(QUADS):
-                rows = w2_scales.bitcast(I32)[:, 4 * q : 4 * q + 4, :].rearrange("a r e -> r a e")
-                nc.sync.dma_start(out=weight_scales[32 * q : 32 * q + 4, 0:PASSES, :], in_=rows)
+                rows = scales.bitcast(I32)[:, 4 * q : 4 * q + 4, :].rearrange("a r e -> r a e")
+                nc.sync.dma_start(out=planes[32 * q : 32 * q + 4, :, :], in_=rows)
 
         def load_w1(a):
             rows = w1[P * PACK * a : P * PACK * (a + 1), :]
@@ -112,6 +115,28 @@ def tile_list_citation_topic_scores_kernel(
             for k in range(count // TILE):
                 picked_scales[name, start // TILE + k] = plane[:, k * TILE : (k + 1) * TILE]
             return plane
+
+        def gather_own_rows():
+            rows = vector_tile([P, S], U8, "own_rows")
+            nc.vector.tensor_copy(rows[:], scale_rows[:].bitcast(U8).indirect(offsets[OWN][:]))
+            return rows
+
+        def move_own_rows(rows):
+            for a in range(PASSES):
+                for q in range(QUADS):
+                    first = ROWS_AT + 16 * a + 4 * q
+                    nc.sync.dma_start(
+                        out=own_plane[32 * q + 4 * a : 32 * q + 4 * a + 4, :], in_=rows[first : first + 4, :].bitcast(I32)
+                    )
+            for u in range(TILES):
+                picked_scales[OWN, u] = own_plane[:].bitcast(U8)[:, u * TILE : (u + 1) * TILE]
+
+        def gather_first_scales(queue, start):
+            plane = gather_scales(FIRST, start, HALF)
+            queue.dma_start(
+                out=first_scales_pass1[0:MOVED_ROWS, start // 4 : (start + HALF) // 4],
+                in_=plane[4 : 4 + MOVED_ROWS, :].bitcast(I32),
+            )
 
         def gather_words(name, a, pair, pairs=1):
             words = vector_tile([P, pairs * PAIR], U32, "words_%s%d" % (name, a))
@@ -129,16 +154,16 @@ def tile_list_citation_topic_scores_kernel(
         def round_on_gpsimd(dst, src):
             nc.gpsimd.tensor_scalar(out=dst, in0=src, scalar1=1.0, scalar2=0.0, op0=ALU.mult, op1=ALU.add)
 
-        def round_w1_on_gpsimd(a):
+        def round_w1_on_gpsimd(a, places):
             src = w1_raw[a][:].rearrange("p j (g t i) -> p t g i j", t=PACK, i=RUN)
             dst = w1_bf16[a][:].rearrange("p (t g i j) -> p t g i j", t=PACK, i=RUN, j=PACK)
-            for t in range(PACK):
+            for t in places:
                 round_on_gpsimd(dst[:, t], src[:, t])
 
-        def round_w1_on_scalar(a):
+        def round_w1_on_scalar(a, places):
             src = w1_raw[a][:].rearrange("p j (g t u i) -> p t g u j i", t=PACK, u=2, i=4)
             dst = w1_bf16[a][:].rearrange("p (t g u i j) -> p t g u j i", t=PACK, u=2, i=4, j=PACK)
-            for t in range(PACK):
+            for t in places:
                 nc.scalar.copy(out=dst[:, t], in_=src[:, t])
 
         def quantize_w1(a):
@@ -146,7 +171,7 @@ def tile_list_citation_topic_scores_kernel(
             nc.vector.quantize_mx(out=w1_codes[a][:].bitcast(FP8X4), scales=w1_scales[:, a, :], in_=w1_bf16[a][:])
 
         def round_w4():
-            w4_tiles["bf16"] = kept([P, PACK * N], BF16, "w4_bf16", tag="own_then_w4")
+            w4_tiles["bf16"] = kept([P, PACK * N], BF16, "w4_bf16", tag="w1_bf16_1")
             round_on_gpsimd(
                 w4_tiles["bf16"][:].rearrange("p (e m t) -> p e m t", e=2, t=PACK),
                 w4_raw[:].rearrange("p t (m e) -> p e m t", e=2),
@@ -165,22 +190,25 @@ def tile_list_citation_topic_scores_kernel(
         def by_two_tokens(bank):
             return bank[:].rearrange("p t (m i) -> p m t i", i=2)
 
+        def cited_pass(name, u, a):
+            if a == 0:
+                cited_bank[name, u] = next_bank([P, H], "cited_bank")
+            if name == LAST:
+                weight, weight_plane = w3_codes[a][:].bitcast(FP8X4), w3_planes[:].bitcast(U8)[:, a, :]
+                token_plane = picked_scales[LAST, u][4 * a :, :]
+            else:
+                weight, weight_plane = w2_codes[:, a, :].bitcast(U8).bitcast(FP4X4), w2_planes[:].bitcast(U8)[:, a, :]
+                moved_plane = first_scales_pass1[:].bitcast(U8)[:, u * TILE : (u + 1) * TILE]
+                token_plane = moved_plane if a else picked_scales[FIRST, u]
+            nc.tensor.matmul_mx(
+                out=cited_bank[name, u][:], lhsT=picked_words[name, a, u].bitcast(FP8X4), lhsT_scale=token_plane,
+                rhs=weight, rhs_scale=weight_plane, start=(a == 0), stop=(a == PASSES - 1),
+            )
+
         def cited_products(name, pair):
-            planes = weight_scales[:].bitcast(U8)
             for u in tiles_of(pair):
-                bank = cited_bank[name, u] = next_bank([P, H], "cited_bank")
                 for a in range(PASSES):
-                    if name == LAST:
-                        weight, weight_plane = w3_codes[a][:].bitcast(FP8X4), planes[4 * a :, PASSES, :]
-                        token_plane = picked_scales[LAST, u][4 * a :, :]
-                    else:
-                        weight, weight_plane = w2_codes[:, a, :].bitcast(U8).bitcast(FP4X4), planes[:, a, :]
-                        moved_plane = first_scales_pass1[:].bitcast(U8)[:, u * TILE : (u + 1) * TILE]
-                        token_plane = moved_plane if a else picked_scales[FIRST, u]
-                    nc.tensor.matmul_mx(
-                        out=bank[:], lhsT=picked_words[name, a, u].bitcast(FP8X4), lhsT_scale=token_plane,
-                        rhs=weight, rhs_scale=weight_plane, start=(a == 0), stop=(a == PASSES - 1),
-                    )
+                    cited_pass(name, u, a)
 
         def stage(name, pair):
             for u in tiles_of(pair):
@@ -190,13 +218,8 @@ def tile_list_citation_topic_scores_kernel(
                     out=staged[name, u][:], in_=sums, func=ACT.Copy, scale=-1.0 if name == LAST else 1.0
                 )
 
-        def both_products(pair):
-            for name in (LAST, FIRST):
-                cited_products(name, pair)
-                stage(name, pair)
-
-        def absolute_differences(pair):
-            for u in tiles_of(pair):
+        def absolute_differences(*tiles):
+            for u in tiles:
                 bank = next_bank([P, PACK, TILE], "diff_bank")
                 for t in range(PACK):
                     for name in (FIRST, LAST):
@@ -204,7 +227,7 @@ def tile_list_citation_topic_scores_kernel(
                             out=bank[:, t, :], lhsT=staged[name, u][:, t].rearrange("p g i -> p (g i)"),
                             rhs=identity[:], start=(name == FIRST), stop=(name == LAST), is_transpose=True,
                         )
-                walk = by_two_tokens(bank) if pair else by_token(bank)
+                walk = by_two_tokens(bank) if u >= 2 else by_token(bank)
                 distance[u] = scalar_tile(list(walk.shape), F32, "distance")
                 nc.scalar.activation(out=distance[u][:], in_=walk, func=ACT.Abs)
 
@@ -220,10 +243,7 @@ def tile_list_citation_topic_scores_kernel(
                     )
 
         def add_on_gpsimd(u):
-            if u % 2 == 0:
-                own = scalar_tile([P, TILE, PACK], F32, "own")
-            else:
-                own = kept([P, TILE, PACK], F32, "own_second", tag="own_then_w4")
+            own = scalar_tile([P, TILE, PACK], F32, "own")
             nc.scalar.activation(out=own[:], in_=by_token(own_bank[u]), func=ACT.Copy)
             if u % 2 == 0:
                 h_sum[u // 2] = kept([P, 2, TILE, PACK], BF16, "h_sum_first")
@@ -286,82 +306,95 @@ def tile_list_citation_topic_scores_kernel(
 
 
         nc.gpsimd.memset(table_scales[:], 0)
-        nc.vector.memset(weight_scales[:], 0)
+        nc.vector.memset(w3_planes[:], 0)
+        nc.vector.memset(scale_rows[0:ROWS_AT, :], 0)
+        nc.vector.memset(w2_planes[:], 0)
+        for q in range(QUADS - 1):
+            load_table_planes(nc.gpsimd, q)
         nc.vector.memset(first_scales_pass1[:], 0)
-        make_identity(nc, identity[:])
+        nc.vector.memset(own_plane[:], 0)
 
-        nc.sync.dma_start(offsets[FIRST][:], offs2)
-        load_both_planes(table_scales, tab_scales)
+        nc.sync.dma_start(offsets[OWN][:], offs)
+        nc.sync.dma_start(out=scale_rows[ROWS_AT:P, :], in_=tab_scales.rearrange("a q t -> (a q) t").bitcast(I32))
         nc.sync.dma_start(offsets[LAST][:], offs3)
+        nc.sync.dma_start(offsets[FIRST][:], offs2)
         load_words(table_words[0], tab_words[0])
+        load_table_planes(nc.sync, QUADS - 1)
+        load_weight_planes(w3_planes, w3_scales)
         load_words(w3_codes[0], w3_words[0])
-        load_both_planes(weight_scales[:, PASSES, :], w3_scales)
         load_words(table_words[1], tab_words[1])
         load_words(w3_codes[1], w3_words[1])
         nc.sync.dma_start(out=w2_codes[:], in_=w2_words.rearrange("a p e -> p a e").bitcast(I32))
-        first_scales = gather_scales(FIRST, 0, S)
-        nc.sync.dma_start(out=first_scales_pass1[0:MOVED_ROWS, :], in_=first_scales[4 : 4 + MOVED_ROWS, :].bitcast(I32))
-        load_w2_planes()
+        load_weight_planes(w2_planes, w2_scales)
+
+        own_rows = gather_own_rows()
+        identity = kept([P, P], F32, "identity", tag="scale_rows")
+        make_identity(nc, identity[:])
+        gather_words(LAST, 0, 0, pairs=2)
+        gather_scales(LAST, 0, HALF)
+        gather_first_scales(nc.gpsimd, 0)
         load_w1(0)
-        nc.sync.dma_start(offsets[OWN][:], offs)
         load_w1(1)
+        gather_words(LAST, 1, 0)
+        gather_words(LAST, 1, 1)
+        gather_words(FIRST, 0, 0, pairs=2)
+        gather_words(FIRST, 1, 0)
+        gather_words(FIRST, 1, 1)
+        for name in (LAST, FIRST):
+            for a in range(PASSES):
+                for u in tiles_of(0) + tiles_of(1):
+                    cited_pass(name, u, a)
+            stage(name, 0)
+            stage(name, 1)
+
+        gather_scales(LAST, HALF, HALF)
+        gather_passes(LAST, 2)
+        move_own_rows(own_rows)
+        gather_first_scales(nc.sync, HALF)
         for t in range(PACK):
             nc.sync.dma_start(out=w4_raw[:, t, :], in_=w4.rearrange("(g t i) n -> t g i n", t=PACK, i=RUN)[t])
         nc.sync.dma_start(out=bias[:], in_=b.rearrange("(m e) -> m e", e=2))
-
-        gather_scales(LAST, 0, HALF)
-        gather_words(LAST, 0, 0, pairs=2)
-        gather_words(FIRST, 0, 0)
-        gather_words(LAST, 1, 0)
-        gather_words(FIRST, 1, 0)
-        gather_words(LAST, 1, 1)
-        gather_passes(FIRST, 1)
-        both_products(0)
-        both_products(1)
-
-        gather_scales(LAST, HALF, HALF)
-        gather_passes(LAST, 2, pairs=2)
+        gather_passes(LAST, 3)
         gather_passes(FIRST, 2)
-        round_w1_on_gpsimd(0)
-        round_w1_on_scalar(1)
-        absolute_differences(0)
-
-        gather_scales(OWN, 0, HALF)
         gather_passes(OWN, 0)
+        absolute_differences(0)
+        round_w1_on_gpsimd(0, range(PACK))
+        round_w1_on_gpsimd(1, range(1))
+        round_w1_on_scalar(1, range(1, PACK))
         for a in range(PASSES):
             quantize_w1(a)
+        round_w4()
         gather_passes(FIRST, 3)
         gather_passes(OWN, 1)
-        gather_scales(OWN, HALF, HALF)
         gather_passes(OWN, 2)
         gather_passes(OWN, 3)
 
         cited_products(LAST, 2)
         stage(LAST, 2)
-        absolute_differences(1)
-        cited_products(FIRST, 2)
-        stage(FIRST, 2)
+        absolute_differences(1, 2)
         cited_products(LAST, 3)
+        absolute_differences(3)
+        cited_products(FIRST, 2)
+        stage(LAST, 3)
+        stage(FIRST, 2)
         for u in tiles_of(0):
             own_product(u)
             add_on_gpsimd(u)
-        round_w4()
-        stage(LAST, 3)
-        absolute_differences(2)
         cited_products(FIRST, 3)
+        absolute_differences(*tiles_of(2))
         stage(FIRST, 3)
 
         second_last, last = tiles_of(PAIRS - 1)
         for u in tiles_of(1) + tiles_of(2):
             own_product(u)
-        relu_on_scalar(0)
         for u in tiles_of(1):
             add_on_vector(u)
-        relu_on_scalar(1)
-        absolute_differences(3)
+        relu_on_scalar(0)
+        absolute_differences(*tiles_of(3))
         own_product(second_last)
-        for u in tiles_of(2):
-            add_on_vector(u)
+        add_on_vector(tiles_of(2)[0])
+        relu_on_vector(PAIR, PAIR)
+        add_on_vector(tiles_of(2)[1])
         quantize_w4()
 
         finish_pair(0)

@@ -98,8 +98,8 @@ def tile_list_citation_topic_scores_kernel(
             rows = tab_scales.bitcast(I32)[:, 4 * q : 4 * q + 4, :]
             queue.dma_start(out=table_scales[32 * q : 32 * q + 8, :], in_=rows)
 
-        def load_weight_planes(planes, scales):
-            for q in range(QUADS):
+        def load_weight_planes(planes, scales, quadrants):
+            for q in quadrants:
                 rows = scales.bitcast(I32)[:, 4 * q : 4 * q + 4, :].rearrange("a r e -> r a e")
                 nc.sync.dma_start(out=planes[32 * q : 32 * q + 4, :, :], in_=rows)
 
@@ -309,35 +309,35 @@ def tile_list_citation_topic_scores_kernel(
         nc.vector.memset(w3_planes[:], 0)
         nc.vector.memset(scale_rows[0:ROWS_AT, :], 0)
         nc.vector.memset(w2_planes[:], 0)
-        for q in range(QUADS - 1):
-            load_table_planes(nc.gpsimd, q)
         nc.vector.memset(first_scales_pass1[:], 0)
         nc.vector.memset(own_plane[:], 0)
 
         nc.sync.dma_start(offsets[OWN][:], offs)
         nc.sync.dma_start(out=scale_rows[ROWS_AT:P, :], in_=tab_scales.rearrange("a q t -> (a q) t").bitcast(I32))
-        nc.sync.dma_start(offsets[LAST][:], offs3)
         nc.sync.dma_start(offsets[FIRST][:], offs2)
+        for q in range(QUADS):
+            load_table_planes(nc.sync, q)
+        nc.sync.dma_start(offsets[LAST][:], offs3)
         load_words(table_words[0], tab_words[0])
-        load_table_planes(nc.sync, QUADS - 1)
-        load_weight_planes(w3_planes, w3_scales)
         load_words(w3_codes[0], w3_words[0])
+        load_weight_planes(w3_planes, w3_scales, range(QUADS))
+        load_weight_planes(w2_planes, w2_scales, range(1))
         load_words(table_words[1], tab_words[1])
         load_words(w3_codes[1], w3_words[1])
         nc.sync.dma_start(out=w2_codes[:], in_=w2_words.rearrange("a p e -> p a e").bitcast(I32))
-        load_weight_planes(w2_planes, w2_scales)
+        load_weight_planes(w2_planes, w2_scales, range(1, QUADS))
 
         own_rows = gather_own_rows()
         identity = kept([P, P], F32, "identity", tag="scale_rows")
         make_identity(nc, identity[:])
-        gather_words(LAST, 0, 0, pairs=2)
+        gather_first_scales(nc.sync, 0)
         gather_scales(LAST, 0, HALF)
-        gather_first_scales(nc.gpsimd, 0)
+        gather_words(LAST, 0, 0, pairs=2)
         load_w1(0)
         load_w1(1)
+        gather_words(FIRST, 0, 0, pairs=2)
         gather_words(LAST, 1, 0)
         gather_words(LAST, 1, 1)
-        gather_words(FIRST, 0, 0, pairs=2)
         gather_words(FIRST, 1, 0)
         gather_words(FIRST, 1, 1)
         for name in (LAST, FIRST):

@@ -33,8 +33,8 @@ ROWS_AT = P - 32
 MOVED_ROWS = 32 * (QUADS - 1) + 4
 
 BANKS = 8
-VECTOR_TILES = 46
-SCALAR_TILES = 33
+VECTOR_TILES = 50
+SCALAR_TILES = 35
 
 
 def tile_list_citation_topic_scores_kernel(
@@ -67,7 +67,7 @@ def tile_list_citation_topic_scores_kernel(
         w2_codes = kept([P, PASSES, H // 2], I32, "w2_codes")
         w3_codes = [kept([P, H], I32, "w3_codes%d" % a) for a in range(PASSES)]
         w1_raw = [kept([P, PACK, H], F32, "w1_raw%d" % a) for a in range(PASSES)]
-        w1_bf16 = [kept([P, PACK * H], BF16, "w1_bf16_%d" % a) for a in range(PASSES)]
+        w1_bf16 = {}
         w1_scales = kept([P, PASSES, H], U8, "w1_scales")
         w4_raw = kept([P, PACK, N], F32, "w4_raw")
         w4_scales = kept([P, N], U8, "w4_scales")
@@ -154,24 +154,33 @@ def tile_list_citation_topic_scores_kernel(
         def round_on_gpsimd(dst, src):
             nc.gpsimd.tensor_scalar(out=dst, in0=src, scalar1=1.0, scalar2=0.0, op0=ALU.mult, op1=ALU.add)
 
-        def round_w1_on_gpsimd(a, places):
+        def round_w1_on_gpsimd(a, first, count):
+            w1_bf16[a, first] = kept([P, count, PACK * P], BF16, "w1_bf16_%d_%d" % (a, first))
             src = w1_raw[a][:].rearrange("p j (g t i) -> p t g i j", t=PACK, i=RUN)
-            dst = w1_bf16[a][:].rearrange("p (t g i j) -> p t g i j", t=PACK, i=RUN, j=PACK)
-            for t in places:
-                round_on_gpsimd(dst[:, t], src[:, t])
+            dst = w1_bf16[a, first][:].rearrange("p t (g i j) -> p t g i j", i=RUN, j=PACK)
+            for k in range(count):
+                round_on_gpsimd(dst[:, k], src[:, first + k])
 
-        def round_w1_on_scalar(a, places):
+        def round_w1_on_scalar(a, first, count):
+            w1_bf16[a, first] = scalar_tile([P, count, PACK * P], BF16, "w1_bf16")
             src = w1_raw[a][:].rearrange("p j (g t u i) -> p t g u j i", t=PACK, u=2, i=4)
-            dst = w1_bf16[a][:].rearrange("p (t g u i j) -> p t g u j i", t=PACK, u=2, i=4, j=PACK)
-            for t in places:
-                nc.scalar.copy(out=dst[:, t], in_=src[:, t])
+            dst = w1_bf16[a, first][:].rearrange("p t (g u i j) -> p t g u j i", u=2, i=4, j=PACK)
+            for k in range(count):
+                nc.scalar.copy(out=dst[:, k], in_=src[:, first + k])
 
-        def quantize_w1(a):
-            w1_codes[a] = vector_tile([P, H], U32, "w1_codes%d" % a)
-            nc.vector.quantize_mx(out=w1_codes[a][:].bitcast(FP8X4), scales=w1_scales[:, a, :], in_=w1_bf16[a][:])
+        def quantize_w1():
+            for (a, first), rounded in w1_bf16.items():
+                count = rounded.shape[1]
+                codes = vector_tile([P, count * P], U32, "w1_codes")
+                nc.vector.quantize_mx(
+                    out=codes[:].bitcast(FP8X4), scales=w1_scales[:, a, first * P : (first + count) * P],
+                    in_=rounded[:].rearrange("p t c -> p (t c)"),
+                )
+                for k in range(count):
+                    w1_codes[a, first + k] = codes[:, k * P : (k + 1) * P]
 
         def round_w4():
-            w4_tiles["bf16"] = kept([P, PACK * N], BF16, "w4_bf16", tag="w1_bf16_1")
+            w4_tiles["bf16"] = kept([P, PACK * N], BF16, "w4_bf16", tag="w1_bf16_0_0")
             round_on_gpsimd(
                 w4_tiles["bf16"][:].rearrange("p (e m t) -> p e m t", e=2, t=PACK),
                 w4_raw[:].rearrange("p t (m e) -> p e m t", e=2),
@@ -237,7 +246,7 @@ def tile_list_citation_topic_scores_kernel(
                 channels = slice(t * P, (t + 1) * P)
                 for a in range(PASSES):
                     nc.tensor.matmul_mx(
-                        out=own_bank[u][:, t, :], lhsT=w1_codes[a][:, channels].bitcast(FP8X4),
+                        out=own_bank[u][:, t, :], lhsT=w1_codes[a, t].bitcast(FP8X4),
                         lhsT_scale=w1_scales[:, a, channels], rhs=picked_words[OWN, a, u].bitcast(FP8X4),
                         rhs_scale=picked_scales[OWN, u][4 * a :, :], start=(a == 0), stop=(a == PASSES - 1),
                     )
@@ -304,6 +313,14 @@ def tile_list_citation_topic_scores_kernel(
                 add_bias_on_scalar(result[:, e, :], bank[:, e, :], e)
             store(pair * PAIR, PAIR, result)
 
+        def finish_tile(u, second_adder):
+            result = scalar_tile([P, 2, TILE], F32, "result")
+            for e, adder in enumerate((add_bias_on_scalar, second_adder)):
+                bank = next_bank([P, TILE], "score_bank")
+                score_product(bank[:], e, u * TILE, TILE)
+                adder(result[:, e, :], bank[:], e)
+            store(u * TILE, TILE, result)
+
 
         nc.gpsimd.memset(table_scales[:], 0)
         nc.vector.memset(w3_planes[:], 0)
@@ -317,29 +334,27 @@ def tile_list_citation_topic_scores_kernel(
         nc.sync.dma_start(offsets[FIRST][:], offs2)
         for q in range(QUADS):
             load_table_planes(nc.sync, q)
-        nc.sync.dma_start(offsets[LAST][:], offs3)
         load_words(table_words[0], tab_words[0])
+        nc.sync.dma_start(offsets[LAST][:], offs3)
         load_words(w3_codes[0], w3_words[0])
         load_weight_planes(w3_planes, w3_scales, range(QUADS))
-        load_weight_planes(w2_planes, w2_scales, range(1))
         load_words(table_words[1], tab_words[1])
         load_words(w3_codes[1], w3_words[1])
         nc.sync.dma_start(out=w2_codes[:], in_=w2_words.rearrange("a p e -> p a e").bitcast(I32))
-        load_weight_planes(w2_planes, w2_scales, range(1, QUADS))
+        load_weight_planes(w2_planes, w2_scales, range(QUADS))
+        load_w1(0)
 
         own_rows = gather_own_rows()
         identity = kept([P, P], F32, "identity", tag="scale_rows")
         make_identity(nc, identity[:])
         gather_first_scales(nc.sync, 0)
         gather_scales(LAST, 0, HALF)
-        gather_words(LAST, 0, 0, pairs=2)
-        load_w1(0)
         load_w1(1)
+        gather_words(LAST, 0, 0, pairs=2)
         gather_words(FIRST, 0, 0, pairs=2)
-        gather_words(LAST, 1, 0)
-        gather_words(LAST, 1, 1)
-        gather_words(FIRST, 1, 0)
-        gather_words(FIRST, 1, 1)
+        for name in (LAST, FIRST):
+            for pair in range(2):
+                gather_words(name, 1, pair)
         for name in (LAST, FIRST):
             for a in range(PASSES):
                 for u in tiles_of(0) + tiles_of(1):
@@ -358,11 +373,11 @@ def tile_list_citation_topic_scores_kernel(
         gather_passes(FIRST, 2)
         gather_passes(OWN, 0)
         absolute_differences(0)
-        round_w1_on_gpsimd(0, range(PACK))
-        round_w1_on_gpsimd(1, range(1))
-        round_w1_on_scalar(1, range(1, PACK))
-        for a in range(PASSES):
-            quantize_w1(a)
+        round_w1_on_gpsimd(0, 0, PACK)
+        round_w1_on_gpsimd(1, 0, 1)
+        round_w1_on_scalar(1, 1, 1)
+        round_w1_on_scalar(1, 2, 2)
+        quantize_w1()
         round_w4()
         gather_passes(FIRST, 3)
         gather_passes(OWN, 1)
@@ -387,14 +402,14 @@ def tile_list_citation_topic_scores_kernel(
         second_last, last = tiles_of(PAIRS - 1)
         for u in tiles_of(1) + tiles_of(2):
             own_product(u)
+        relu_on_scalar(0)
         for u in tiles_of(1):
             add_on_vector(u)
-        relu_on_scalar(0)
+        relu_on_scalar(1)
         absolute_differences(*tiles_of(3))
         own_product(second_last)
-        add_on_vector(tiles_of(2)[0])
-        relu_on_vector(PAIR, PAIR)
-        add_on_vector(tiles_of(2)[1])
+        for u in tiles_of(2):
+            add_on_vector(u)
         quantize_w4()
 
         finish_pair(0)
@@ -403,20 +418,11 @@ def tile_list_citation_topic_scores_kernel(
         finish_pair(1)
         add_on_vector(second_last)
         finish_pair(2)
-        add_on_vector(last)
 
-        last_starts = [u * TILE for u in tiles_of(PAIRS - 1)]
-        for start in last_starts:
-            relu_on_vector(start, TILE)
-        results, banks = {}, {}
-        for start in last_starts:
-            quantize_h(start, TILE)
-            results[start] = scalar_tile([P, 2, TILE], F32, "result")
-            for e in range(2):
-                banks[start, e] = next_bank([P, TILE], "score_bank")
-                score_product(banks[start, e][:], e, start, TILE)
-        for start in last_starts:
-            add_bias_on_scalar(results[start][:, 0, :], banks[start, 0][:], 0)
-            add_bias_on_vector(results[start][:, 1, :], banks[start, 1][:], 1)
-        for start in last_starts:
-            store(start, TILE, results[start])
+        relu_on_vector(second_last * TILE, TILE)
+        add_on_vector(last)
+        quantize_h(second_last * TILE, TILE)
+        relu_on_vector(last * TILE, TILE)
+        quantize_h(last * TILE, TILE)
+        finish_tile(second_last, add_bias_on_scalar)
+        finish_tile(last, add_bias_on_vector)

@@ -331,11 +331,11 @@ def tile_list_citation_topic_scores_kernel(
 
         nc.sync.dma_start(offsets[OWN][:], offs)
         nc.sync.dma_start(out=scale_rows[ROWS_AT:P, :], in_=tab_scales.rearrange("a q t -> (a q) t").bitcast(I32))
-        nc.sync.dma_start(offsets[FIRST][:], offs2)
+        nc.sync.dma_start(offsets[LAST][:], offs3)
         for q in range(QUADS):
             load_table_planes(nc.sync, q)
         load_words(table_words[0], tab_words[0])
-        nc.sync.dma_start(offsets[LAST][:], offs3)
+        nc.sync.dma_start(offsets[FIRST][:], offs2)
         load_words(w3_codes[0], w3_words[0])
         load_weight_planes(w3_planes, w3_scales, range(QUADS))
         load_words(table_words[1], tab_words[1])
@@ -347,14 +347,16 @@ def tile_list_citation_topic_scores_kernel(
         own_rows = gather_own_rows()
         identity = kept([P, P], F32, "identity", tag="scale_rows")
         make_identity(nc, identity[:])
-        gather_first_scales(nc.sync, 0)
         gather_scales(LAST, 0, HALF)
-        load_w1(1)
         gather_words(LAST, 0, 0, pairs=2)
-        gather_words(FIRST, 0, 0, pairs=2)
-        for name in (LAST, FIRST):
-            for pair in range(2):
-                gather_words(name, 1, pair)
+        gather_first_scales(nc.sync, 0)
+        load_w1(1)
+        gather_words(FIRST, 0, 0)
+        gather_words(LAST, 1, 0)
+        gather_words(LAST, 1, 1)
+        gather_words(FIRST, 0, 1)
+        gather_words(FIRST, 1, 0)
+        gather_words(FIRST, 1, 1)
         for name in (LAST, FIRST):
             for a in range(PASSES):
                 for u in tiles_of(0) + tiles_of(1):
@@ -374,15 +376,13 @@ def tile_list_citation_topic_scores_kernel(
         gather_passes(OWN, 0)
         absolute_differences(0)
         round_w1_on_gpsimd(0, 0, PACK)
-        round_w1_on_gpsimd(1, 0, 1)
-        round_w1_on_scalar(1, 1, 1)
+        round_w1_on_gpsimd(1, 0, 2)
         round_w1_on_scalar(1, 2, 2)
         quantize_w1()
         round_w4()
         gather_passes(FIRST, 3)
         gather_passes(OWN, 1)
-        gather_passes(OWN, 2)
-        gather_passes(OWN, 3)
+        gather_passes(OWN, 2, pairs=2)
 
         cited_products(LAST, 2)
         stage(LAST, 2)
@@ -412,8 +412,8 @@ def tile_list_citation_topic_scores_kernel(
             add_on_vector(u)
         quantize_w4()
 
-        finish_pair(0)
         own_product(last)
+        finish_pair(0)
         relu_on_vector(2 * PAIR, PAIR)
         finish_pair(1)
         add_on_vector(second_last)

@@ -78,6 +78,7 @@ def tile_list_citation_topic_scores_kernel(
         bias = kept([P, 2], F32, "bias")
         picked_words = {}
         picked_scales = {}
+        pair_words = {}
         staged = {}
         distance = {}
         cited_bank = {}
@@ -128,8 +129,6 @@ def tile_list_citation_topic_scores_kernel(
                     nc.sync.dma_start(
                         out=own_plane[32 * q + 4 * a : 32 * q + 4 * a + 4, :], in_=rows[first : first + 4, :].bitcast(I32)
                     )
-            for u in range(TILES):
-                picked_scales[OWN, u] = own_plane[:].bitcast(U8)[:, u * TILE : (u + 1) * TILE]
 
         def gather_first_scales(queue, start):
             plane = gather_scales(FIRST, start, HALF)
@@ -145,6 +144,8 @@ def tile_list_citation_topic_scores_kernel(
             nc.vector.tensor_copy(words[:], window.indirect(offsets[name][:, columns]))
             for k in range(2 * pairs):
                 picked_words[name, a, 2 * pair + k] = words[:, k * TILE : (k + 1) * TILE]
+            for k in range(pairs):
+                pair_words[name, a, pair + k] = words[:, k * PAIR : (k + 1) * PAIR]
 
         def gather_passes(name, pair, pairs=1):
             for a in range(PASSES):
@@ -196,9 +197,6 @@ def tile_list_citation_topic_scores_kernel(
         def by_token(bank):
             return bank[:].rearrange("p t n -> p n t")
 
-        def by_two_tokens(bank):
-            return bank[:].rearrange("p t (m i) -> p m t i", i=2)
-
         def cited_pass(name, u, a):
             if a == 0:
                 cited_bank[name, u] = next_bank([P, H], "cited_bank")
@@ -227,58 +225,70 @@ def tile_list_citation_topic_scores_kernel(
                     out=staged[name, u][:], in_=sums, func=ACT.Copy, scale=-1.0 if name == LAST else 1.0
                 )
 
-        def absolute_differences(*tiles):
-            for u in tiles:
-                bank = next_bank([P, PACK, TILE], "diff_bank")
-                for t in range(PACK):
-                    for name in (FIRST, LAST):
-                        nc.tensor.matmul(
-                            out=bank[:, t, :], lhsT=staged[name, u][:, t].rearrange("p g i -> p (g i)"),
-                            rhs=identity[:], start=(name == FIRST), stop=(name == LAST), is_transpose=True,
-                        )
-                walk = by_two_tokens(bank) if u >= 2 else by_token(bank)
-                distance[u] = scalar_tile(list(walk.shape), F32, "distance")
-                nc.scalar.activation(out=distance[u][:], in_=walk, func=ACT.Abs)
+        def share(u):
+            if u // 2 == PAIRS - 1:
+                return range(PACK), u * TILE, TILE
+            return range(2 * (u % 2), 2 * (u % 2) + 2), u // 2 * PAIR, PAIR
+
+        def absolute_differences(*banks):
+            for u in banks:
+                places, start, count = share(u)
+                bank = next_bank([P, len(places), count], "diff_bank")
+                for k, t in enumerate(places):
+                    for first in range(0, count, TILE):
+                        for name in (FIRST, LAST):
+                            nc.tensor.matmul(
+                                out=bank[:, k, first : first + TILE],
+                                lhsT=staged[name, (start + first) // TILE][:, t].rearrange("p g i -> p (g i)"),
+                                rhs=identity[:], start=(name == FIRST), stop=(name == LAST), is_transpose=True,
+                            )
+                distance[u] = scalar_tile([P, count, len(places)], F32, "distance")
+                nc.scalar.activation(out=distance[u][:], in_=by_token(bank), func=ACT.Abs)
 
         def own_product(u):
-            own_bank[u] = next_bank([P, PACK, TILE], "own_bank")
-            for t in range(PACK):
-                channels = slice(t * P, (t + 1) * P)
+            places, start, count = share(u)
+            own_bank[u] = next_bank([P, len(places), count], "own_bank")
+            for k, t in enumerate(places):
                 for a in range(PASSES):
+                    words = pair_words[OWN, a, u // 2][:, start % PAIR : start % PAIR + count]
                     nc.tensor.matmul_mx(
-                        out=own_bank[u][:, t, :], lhsT=w1_codes[a, t].bitcast(FP8X4),
-                        lhsT_scale=w1_scales[:, a, channels], rhs=picked_words[OWN, a, u].bitcast(FP8X4),
-                        rhs_scale=picked_scales[OWN, u][4 * a :, :], start=(a == 0), stop=(a == PASSES - 1),
+                        out=own_bank[u][:, k, :], lhsT=w1_codes[a, t].bitcast(FP8X4),
+                        lhsT_scale=w1_scales[:, a, t * P : (t + 1) * P], rhs=words.bitcast(FP8X4),
+                        rhs_scale=own_plane[:].bitcast(U8)[4 * a :, start : start + count],
+                        start=(a == 0), stop=(a == PASSES - 1),
                     )
 
+        def sum_of(u):
+            return h_sum[u // 2][:, u % 2].rearrange("p (n t) -> p n t", t=len(share(u)[0]))
+
         def add_on_gpsimd(u):
-            own = scalar_tile([P, TILE, PACK], F32, "own")
+            own = scalar_tile(list(distance[u].shape), F32, "own")
             nc.scalar.activation(out=own[:], in_=by_token(own_bank[u]), func=ACT.Copy)
             if u % 2 == 0:
-                h_sum[u // 2] = kept([P, 2, TILE, PACK], BF16, "h_sum_first")
-            nc.gpsimd.tensor_tensor(out=h_sum[u // 2][:, u % 2], in0=own[:], in1=distance[u][:], op=ALU.add)
+                h_sum[u // 2] = kept([P, 2, H], BF16, "h_sum_first")
+            nc.gpsimd.tensor_tensor(out=sum_of(u), in0=own[:], in1=distance[u][:], op=ALU.add)
 
         def add_on_vector(u):
             if u % 2 == 0:
-                h_sum[u // 2] = vector_tile([P, 2, TILE, PACK], BF16, "h_sum")
-            nc.vector.tensor_tensor(
-                out=h_sum[u // 2][:, u % 2].rearrange("p (m i) t -> p m t i", i=2), in0=by_two_tokens(own_bank[u]),
-                in1=distance[u][:], op=ALU.add,
-            )
+                h_sum[u // 2] = vector_tile([P, 2, H], BF16, "h_sum")
+            nc.vector.tensor_tensor(out=sum_of(u), in0=by_token(own_bank[u]), in1=distance[u][:], op=ALU.add)
 
-        def sums_of(start, count):
-            first = PACK * (start % PAIR)
-            return h_sum[start // PAIR][:].rearrange("p u n t -> p (u n t)")[:, first : first + PACK * count]
+        def woven(pair):
+            return h_sum[pair][:].rearrange("p u (n t) -> p n u t", t=2)
 
         def relu_on_scalar(pair):
             h_bf16[pair * PAIR] = scalar_tile([P, PACK * PAIR], BF16, "h_relu")
-            nc.scalar.activation(out=h_bf16[pair * PAIR][:], in_=sums_of(pair * PAIR, PAIR), func=ACT.Relu)
+            nc.scalar.activation(
+                out=h_bf16[pair * PAIR][:].rearrange("p (n u t) -> p n u t", u=2, t=2), in_=woven(pair), func=ACT.Relu
+            )
 
         def relu_on_vector(start, count):
             h_bf16[start] = vector_tile([P, PACK * count], BF16, "h_bf16")
-            nc.vector.tensor_scalar(
-                out=h_bf16[start][:], in0=sums_of(start, count), scalar1=0.0, scalar2=None, op0=ALU.max
-            )
+            if count == PAIR:
+                result, sums = h_bf16[start][:].rearrange("p (n u t) -> p n u t", u=2, t=2), woven(start // PAIR)
+            else:
+                result, sums = h_bf16[start][:], h_sum[start // PAIR][:, start // TILE % 2]
+            nc.vector.tensor_scalar(out=result, in0=sums, scalar1=0.0, scalar2=None, op0=ALU.max)
 
         def quantize_h(start, count):
             h_codes[start] = vector_tile([P, count], U32, "h_codes")

@@ -27,6 +27,8 @@ TILES = S // TILE
 PAIR = 2 * TILE
 PAIRS = S // PAIR
 HALF = S // 2
+EARLY = 3 * PAIR
+SHARE = 4
 OWN, FIRST, LAST = "own", "first", "last"
 
 ROWS_AT = P - 32
@@ -66,22 +68,30 @@ def tile_list_citation_topic_scores_kernel(
         w3_planes = kept([P, PASSES, H // 4], I32, "w3_planes")
         w2_codes = kept([P, PASSES, H // 2], I32, "w2_codes")
         w3_codes = [kept([P, H], I32, "w3_codes%d" % a) for a in range(PASSES)]
-        w1_raw = [kept([P, PACK, H], F32, "w1_raw%d" % a) for a in range(PASSES)]
-        w1_bf16 = {}
+        w1_raw = {
+            (a, half): kept([P, PACK, H // 2], F32, "w1_raw%d%d" % (a, half)) for a in range(PASSES) for half in range(2)
+        }
+        w1_bf16 = {
+            (0, 0): kept([P, PACK * H], BF16, "w1_bf16_00"),
+            (1, 0): kept([P, SHARE * H], BF16, "w1_bf16_10"),
+        }
         w1_scales = kept([P, PASSES, H], U8, "w1_scales")
         w4_raw = kept([P, PACK, N], F32, "w4_raw")
         w4_scales = kept([P, N], U8, "w4_scales")
         h_scales = kept([P, S], U8, "h_scales")
         first_scales_pass1 = kept([P, S // 4], I32, "first_scales_pass1")
         scale_rows = kept([P, T // 4], I32, "scale_rows")
-        own_plane = kept([P, S // 4], I32, "own_plane")
+        own_plane = kept([P, EARLY // 4], I32, "own_plane")
         bias = kept([P, 2], F32, "bias")
         picked_words = {}
         picked_scales = {}
+        scale_planes = {}
         pair_words = {}
         staged = {}
         distance = {}
         cited_bank = {}
+        diff_bank = {}
+        own_copy = {}
         own_bank = {}
         h_sum = {}
         h_bf16, h_codes = {}, {}
@@ -104,9 +114,9 @@ def tile_list_citation_topic_scores_kernel(
                 rows = scales.bitcast(I32)[:, 4 * q : 4 * q + 4, :].rearrange("a r e -> r a e")
                 nc.sync.dma_start(out=planes[32 * q : 32 * q + 4, :, :], in_=rows)
 
-        def load_w1(a):
-            rows = w1[P * PACK * a : P * PACK * (a + 1), :]
-            nc.sync.dma_start(out=w1_raw[a][:], in_=rows.rearrange("(p j) r -> p j r", j=PACK))
+        def load_w1(a, half):
+            rows = w1[P * PACK * a : P * PACK * (a + 1), half * H // 2 : (half + 1) * H // 2]
+            nc.sync.dma_start(out=w1_raw[a, half][:], in_=rows.rearrange("(p j) r -> p j r", j=PACK))
 
 
         def gather_scales(name, start, count):
@@ -115,20 +125,20 @@ def tile_list_citation_topic_scores_kernel(
             nc.vector.tensor_copy(plane[:], window.indirect(offsets[name][:, start // 16 : (start + count) // 16]))
             for k in range(count // TILE):
                 picked_scales[name, start // TILE + k] = plane[:, k * TILE : (k + 1) * TILE]
+            scale_planes[name, start] = plane
             return plane
 
         def gather_own_rows():
-            rows = vector_tile([P, S], U8, "own_rows")
-            nc.vector.tensor_copy(rows[:], scale_rows[:].bitcast(U8).indirect(offsets[OWN][:]))
+            rows = vector_tile([P, EARLY], U8, "own_rows")
+            nc.vector.tensor_copy(rows[:], scale_rows[:].bitcast(U8).indirect(offsets[OWN][:, 0 : EARLY // 16]))
             return rows
 
-        def move_own_rows(rows):
-            for a in range(PASSES):
-                for q in range(QUADS):
-                    first = ROWS_AT + 16 * a + 4 * q
-                    nc.sync.dma_start(
-                        out=own_plane[32 * q + 4 * a : 32 * q + 4 * a + 4, :], in_=rows[first : first + 4, :].bitcast(I32)
-                    )
+        def move_own_rows(rows, a):
+            for q in range(QUADS):
+                first = ROWS_AT + 16 * a + 4 * q
+                nc.sync.dma_start(
+                    out=own_plane[32 * q + 4 * a : 32 * q + 4 * a + 4, :], in_=rows[first : first + 4, :].bitcast(I32)
+                )
 
         def gather_first_scales(queue, start):
             plane = gather_scales(FIRST, start, HALF)
@@ -136,6 +146,12 @@ def tile_list_citation_topic_scores_kernel(
                 out=first_scales_pass1[0:MOVED_ROWS, start // 4 : (start + HALF) // 4],
                 in_=plane[4 : 4 + MOVED_ROWS, :].bitcast(I32),
             )
+
+        def gather_tile(name, a, u):
+            words = vector_tile([P, TILE], U32, "words_%s%d" % (name, a))
+            columns = slice(u * TILE // 16, (u + 1) * TILE // 16)
+            nc.vector.tensor_copy(words[:], table_words[a][:].bitcast(U32).indirect(offsets[name][:, columns]))
+            picked_words[name, a, u] = words[:]
 
         def gather_words(name, a, pair, pairs=1):
             words = vector_tile([P, pairs * PAIR], U32, "words_%s%d" % (name, a))
@@ -155,33 +171,32 @@ def tile_list_citation_topic_scores_kernel(
         def round_on_gpsimd(dst, src):
             nc.gpsimd.tensor_scalar(out=dst, in0=src, scalar1=1.0, scalar2=0.0, op0=ALU.mult, op1=ALU.add)
 
-        def round_w1_on_gpsimd(a, first, count):
-            w1_bf16[a, first] = kept([P, count, PACK * P], BF16, "w1_bf16_%d_%d" % (a, first))
-            src = w1_raw[a][:].rearrange("p j (g t i) -> p t g i j", t=PACK, i=RUN)
-            dst = w1_bf16[a, first][:].rearrange("p t (g i j) -> p t g i j", i=RUN, j=PACK)
-            for k in range(count):
-                round_on_gpsimd(dst[:, k], src[:, first + k])
+        def rounded(a, first, half):
+            blocks = w1_bf16[a, first][:].rearrange("p (t g c) -> p t g c", g=2 * RUN, c=RUN * PACK)
+            return blocks[:, :, half * RUN : (half + 1) * RUN, :]
 
-        def round_w1_on_scalar(a, first, count):
-            w1_bf16[a, first] = scalar_tile([P, count, PACK * P], BF16, "w1_bf16")
-            src = w1_raw[a][:].rearrange("p j (g t u i) -> p t g u j i", t=PACK, u=2, i=4)
-            dst = w1_bf16[a, first][:].rearrange("p t (g u i j) -> p t g u j i", u=2, i=4, j=PACK)
-            for k in range(count):
-                nc.scalar.copy(out=dst[:, k], in_=src[:, first + k])
+        def round_w1_on_gpsimd(a, half, count):
+            src = w1_raw[a, half][:].rearrange("p j (g t i) -> p g t i j", t=PACK, i=RUN)[:, :, 0:count]
+            round_on_gpsimd(rounded(a, 0, half).rearrange("p t g (i j) -> p g t i j", j=PACK), src)
 
-        def quantize_w1():
-            for (a, first), rounded in w1_bf16.items():
-                count = rounded.shape[1]
-                codes = vector_tile([P, count * P], U32, "w1_codes")
-                nc.vector.quantize_mx(
-                    out=codes[:].bitcast(FP8X4), scales=w1_scales[:, a, first * P : (first + count) * P],
-                    in_=rounded[:].rearrange("p t c -> p (t c)"),
-                )
-                for k in range(count):
-                    w1_codes[a, first + k] = codes[:, k * P : (k + 1) * P]
+        def round_w1_on_scalar(a, half, first):
+            src = w1_raw[a, half][:].rearrange("p j (g t u i) -> p t g u j i", t=PACK, u=2, i=4)
+            dst = rounded(a, first, half).rearrange("p t g (u i j) -> p t g u j i", u=2, j=PACK)
+            for t in range(first, PACK):
+                nc.scalar.copy(out=dst[:, t - first], in_=src[:, t])
+
+        def quantize_w1(a, first):
+            count = w1_bf16[a, first].shape[1] // H
+            codes = vector_tile([P, count * P], U32, "w1_codes")
+            nc.vector.quantize_mx(
+                out=codes[:].bitcast(FP8X4), scales=w1_scales[:, a, first * P : (first + count) * P],
+                in_=w1_bf16[a, first][:],
+            )
+            for k in range(count):
+                w1_codes[a, first + k] = codes[:, k * P : (k + 1) * P]
 
         def round_w4():
-            w4_tiles["bf16"] = kept([P, PACK * N], BF16, "w4_bf16", tag="w1_bf16_0_0")
+            w4_tiles["bf16"] = kept([P, PACK * N], BF16, "w4_bf16", tag="w1_bf16_10")
             round_on_gpsimd(
                 w4_tiles["bf16"][:].rearrange("p (e m t) -> p e m t", e=2, t=PACK),
                 w4_raw[:].rearrange("p t (m e) -> p e m t", e=2),
@@ -197,8 +212,8 @@ def tile_list_citation_topic_scores_kernel(
         def by_token(bank):
             return bank[:].rearrange("p t n -> p n t")
 
-        def cited_pass(name, u, a):
-            if a == 0:
+        def cited_pass(name, u, a, first=0):
+            if a == first:
                 cited_bank[name, u] = next_bank([P, H], "cited_bank")
             if name == LAST:
                 weight, weight_plane = w3_codes[a][:].bitcast(FP8X4), w3_planes[:].bitcast(U8)[:, a, :]
@@ -209,16 +224,16 @@ def tile_list_citation_topic_scores_kernel(
                 token_plane = moved_plane if a else picked_scales[FIRST, u]
             nc.tensor.matmul_mx(
                 out=cited_bank[name, u][:], lhsT=picked_words[name, a, u].bitcast(FP8X4), lhsT_scale=token_plane,
-                rhs=weight, rhs_scale=weight_plane, start=(a == 0), stop=(a == PASSES - 1),
+                rhs=weight, rhs_scale=weight_plane, start=(a == first), stop=(a != first),
             )
 
-        def cited_products(name, pair):
+        def cited_products(name, pair, first=0):
             for u in tiles_of(pair):
-                for a in range(PASSES):
-                    cited_pass(name, u, a)
+                for a in (first, 1 - first):
+                    cited_pass(name, u, a, first)
 
-        def stage(name, pair):
-            for u in tiles_of(pair):
+        def stage(name, *tiles):
+            for u in tiles:
                 staged[name, u] = scalar_tile([P, PACK, H // (PACK * RUN), RUN], F32, "staged_" + name)
                 sums = cited_bank[name, u][:].rearrange("p (g t i) -> p t g i", t=PACK, i=RUN)
                 nc.scalar.activation(
@@ -230,7 +245,7 @@ def tile_list_citation_topic_scores_kernel(
                 return range(PACK), u * TILE, TILE
             return range(2 * (u % 2), 2 * (u % 2) + 2), u // 2 * PAIR, PAIR
 
-        def absolute_differences(*banks):
+        def differences(*banks):
             for u in banks:
                 places, start, count = share(u)
                 bank = next_bank([P, len(places), count], "diff_bank")
@@ -242,34 +257,43 @@ def tile_list_citation_topic_scores_kernel(
                                 lhsT=staged[name, (start + first) // TILE][:, t].rearrange("p g i -> p (g i)"),
                                 rhs=identity[:], start=(name == FIRST), stop=(name == LAST), is_transpose=True,
                             )
+                diff_bank[u] = bank
+
+        def absolute_values(*banks):
+            for u in banks:
+                places, start, count = share(u)
                 distance[u] = scalar_tile([P, count, len(places)], F32, "distance")
-                nc.scalar.activation(out=distance[u][:], in_=by_token(bank), func=ACT.Abs)
+                nc.scalar.activation(out=distance[u][:], in_=by_token(diff_bank[u]), func=ACT.Abs)
 
         def own_product(u):
             places, start, count = share(u)
             own_bank[u] = next_bank([P, len(places), count], "own_bank")
+            plane = own_plane[:].bitcast(U8) if start < EARLY else scale_planes[OWN, EARLY][:]
             for k, t in enumerate(places):
                 for a in range(PASSES):
                     words = pair_words[OWN, a, u // 2][:, start % PAIR : start % PAIR + count]
                     nc.tensor.matmul_mx(
                         out=own_bank[u][:, k, :], lhsT=w1_codes[a, t].bitcast(FP8X4),
                         lhsT_scale=w1_scales[:, a, t * P : (t + 1) * P], rhs=words.bitcast(FP8X4),
-                        rhs_scale=own_plane[:].bitcast(U8)[4 * a :, start : start + count],
+                        rhs_scale=plane[4 * a :, start % EARLY : start % EARLY + count],
                         start=(a == 0), stop=(a == PASSES - 1),
                     )
 
         def sum_of(u):
             return h_sum[u // 2][:, u % 2].rearrange("p (n t) -> p n t", t=len(share(u)[0]))
 
-        def add_on_gpsimd(u):
+        def copy_own(u):
             own = scalar_tile(list(distance[u].shape), F32, "own")
             nc.scalar.activation(out=own[:], in_=by_token(own_bank[u]), func=ACT.Copy)
-            if u % 2 == 0:
-                h_sum[u // 2] = kept([P, 2, H], BF16, "h_sum_first")
-            nc.gpsimd.tensor_tensor(out=sum_of(u), in0=own[:], in1=distance[u][:], op=ALU.add)
+            own_copy[u] = own
+
+        def add_on_gpsimd(u):
+            if u // 2 not in h_sum:
+                h_sum[u // 2] = kept([P, 2, H], BF16, "h_sum_early")
+            nc.gpsimd.tensor_tensor(out=sum_of(u), in0=own_copy[u][:], in1=distance[u][:], op=ALU.add)
 
         def add_on_vector(u):
-            if u % 2 == 0:
+            if u // 2 not in h_sum:
                 h_sum[u // 2] = vector_tile([P, 2, H], BF16, "h_sum")
             nc.vector.tensor_tensor(out=sum_of(u), in0=by_token(own_bank[u]), in1=distance[u][:], op=ALU.add)
 
@@ -280,6 +304,13 @@ def tile_list_citation_topic_scores_kernel(
             h_bf16[pair * PAIR] = scalar_tile([P, PACK * PAIR], BF16, "h_relu")
             nc.scalar.activation(
                 out=h_bf16[pair * PAIR][:].rearrange("p (n u t) -> p n u t", u=2, t=2), in_=woven(pair), func=ACT.Relu
+            )
+
+        def relu_on_gpsimd(pair):
+            h_bf16[pair * PAIR] = kept([P, PACK * PAIR], BF16, "h_relu%d" % pair)
+            nc.gpsimd.tensor_scalar(
+                out=h_bf16[pair * PAIR][:].rearrange("p (n u t) -> p n u t", u=2, t=2), in0=woven(pair),
+                scalar1=0.0, scalar2=0.0, op0=ALU.max, op1=ALU.add,
             )
 
         def relu_on_vector(start, count):
@@ -314,7 +345,6 @@ def tile_list_citation_topic_scores_kernel(
             nc.sync.dma_start(out=out.rearrange("(m e) s -> m e s", e=2)[:, :, start : start + count], in_=result[:])
 
         def finish_pair(pair):
-            quantize_h(pair * PAIR, PAIR)
             bank = next_bank([P, 2, PAIR], "score_bank")
             for e in range(2):
                 score_product(bank[:, e, :], e, pair * PAIR, PAIR)
@@ -352,83 +382,107 @@ def tile_list_citation_topic_scores_kernel(
         load_words(w3_codes[1], w3_words[1])
         nc.sync.dma_start(out=w2_codes[:], in_=w2_words.rearrange("a p e -> p a e").bitcast(I32))
         load_weight_planes(w2_planes, w2_scales, range(QUADS))
-        load_w1(0)
+        load_w1(0, 0)
 
         own_rows = gather_own_rows()
-        identity = kept([P, P], F32, "identity", tag="scale_rows")
+        identity = kept([P, P], F32, "identity")
         make_identity(nc, identity[:])
-        gather_scales(LAST, 0, HALF)
-        gather_words(LAST, 0, 0, pairs=2)
+        gather_scales(LAST, 0, EARLY)
+        gather_words(LAST, 0, 0)
+        gather_words(LAST, 0, 1)
         gather_first_scales(nc.sync, 0)
-        load_w1(1)
+        load_w1(0, 1)
+        load_w1(1, 0)
+        move_own_rows(own_rows, 0)
+        load_w1(1, 1)
+        move_own_rows(own_rows, 1)
+        for t in range(PACK):
+            nc.sync.dma_start(out=w4_raw[:, t, :], in_=w4.rearrange("(g t i) n -> t g i n", t=PACK, i=RUN)[t])
+        nc.sync.dma_start(out=bias[:], in_=b.rearrange("(m e) -> m e", e=2))
         gather_words(FIRST, 0, 0)
-        gather_words(LAST, 1, 0)
+        gather_tile(LAST, 1, 0)
+        gather_tile(LAST, 1, 1)
         gather_words(LAST, 1, 1)
         gather_words(FIRST, 0, 1)
         gather_words(FIRST, 1, 0)
         gather_words(FIRST, 1, 1)
-        for name in (LAST, FIRST):
-            for a in range(PASSES):
-                for u in tiles_of(0) + tiles_of(1):
-                    cited_pass(name, u, a)
-            stage(name, 0)
-            stage(name, 1)
+        for a in range(PASSES):
+            for u in tiles_of(0) + tiles_of(1):
+                cited_pass(LAST, u, a)
+        stage(LAST, *tiles_of(0))
+        stage(LAST, *tiles_of(1))
+        for u in range(3):
+            cited_pass(FIRST, u, 0)
+        cited_pass(FIRST, 0, 1)
+        cited_pass(FIRST, 1, 1)
+        cited_pass(FIRST, 2, 1)
+        cited_pass(FIRST, 3, 1, first=1)
+        cited_pass(FIRST, 3, 0, first=1)
+        stage(FIRST, 0, 1, 2, 3)
 
-        gather_scales(LAST, HALF, HALF)
         gather_passes(LAST, 2)
-        move_own_rows(own_rows)
         gather_first_scales(nc.sync, HALF)
-        for t in range(PACK):
-            nc.sync.dma_start(out=w4_raw[:, t, :], in_=w4.rearrange("(g t i) n -> t g i n", t=PACK, i=RUN)[t])
-        nc.sync.dma_start(out=bias[:], in_=b.rearrange("(m e) -> m e", e=2))
+        gather_scales(LAST, EARLY, S - EARLY)
         gather_passes(LAST, 3)
         gather_passes(FIRST, 2)
         gather_passes(OWN, 0)
-        absolute_differences(0)
-        round_w1_on_gpsimd(0, 0, PACK)
-        round_w1_on_gpsimd(1, 0, 2)
-        round_w1_on_scalar(1, 2, 2)
-        quantize_w1()
+        for a in range(PASSES):
+            for half in range(2):
+                round_w1_on_gpsimd(a, half, PACK)
+        quantize_w1(0, 0)
+        quantize_w1(1, 0)
         round_w4()
         gather_passes(FIRST, 3)
         gather_passes(OWN, 1)
-        gather_passes(OWN, 2, pairs=2)
+        gather_passes(OWN, 2)
+        gather_scales(OWN, EARLY, S - EARLY)
+        gather_passes(OWN, 3)
 
+        differences(0, 1)
         cited_products(LAST, 2)
-        stage(LAST, 2)
-        absolute_differences(1, 2)
+        absolute_values(0, 1)
+        differences(2, 3)
+        stage(LAST, 4, 5)
         cited_products(LAST, 3)
-        absolute_differences(3)
-        cited_products(FIRST, 2)
-        stage(LAST, 3)
-        stage(FIRST, 2)
+        absolute_values(2, 3)
+        cited_products(FIRST, 2, first=1)
+        stage(LAST, 6, 7)
+        own_product(0)
+        own_product(1)
+        stage(FIRST, 4, 5)
         for u in tiles_of(0):
-            own_product(u)
+            copy_own(u)
             add_on_gpsimd(u)
-        cited_products(FIRST, 3)
-        absolute_differences(*tiles_of(2))
-        stage(FIRST, 3)
+        cited_products(FIRST, 3, first=1)
+        own_product(2)
+        own_product(3)
+        stage(FIRST, 6, 7)
+        copy_own(2)
+        differences(4, 5)
+        absolute_values(4, 5)
+        own_product(4)
+        own_product(5)
+        differences(6, 7)
 
         second_last, last = tiles_of(PAIRS - 1)
-        for u in tiles_of(1) + tiles_of(2):
-            own_product(u)
-        relu_on_scalar(0)
-        for u in tiles_of(1):
-            add_on_vector(u)
-        relu_on_scalar(1)
-        absolute_differences(*tiles_of(3))
-        own_product(second_last)
-        for u in tiles_of(2):
-            add_on_vector(u)
+        add_on_vector(3)
+        add_on_gpsimd(2)
         quantize_w4()
-
-        own_product(last)
+        relu_on_vector(0, PAIR)
+        relu_on_scalar(1)
+        absolute_values(6, 7)
+        add_on_vector(4)
+        quantize_h(0, PAIR)
+        add_on_vector(5)
+        own_product(second_last)
         finish_pair(0)
+        quantize_h(PAIR, PAIR)
         relu_on_vector(2 * PAIR, PAIR)
+        own_product(last)
         finish_pair(1)
         add_on_vector(second_last)
+        quantize_h(2 * PAIR, PAIR)
         finish_pair(2)
-
         relu_on_vector(second_last * TILE, TILE)
         add_on_vector(last)
         quantize_h(second_last * TILE, TILE)

@@ -88,6 +88,7 @@ def tile_list_citation_topic_scores_kernel(
         scale_planes = {}
         pair_words = {}
         staged = {}
+        subtracted = {}
         distance = {}
         cited_bank = {}
         diff_bank = {}
@@ -240,6 +241,10 @@ def tile_list_citation_topic_scores_kernel(
                     out=staged[name, u][:], in_=sums, func=ACT.Copy, scale=-1.0 if name == LAST else 1.0
                 )
 
+        def subtract_on_gpsimd(u):
+            subtracted[u] = kept([P, PACK, H // (PACK * RUN), RUN], F32, "subtracted%d" % u)
+            nc.gpsimd.tensor_tensor(out=subtracted[u][:], in0=staged[FIRST, u][:], in1=staged[LAST, u][:], op=ALU.add)
+
         def share(u):
             if u // 2 == PAIRS - 1:
                 return range(PACK), u * TILE, TILE
@@ -251,11 +256,12 @@ def tile_list_citation_topic_scores_kernel(
                 bank = next_bank([P, len(places), count], "diff_bank")
                 for k, t in enumerate(places):
                     for first in range(0, count, TILE):
-                        for name in (FIRST, LAST):
+                        tile = (start + first) // TILE
+                        terms = [subtracted[tile]] if tile in subtracted else [staged[FIRST, tile], staged[LAST, tile]]
+                        for n, term in enumerate(terms):
                             nc.tensor.matmul(
-                                out=bank[:, k, first : first + TILE],
-                                lhsT=staged[name, (start + first) // TILE][:, t].rearrange("p g i -> p (g i)"),
-                                rhs=identity[:], start=(name == FIRST), stop=(name == LAST), is_transpose=True,
+                                out=bank[:, k, first : first + TILE], lhsT=term[:, t].rearrange("p g i -> p (g i)"),
+                                rhs=identity[:], start=(n == 0), stop=(n == len(terms) - 1), is_transpose=True,
                             )
                 diff_bank[u] = bank
 
@@ -289,7 +295,7 @@ def tile_list_citation_topic_scores_kernel(
 
         def add_on_gpsimd(u):
             if u // 2 not in h_sum:
-                h_sum[u // 2] = kept([P, 2, H], BF16, "h_sum_early")
+                h_sum[u // 2] = kept([P, 2, H], BF16, "h_sum_early%d" % (u // 2))
             nc.gpsimd.tensor_tensor(out=sum_of(u), in0=own_copy[u][:], in1=distance[u][:], op=ALU.add)
 
         def add_on_vector(u):
@@ -369,8 +375,8 @@ def tile_list_citation_topic_scores_kernel(
         nc.vector.memset(first_scales_pass1[:], 0)
         nc.vector.memset(own_plane[:], 0)
 
-        nc.sync.dma_start(offsets[OWN][:], offs)
         nc.sync.dma_start(out=scale_rows[ROWS_AT:P, :], in_=tab_scales.rearrange("a q t -> (a q) t").bitcast(I32))
+        nc.sync.dma_start(offsets[OWN][:], offs)
         nc.sync.dma_start(offsets[LAST][:], offs3)
         for q in range(QUADS):
             load_table_planes(nc.sync, q)
@@ -432,17 +438,17 @@ def tile_list_citation_topic_scores_kernel(
         quantize_w1(0, 0)
         quantize_w1(1, 0)
         round_w4()
-        gather_passes(FIRST, 3)
         gather_passes(OWN, 1)
+        gather_passes(FIRST, 3)
         gather_passes(OWN, 2)
         gather_scales(OWN, EARLY, S - EARLY)
         gather_passes(OWN, 3)
 
-        differences(0, 1)
         cited_products(LAST, 2)
-        absolute_values(0, 1)
-        differences(2, 3)
+        differences(0, 1)
         stage(LAST, 4, 5)
+        differences(2, 3)
+        absolute_values(0, 1)
         cited_products(LAST, 3)
         absolute_values(2, 3)
         cited_products(FIRST, 2, first=1)
@@ -453,13 +459,13 @@ def tile_list_citation_topic_scores_kernel(
         for u in tiles_of(0):
             copy_own(u)
             add_on_gpsimd(u)
-        cited_products(FIRST, 3, first=1)
+        differences(4, 5)
         own_product(2)
         own_product(3)
-        stage(FIRST, 6, 7)
-        copy_own(2)
-        differences(4, 5)
         absolute_values(4, 5)
+        copy_own(2)
+        cited_products(FIRST, 3, first=1)
+        stage(FIRST, 6, 7)
         own_product(4)
         own_product(5)
         differences(6, 7)
@@ -467,26 +473,26 @@ def tile_list_citation_topic_scores_kernel(
         second_last, last = tiles_of(PAIRS - 1)
         add_on_vector(3)
         add_on_gpsimd(2)
+        add_on_vector(4)
         quantize_w4()
         relu_on_vector(0, PAIR)
         relu_on_scalar(1)
         absolute_values(6, 7)
-        add_on_vector(4)
-        quantize_h(0, PAIR)
         add_on_vector(5)
+        quantize_h(0, PAIR)
         own_product(second_last)
+        own_product(last)
         finish_pair(0)
         quantize_h(PAIR, PAIR)
         relu_on_vector(2 * PAIR, PAIR)
-        own_product(last)
         finish_pair(1)
         add_on_vector(second_last)
         quantize_h(2 * PAIR, PAIR)
         finish_pair(2)
-        relu_on_vector(second_last * TILE, TILE)
         add_on_vector(last)
-        quantize_h(second_last * TILE, TILE)
-        relu_on_vector(last * TILE, TILE)
-        quantize_h(last * TILE, TILE)
+        for u in tiles_of(PAIRS - 1):
+            relu_on_vector(u * TILE, TILE)
+        for u in tiles_of(PAIRS - 1):
+            quantize_h(u * TILE, TILE)
         finish_tile(second_last, add_bias_on_scalar)
         finish_tile(last, add_bias_on_vector)

@@ -28,7 +28,7 @@ PAIR = 2 * TILE
 PAIRS = S // PAIR
 HALF = S // 2
 EARLY = 3 * PAIR
-SHARE = 4
+SHARE = 3
 OWN, FIRST, LAST = "own", "first", "last"
 
 ROWS_AT = P - 32
@@ -316,7 +316,7 @@ def tile_list_citation_topic_scores_kernel(
             h_bf16[pair * PAIR] = kept([P, PACK * PAIR], BF16, "h_relu%d" % pair)
             nc.gpsimd.tensor_scalar(
                 out=h_bf16[pair * PAIR][:].rearrange("p (n u t) -> p n u t", u=2, t=2), in0=woven(pair),
-                scalar1=0.0, scalar2=0.0, op0=ALU.max, op1=ALU.add,
+                scalar1=float("inf"), scalar2=0.0, op0=ALU.min, op1=ALU.max,
             )
 
         def relu_on_vector(start, count):
@@ -396,8 +396,8 @@ def tile_list_citation_topic_scores_kernel(
         gather_scales(LAST, 0, EARLY)
         gather_words(LAST, 0, 0)
         gather_words(LAST, 0, 1)
-        gather_first_scales(nc.sync, 0)
         load_w1(0, 1)
+        gather_first_scales(nc.sync, 0)
         load_w1(1, 0)
         move_own_rows(own_rows, 0)
         load_w1(1, 1)
@@ -428,31 +428,33 @@ def tile_list_citation_topic_scores_kernel(
 
         gather_passes(LAST, 2)
         gather_first_scales(nc.sync, HALF)
-        gather_scales(LAST, EARLY, S - EARLY)
-        gather_passes(LAST, 3)
         gather_passes(FIRST, 2)
         gather_passes(OWN, 0)
         for a in range(PASSES):
             for half in range(2):
-                round_w1_on_gpsimd(a, half, PACK)
+                round_w1_on_gpsimd(a, half, SHARE if a else PACK)
+        cited_products(LAST, 2)
+        differences(0, 1)
+        stage(LAST, 4, 5)
+        w1_bf16[1, SHARE] = scalar_tile([P, (PACK - SHARE) * H], BF16, "w1_bf16_rest")
+        round_w1_on_scalar(1, 1, SHARE)
+        round_w1_on_scalar(1, 0, SHARE)
         quantize_w1(0, 0)
+        quantize_w1(1, SHARE)
         quantize_w1(1, 0)
         round_w4()
         gather_passes(OWN, 1)
+        gather_scales(LAST, EARLY, S - EARLY)
+        gather_passes(LAST, 3)
         gather_passes(FIRST, 3)
         gather_passes(OWN, 2)
         gather_scales(OWN, EARLY, S - EARLY)
         gather_passes(OWN, 3)
 
-        cited_products(LAST, 2)
-        differences(0, 1)
-        stage(LAST, 4, 5)
         differences(2, 3)
         absolute_values(0, 1)
-        cited_products(LAST, 3)
-        absolute_values(2, 3)
         cited_products(FIRST, 2, first=1)
-        stage(LAST, 6, 7)
+        absolute_values(2, 3)
         own_product(0)
         own_product(1)
         stage(FIRST, 4, 5)
@@ -463,31 +465,33 @@ def tile_list_citation_topic_scores_kernel(
         own_product(2)
         own_product(3)
         absolute_values(4, 5)
-        copy_own(2)
+        for u in tiles_of(1):
+            copy_own(u)
+            add_on_gpsimd(u)
+        relu_on_gpsimd(1)
+        cited_products(LAST, 3)
         cited_products(FIRST, 3, first=1)
+        stage(LAST, 6, 7)
         stage(FIRST, 6, 7)
+        relu_on_scalar(0)
         own_product(4)
         own_product(5)
         differences(6, 7)
+        absolute_values(6, 7)
 
         second_last, last = tiles_of(PAIRS - 1)
-        add_on_vector(3)
-        add_on_gpsimd(2)
         add_on_vector(4)
-        quantize_w4()
-        relu_on_vector(0, PAIR)
-        relu_on_scalar(1)
-        absolute_values(6, 7)
         add_on_vector(5)
+        quantize_w4()
         quantize_h(0, PAIR)
-        own_product(second_last)
-        own_product(last)
-        finish_pair(0)
-        quantize_h(PAIR, PAIR)
         relu_on_vector(2 * PAIR, PAIR)
+        own_product(second_last)
+        finish_pair(0)
+        own_product(last)
+        quantize_h(PAIR, PAIR)
+        quantize_h(2 * PAIR, PAIR)
         finish_pair(1)
         add_on_vector(second_last)
-        quantize_h(2 * PAIR, PAIR)
         finish_pair(2)
         add_on_vector(last)
         for u in tiles_of(PAIRS - 1):

@@ -20,6 +20,7 @@ ALU = mybir.AluOpType
 P = 128
 PACK = 4
 RUN = 8
+BLOCK = PACK * RUN
 PASSES = K // (P * PACK)
 QUADS = 4
 TILE = 128
@@ -68,9 +69,8 @@ def tile_list_citation_topic_scores_kernel(
         w3_planes = kept([P, PASSES, H // 4], I32, "w3_planes")
         w2_codes = kept([P, PASSES, H // 2], I32, "w2_codes")
         w3_codes = [kept([P, H], I32, "w3_codes%d" % a) for a in range(PASSES)]
-        w1_raw = {
-            (a, half): kept([P, PACK, H // 2], F32, "w1_raw%d%d" % (a, half)) for a in range(PASSES) for half in range(2)
-        }
+        w1_parts = [(0, 0, H // 2), (0, H // 2, H // 2), (1, 0, H)]
+        w1_raw = [kept([P, PACK, count], F32, "w1_raw%d" % k) for k, (a, first, count) in enumerate(w1_parts)]
         w1_bf16 = {
             (0, 0): kept([P, PACK * H], BF16, "w1_bf16_00"),
             (1, 0): kept([P, SHARE * H], BF16, "w1_bf16_10"),
@@ -115,9 +115,10 @@ def tile_list_citation_topic_scores_kernel(
                 rows = scales.bitcast(I32)[:, 4 * q : 4 * q + 4, :].rearrange("a r e -> r a e")
                 nc.sync.dma_start(out=planes[32 * q : 32 * q + 4, :, :], in_=rows)
 
-        def load_w1(a, half):
-            rows = w1[P * PACK * a : P * PACK * (a + 1), half * H // 2 : (half + 1) * H // 2]
-            nc.sync.dma_start(out=w1_raw[a, half][:], in_=rows.rearrange("(p j) r -> p j r", j=PACK))
+        def load_w1(part):
+            a, first, count = w1_parts[part]
+            rows = w1[P * PACK * a : P * PACK * (a + 1), first : first + count]
+            nc.sync.dma_start(out=w1_raw[part][:], in_=rows.rearrange("(p j) r -> p j r", j=PACK))
 
 
         def gather_scales(name, start, count):
@@ -134,9 +135,10 @@ def tile_list_citation_topic_scores_kernel(
             nc.vector.tensor_copy(rows[:], scale_rows[:].bitcast(U8).indirect(offsets[OWN][:, 0 : EARLY // 16]))
             return rows
 
-        def move_own_rows(rows, a):
-            for q in range(QUADS):
-                first = ROWS_AT + 16 * a + 4 * q
+        def move_own_rows(rows, runs):
+            for run in runs:
+                a, q = divmod(run, QUADS)
+                first = ROWS_AT + 4 * run
                 nc.sync.dma_start(
                     out=own_plane[32 * q + 4 * a : 32 * q + 4 * a + 4, :], in_=rows[first : first + 4, :].bitcast(I32)
                 )
@@ -172,17 +174,18 @@ def tile_list_citation_topic_scores_kernel(
         def round_on_gpsimd(dst, src):
             nc.gpsimd.tensor_scalar(out=dst, in0=src, scalar1=1.0, scalar2=0.0, op0=ALU.mult, op1=ALU.add)
 
-        def rounded(a, first, half):
-            blocks = w1_bf16[a, first][:].rearrange("p (t g c) -> p t g c", g=2 * RUN, c=RUN * PACK)
-            return blocks[:, :, half * RUN : (half + 1) * RUN, :]
+        def rounded(part, place):
+            a, first, count = w1_parts[part]
+            blocks = w1_bf16[a, place][:].rearrange("p (t g c) -> p t g c", g=H // BLOCK, c=BLOCK)
+            return blocks[:, :, first // BLOCK : (first + count) // BLOCK, :]
 
-        def round_w1_on_gpsimd(a, half, count):
-            src = w1_raw[a, half][:].rearrange("p j (g t i) -> p g t i j", t=PACK, i=RUN)[:, :, 0:count]
-            round_on_gpsimd(rounded(a, 0, half).rearrange("p t g (i j) -> p g t i j", j=PACK), src)
+        def round_w1_on_gpsimd(part, places):
+            src = w1_raw[part][:].rearrange("p j (g t i) -> p g t i j", t=PACK, i=RUN)[:, :, 0:places]
+            round_on_gpsimd(rounded(part, 0).rearrange("p t g (i j) -> p g t i j", j=PACK), src)
 
-        def round_w1_on_scalar(a, half, first):
-            src = w1_raw[a, half][:].rearrange("p j (g t u i) -> p t g u j i", t=PACK, u=2, i=4)
-            dst = rounded(a, first, half).rearrange("p t g (u i j) -> p t g u j i", u=2, j=PACK)
+        def round_w1_on_scalar(part, first):
+            src = w1_raw[part][:].rearrange("p j (g t u i) -> p t g u j i", t=PACK, u=2, i=4)
+            dst = rounded(part, first).rearrange("p t g (u i j) -> p t g u j i", u=2, j=PACK)
             for t in range(first, PACK):
                 nc.scalar.copy(out=dst[:, t - first], in_=src[:, t])
 
@@ -388,7 +391,7 @@ def tile_list_citation_topic_scores_kernel(
         load_words(w3_codes[1], w3_words[1])
         nc.sync.dma_start(out=w2_codes[:], in_=w2_words.rearrange("a p e -> p a e").bitcast(I32))
         load_weight_planes(w2_planes, w2_scales, range(QUADS))
-        load_w1(0, 0)
+        load_w1(0)
 
         own_rows = gather_own_rows()
         identity = kept([P, P], F32, "identity")
@@ -396,15 +399,10 @@ def tile_list_citation_topic_scores_kernel(
         gather_scales(LAST, 0, EARLY)
         gather_words(LAST, 0, 0)
         gather_words(LAST, 0, 1)
-        load_w1(0, 1)
         gather_first_scales(nc.sync, 0)
-        load_w1(1, 0)
-        move_own_rows(own_rows, 0)
-        load_w1(1, 1)
-        move_own_rows(own_rows, 1)
-        for t in range(PACK):
-            nc.sync.dma_start(out=w4_raw[:, t, :], in_=w4.rearrange("(g t i) n -> t g i n", t=PACK, i=RUN)[t])
-        nc.sync.dma_start(out=bias[:], in_=b.rearrange("(m e) -> m e", e=2))
+        load_w1(1)
+        load_w1(2)
+        move_own_rows(own_rows, range(6))
         gather_words(FIRST, 0, 0)
         gather_tile(LAST, 1, 0)
         gather_tile(LAST, 1, 1)
@@ -428,23 +426,26 @@ def tile_list_citation_topic_scores_kernel(
 
         gather_passes(LAST, 2)
         gather_first_scales(nc.sync, HALF)
+        move_own_rows(own_rows, range(6, 8))
+        for t in range(PACK):
+            nc.sync.dma_start(out=w4_raw[:, t, :], in_=w4.rearrange("(g t i) n -> t g i n", t=PACK, i=RUN)[t])
+        nc.sync.dma_start(out=bias[:], in_=b.rearrange("(m e) -> m e", e=2))
         gather_passes(FIRST, 2)
         gather_passes(OWN, 0)
-        for a in range(PASSES):
-            for half in range(2):
-                round_w1_on_gpsimd(a, half, SHARE if a else PACK)
+        round_w1_on_gpsimd(0, PACK)
+        round_w1_on_gpsimd(1, PACK)
+        round_w1_on_gpsimd(2, SHARE)
         cited_products(LAST, 2)
         differences(0, 1)
         stage(LAST, 4, 5)
         w1_bf16[1, SHARE] = scalar_tile([P, (PACK - SHARE) * H], BF16, "w1_bf16_rest")
-        round_w1_on_scalar(1, 1, SHARE)
-        round_w1_on_scalar(1, 0, SHARE)
+        round_w1_on_scalar(2, SHARE)
+        gather_scales(LAST, EARLY, S - EARLY)
         quantize_w1(0, 0)
         quantize_w1(1, SHARE)
         quantize_w1(1, 0)
         round_w4()
         gather_passes(OWN, 1)
-        gather_scales(LAST, EARLY, S - EARLY)
         gather_passes(LAST, 3)
         gather_passes(FIRST, 3)
         gather_passes(OWN, 2)
@@ -455,10 +456,10 @@ def tile_list_citation_topic_scores_kernel(
         absolute_values(0, 1)
         cited_products(FIRST, 2, first=1)
         absolute_values(2, 3)
-        own_product(0)
         own_product(1)
+        own_product(0)
         stage(FIRST, 4, 5)
-        for u in tiles_of(0):
+        for u in (1, 0):
             copy_own(u)
             add_on_gpsimd(u)
         differences(4, 5)
@@ -468,7 +469,6 @@ def tile_list_citation_topic_scores_kernel(
         for u in tiles_of(1):
             copy_own(u)
             add_on_gpsimd(u)
-        relu_on_gpsimd(1)
         cited_products(LAST, 3)
         cited_products(FIRST, 3, first=1)
         stage(LAST, 6, 7)
@@ -483,6 +483,7 @@ def tile_list_citation_topic_scores_kernel(
         add_on_vector(4)
         add_on_vector(5)
         quantize_w4()
+        relu_on_vector(PAIR, PAIR)
         quantize_h(0, PAIR)
         relu_on_vector(2 * PAIR, PAIR)
         own_product(second_last)

@@ -30,6 +30,7 @@ PAIRS = S // PAIR
 HALF = S // 2
 EARLY = 3 * PAIR
 SHARE = 3
+GPSIMD_SUMS = 4
 OWN, FIRST, LAST = "own", "first", "last"
 
 ROWS_AT = P - 32
@@ -59,6 +60,9 @@ def tile_list_citation_topic_scores_kernel(
         def scalar_tile(shape, dtype, name):
             return made.tile(shape, dtype, name=name, tag="scalar", bufs=SCALAR_TILES, align_bytes=64)
 
+        def gpsimd_tile(shape, dtype, name):
+            return made.tile(shape, dtype, name=name, tag="gpsimd", bufs=2, align_bytes=64)
+
         def next_bank(shape, name):
             return psum.tile(shape, F32, name=name, tag="bank")
 
@@ -69,11 +73,11 @@ def tile_list_citation_topic_scores_kernel(
         w3_planes = kept([P, PASSES, H // 4], I32, "w3_planes")
         w2_codes = kept([P, PASSES, H // 2], I32, "w2_codes")
         w3_codes = [kept([P, H], I32, "w3_codes%d" % a) for a in range(PASSES)]
-        w1_parts = [(0, 0, H // 2), (0, H // 2, H // 2), (1, 0, H)]
+        w1_parts = [(a, first, H // 2) for a in range(PASSES) for first in (0, H // 2)]
         w1_raw = [kept([P, PACK, count], F32, "w1_raw%d" % k) for k, (a, first, count) in enumerate(w1_parts)]
         w1_bf16 = {
-            (0, 0): kept([P, PACK * H], BF16, "w1_bf16_00"),
-            (1, 0): kept([P, SHARE * H], BF16, "w1_bf16_10"),
+            (0, 0): gpsimd_tile([P, PACK * H], BF16, "w1_bf16_00"),
+            (1, 0): gpsimd_tile([P, SHARE * H], BF16, "w1_bf16_10"),
         }
         w1_scales = kept([P, PASSES, H], U8, "w1_scales")
         w4_raw = kept([P, PACK, N], F32, "w4_raw")
@@ -200,7 +204,7 @@ def tile_list_citation_topic_scores_kernel(
                 w1_codes[a, first + k] = codes[:, k * P : (k + 1) * P]
 
         def round_w4():
-            w4_tiles["bf16"] = kept([P, PACK * N], BF16, "w4_bf16", tag="w1_bf16_10")
+            w4_tiles["bf16"] = gpsimd_tile([P, PACK * N], BF16, "w4_bf16")
             round_on_gpsimd(
                 w4_tiles["bf16"][:].rearrange("p (e m t) -> p e m t", e=2, t=PACK),
                 w4_raw[:].rearrange("p t (m e) -> p e m t", e=2),
@@ -288,6 +292,18 @@ def tile_list_citation_topic_scores_kernel(
                         start=(a == 0), stop=(a == PASSES - 1),
                     )
 
+        def own_pass(u, a):
+            places, start, count = share(u)
+            if a:
+                own_bank[u] = next_bank([P, len(places), count], "own_bank")
+            for k, t in enumerate(places):
+                nc.tensor.matmul_mx(
+                    out=own_bank[u][:, k, :], lhsT=w1_codes[a, t].bitcast(FP8X4),
+                    lhsT_scale=w1_scales[:, a, t * P : (t + 1) * P], rhs=pair_words[OWN, a, u // 2].bitcast(FP8X4),
+                    rhs_scale=own_plane[:].bitcast(U8)[4 * a :, start : start + count],
+                    start=(a == 1 and k == 0), stop=(a == 0 and k == len(places) - 1),
+                )
+
         def sum_of(u):
             return h_sum[u // 2][:, u % 2].rearrange("p (n t) -> p n t", t=len(share(u)[0]))
 
@@ -297,17 +313,20 @@ def tile_list_citation_topic_scores_kernel(
             own_copy[u] = own
 
         def add_on_gpsimd(u):
-            if u // 2 not in h_sum:
-                h_sum[u // 2] = kept([P, 2, H], BF16, "h_sum_early%d" % (u // 2))
+            if not h_sum:
+                sums = gpsimd_tile([P, 2, 2, H], BF16, "h_sum_early")
+                h_sum[0] = sums[:, 0]
+                if GPSIMD_SUMS == 4:
+                    h_sum[1] = sums[:, 1]
             nc.gpsimd.tensor_tensor(out=sum_of(u), in0=own_copy[u][:], in1=distance[u][:], op=ALU.add)
 
         def add_on_vector(u):
             if u // 2 not in h_sum:
-                h_sum[u // 2] = vector_tile([P, 2, H], BF16, "h_sum")
+                h_sum[u // 2] = vector_tile([P, 2, H], BF16, "h_sum")[:]
             nc.vector.tensor_tensor(out=sum_of(u), in0=by_token(own_bank[u]), in1=distance[u][:], op=ALU.add)
 
         def woven(pair):
-            return h_sum[pair][:].rearrange("p u (n t) -> p n u t", t=2)
+            return h_sum[pair].rearrange("p u (n t) -> p n u t", t=2)
 
         def relu_on_scalar(pair):
             h_bf16[pair * PAIR] = scalar_tile([P, PACK * PAIR], BF16, "h_relu")
@@ -402,7 +421,8 @@ def tile_list_citation_topic_scores_kernel(
         gather_first_scales(nc.sync, 0)
         load_w1(1)
         load_w1(2)
-        move_own_rows(own_rows, range(6))
+        load_w1(3)
+        move_own_rows(own_rows, range(5))
         gather_words(FIRST, 0, 0)
         gather_tile(LAST, 1, 0)
         gather_tile(LAST, 1, 1)
@@ -426,7 +446,7 @@ def tile_list_citation_topic_scores_kernel(
 
         gather_passes(LAST, 2)
         gather_first_scales(nc.sync, HALF)
-        move_own_rows(own_rows, range(6, 8))
+        move_own_rows(own_rows, range(5, 8))
         for t in range(PACK):
             nc.sync.dma_start(out=w4_raw[:, t, :], in_=w4.rearrange("(g t i) n -> t g i n", t=PACK, i=RUN)[t])
         nc.sync.dma_start(out=bias[:], in_=b.rearrange("(m e) -> m e", e=2))
@@ -435,15 +455,17 @@ def tile_list_citation_topic_scores_kernel(
         round_w1_on_gpsimd(0, PACK)
         round_w1_on_gpsimd(1, PACK)
         round_w1_on_gpsimd(2, SHARE)
+        round_w1_on_gpsimd(3, SHARE)
         cited_products(LAST, 2)
         differences(0, 1)
         stage(LAST, 4, 5)
         w1_bf16[1, SHARE] = scalar_tile([P, (PACK - SHARE) * H], BF16, "w1_bf16_rest")
+        round_w1_on_scalar(3, SHARE)
         round_w1_on_scalar(2, SHARE)
         gather_scales(LAST, EARLY, S - EARLY)
-        quantize_w1(0, 0)
         quantize_w1(1, SHARE)
         quantize_w1(1, 0)
+        quantize_w1(0, 0)
         round_w4()
         gather_passes(OWN, 1)
         gather_passes(LAST, 3)
@@ -456,10 +478,11 @@ def tile_list_citation_topic_scores_kernel(
         absolute_values(0, 1)
         cited_products(FIRST, 2, first=1)
         absolute_values(2, 3)
-        own_product(1)
-        own_product(0)
+        for a in (1, 0):
+            for u in tiles_of(0):
+                own_pass(u, a)
         stage(FIRST, 4, 5)
-        for u in (1, 0):
+        for u in tiles_of(0):
             copy_own(u)
             add_on_gpsimd(u)
         differences(4, 5)

@@ -31,6 +31,7 @@ HALF = S // 2
 EARLY = 3 * PAIR
 SHARE = 3
 GPSIMD_SUMS = 4
+WOVEN = 1
 OWN, FIRST, LAST = "own", "first", "last"
 
 ROWS_AT = P - 32
@@ -253,7 +254,7 @@ def tile_list_citation_topic_scores_kernel(
             nc.gpsimd.tensor_tensor(out=subtracted[u][:], in0=staged[FIRST, u][:], in1=staged[LAST, u][:], op=ALU.add)
 
         def share(u):
-            if u // 2 == PAIRS - 1:
+            if u // 2 >= WOVEN:
                 return range(PACK), u * TILE, TILE
             return range(2 * (u % 2), 2 * (u % 2) + 2), u // 2 * PAIR, PAIR
 
@@ -343,8 +344,10 @@ def tile_list_citation_topic_scores_kernel(
 
         def relu_on_vector(start, count):
             h_bf16[start] = vector_tile([P, PACK * count], BF16, "h_bf16")
-            if count == PAIR:
+            if start // PAIR < WOVEN:
                 result, sums = h_bf16[start][:].rearrange("p (n u t) -> p n u t", u=2, t=2), woven(start // PAIR)
+            elif count == PAIR:
+                result, sums = h_bf16[start][:], h_sum[start // PAIR].rearrange("p u c -> p (u c)")
             else:
                 result, sums = h_bf16[start][:], h_sum[start // PAIR][:, start // TILE % 2]
             nc.vector.tensor_scalar(out=result, in0=sums, scalar1=0.0, scalar2=None, op0=ALU.max)
@@ -416,8 +419,7 @@ def tile_list_citation_topic_scores_kernel(
         identity = kept([P, P], F32, "identity")
         make_identity(nc, identity[:])
         gather_scales(LAST, 0, EARLY)
-        gather_words(LAST, 0, 0)
-        gather_words(LAST, 0, 1)
+        gather_words(LAST, 0, 0, pairs=2)
         gather_first_scales(nc.sync, 0)
         load_w1(1)
         load_w1(2)
@@ -428,8 +430,7 @@ def tile_list_citation_topic_scores_kernel(
         gather_tile(LAST, 1, 1)
         gather_words(LAST, 1, 1)
         gather_words(FIRST, 0, 1)
-        gather_words(FIRST, 1, 0)
-        gather_words(FIRST, 1, 1)
+        gather_words(FIRST, 1, 0, pairs=2)
         for a in range(PASSES):
             for u in tiles_of(0) + tiles_of(1):
                 cited_pass(LAST, u, a)

@@ -31,7 +31,7 @@ HALF = S // 2
 EARLY = 3 * PAIR
 SHARE = 3
 GPSIMD_SUMS = 4
-WOVEN = 1
+WOVEN = 0
 OWN, FIRST, LAST = "own", "first", "last"
 
 ROWS_AT = P - 32
@@ -53,21 +53,21 @@ def tile_list_citation_topic_scores_kernel(
         psum = ctx.enter_context(tc.psum_pool(name="psum", bufs=BANKS))
 
         def kept(shape, dtype, name, tag=None):
-            return keep.tile(shape, dtype, name=name, tag=tag or name, align_bytes=64)
+            return keep.tile(shape, dtype, name=name, tag=tag or name, align_bytes=256)
 
         def vector_tile(shape, dtype, name):
-            return made.tile(shape, dtype, name=name, tag="vector", bufs=VECTOR_TILES, align_bytes=64)
+            return made.tile(shape, dtype, name=name, tag="vector", bufs=VECTOR_TILES, align_bytes=256)
 
         def scalar_tile(shape, dtype, name):
-            return made.tile(shape, dtype, name=name, tag="scalar", bufs=SCALAR_TILES, align_bytes=64)
+            return made.tile(shape, dtype, name=name, tag="scalar", bufs=SCALAR_TILES, align_bytes=256)
 
         def gpsimd_tile(shape, dtype, name):
-            return made.tile(shape, dtype, name=name, tag="gpsimd", bufs=2, align_bytes=64)
+            return made.tile(shape, dtype, name=name, tag="gpsimd", bufs=2, align_bytes=256)
 
         def next_bank(shape, name):
             return psum.tile(shape, F32, name=name, tag="bank")
 
-        offsets = {name: lists.tile([P, S // 16], U16, name="offsets_" + name) for name in (OWN, FIRST, LAST)}
+        offsets = {name: lists.tile([P, S // 16], U16, name="offsets_" + name, align_bytes=256) for name in (OWN, FIRST, LAST)}
         table_words = [kept([P, T], I32, "table_words%d" % a) for a in range(PASSES)]
         table_scales = kept([P, T // 4], I32, "table_scales")
         w2_planes = kept([P, PASSES, H // 4], I32, "w2_planes")
@@ -300,7 +300,7 @@ def tile_list_citation_topic_scores_kernel(
             for k, t in enumerate(places):
                 nc.tensor.matmul_mx(
                     out=own_bank[u][:, k, :], lhsT=w1_codes[a, t].bitcast(FP8X4),
-                    lhsT_scale=w1_scales[:, a, t * P : (t + 1) * P], rhs=pair_words[OWN, a, u // 2].bitcast(FP8X4),
+                    lhsT_scale=w1_scales[:, a, t * P : (t + 1) * P], rhs=picked_words[OWN, a, u].bitcast(FP8X4),
                     rhs_scale=own_plane[:].bitcast(U8)[4 * a :, start : start + count],
                     start=(a == 1 and k == 0), stop=(a == 0 and k == len(places) - 1),
                 )
@@ -332,7 +332,7 @@ def tile_list_citation_topic_scores_kernel(
         def relu_on_scalar(pair):
             h_bf16[pair * PAIR] = scalar_tile([P, PACK * PAIR], BF16, "h_relu")
             nc.scalar.activation(
-                out=h_bf16[pair * PAIR][:].rearrange("p (n u t) -> p n u t", u=2, t=2), in_=woven(pair), func=ACT.Relu
+                out=h_bf16[pair * PAIR][:], in_=h_sum[pair].rearrange("p u c -> p (u c)"), func=ACT.Relu
             )
 
         def relu_on_gpsimd(pair):
@@ -426,8 +426,7 @@ def tile_list_citation_topic_scores_kernel(
         load_w1(3)
         move_own_rows(own_rows, range(5))
         gather_words(FIRST, 0, 0)
-        gather_tile(LAST, 1, 0)
-        gather_tile(LAST, 1, 1)
+        gather_words(LAST, 1, 0)
         gather_words(LAST, 1, 1)
         gather_words(FIRST, 0, 1)
         gather_words(FIRST, 1, 0, pairs=2)

@@ -31,7 +31,7 @@ HALF = S // 2
 EARLY = 3 * PAIR
 SHARE = 3
 GPSIMD_SUMS = 4
-WOVEN = 0
+WOVEN = 2
 OWN, FIRST, LAST = "own", "first", "last"
 
 ROWS_AT = P - 32
@@ -300,13 +300,15 @@ def tile_list_citation_topic_scores_kernel(
             for k, t in enumerate(places):
                 nc.tensor.matmul_mx(
                     out=own_bank[u][:, k, :], lhsT=w1_codes[a, t].bitcast(FP8X4),
-                    lhsT_scale=w1_scales[:, a, t * P : (t + 1) * P], rhs=picked_words[OWN, a, u].bitcast(FP8X4),
+                    lhsT_scale=w1_scales[:, a, t * P : (t + 1) * P], rhs=pair_words[OWN, a, u // 2].bitcast(FP8X4),
                     rhs_scale=own_plane[:].bitcast(U8)[4 * a :, start : start + count],
                     start=(a == 1 and k == 0), stop=(a == 0 and k == len(places) - 1),
                 )
 
         def sum_of(u):
-            return h_sum[u // 2][:, u % 2].rearrange("p (n t) -> p n t", t=len(share(u)[0]))
+            if u // 2 < WOVEN:
+                return h_sum[u // 2].rearrange("p u (n v t) -> p (u n) v t", v=2, t=2)[:, :, u % 2, :]
+            return h_sum[u // 2][:, u % 2].rearrange("p (n t) -> p n t", t=PACK)
 
         def copy_own(u):
             own = scalar_tile(list(distance[u].shape), F32, "own")
@@ -344,9 +346,7 @@ def tile_list_citation_topic_scores_kernel(
 
         def relu_on_vector(start, count):
             h_bf16[start] = vector_tile([P, PACK * count], BF16, "h_bf16")
-            if start // PAIR < WOVEN:
-                result, sums = h_bf16[start][:].rearrange("p (n u t) -> p n u t", u=2, t=2), woven(start // PAIR)
-            elif count == PAIR:
+            if count == PAIR:
                 result, sums = h_bf16[start][:], h_sum[start // PAIR].rearrange("p u c -> p (u c)")
             else:
                 result, sums = h_bf16[start][:], h_sum[start // PAIR][:, start // TILE % 2]

from contextlib import ExitStack

import concourse.mybir as mybir
from concourse.masks import make_identity

K, H, N, T, S = 1024, 512, 256, 2048, 1024
FLOPS = 2 * S * H * (3 * K + N)

F32 = mybir.dt.float32
BF16 = mybir.dt.bfloat16
I32 = mybir.dt.int32
U32 = mybir.dt.uint32
U16 = mybir.dt.uint16
U8 = mybir.dt.uint8
FP8X4 = mybir.dt.float8_e4m3fn_x4
FP4X4 = mybir.dt.float4_e2m1fn_x4
ACT = mybir.ActivationFunctionType
ALU = mybir.AluOpType

P = 128
PACK = 4
RUN = 8
BLOCK = PACK * RUN
PASSES = K // (P * PACK)
QUADS = 4
TILE = 128
TILES = S // TILE
PAIR = 2 * TILE
PAIRS = S // PAIR
HALF = S // 2
EARLY = 3 * PAIR
SHARE = 3
GPSIMD_SUMS = 4
WOVEN = 2
OWN, FIRST, LAST = "own", "first", "last"

ROWS_AT = P - 32
MOVED_ROWS = 32 * (QUADS - 1) + 4

BANKS = 8
VECTOR_TILES = 50
SCALAR_TILES = 35


def tile_list_citation_topic_scores_kernel(
    tc, tab_words, tab_scales, offs, offs2, offs3, w1, w2_words, w2_scales, w3_words, w3_scales, w4, b, out
):
    nc = tc.nc
    with ExitStack() as ctx:
        lists = ctx.enter_context(tc.tile_pool(name="lists", bufs=1))
        keep = ctx.enter_context(tc.tile_pool(name="keep", bufs=1))
        made = ctx.enter_context(tc.tile_pool(name="made", bufs=1))
        psum = ctx.enter_context(tc.psum_pool(name="psum", bufs=BANKS))

        def kept(shape, dtype, name, tag=None):
            return keep.tile(shape, dtype, name=name, tag=tag or name, align_bytes=256)

        def vector_tile(shape, dtype, name):
            return made.tile(shape, dtype, name=name, tag="vector", bufs=VECTOR_TILES, align_bytes=256)

        def scalar_tile(shape, dtype, name):
            return made.tile(shape, dtype, name=name, tag="scalar", bufs=SCALAR_TILES, align_bytes=256)

        def gpsimd_tile(shape, dtype, name):
            return made.tile(shape, dtype, name=name, tag="gpsimd", bufs=2, align_bytes=256)

        def next_bank(shape, name):
            return psum.tile(shape, F32, name=name, tag="bank")

        offsets = {name: lists.tile([P, S // 16], U16, name="offsets_" + name, align_bytes=256) for name in (OWN, FIRST, LAST)}
        table_words = [kept([P, T], I32, "table_words%d" % a) for a in range(PASSES)]
        table_scales = kept([P, T // 4], I32, "table_scales")
        w2_planes = kept([P, PASSES, H // 4], I32, "w2_planes")
        w3_planes = kept([P, PASSES, H // 4], I32, "w3_planes")
        w2_codes = kept([P, PASSES, H // 2], I32, "w2_codes")
        w3_codes = [kept([P, H], I32, "w3_codes%d" % a) for a in range(PASSES)]
        w1_parts = [(a, first, H // 2) for a in range(PASSES) for first in (0, H // 2)]
        w1_raw = [kept([P, PACK, count], F32, "w1_raw%d" % k) for k, (a, first, count) in enumerate(w1_parts)]
        w1_bf16 = {
            (0, 0): gpsimd_tile([P, PACK * H], BF16, "w1_bf16_00"),
            (1, 0): gpsimd_tile([P, SHARE * H], BF16, "w1_bf16_10"),
        }
        w1_scales = kept([P, PASSES, H], U8, "w1_scales")
        w4_raw = kept([P, PACK, N], F32, "w4_raw")
        w4_scales = kept([P, N], U8, "w4_scales")
        h_scales = kept([P, S], U8, "h_scales")
        first_scales_pass1 = kept([P, S // 4], I32, "first_scales_pass1")
        scale_rows = kept([P, T // 4], I32, "scale_rows")
        own_plane = kept([P, EARLY // 4], I32, "own_plane")
        bias = kept([P, 2], F32, "bias")
        picked_words = {}
        picked_scales = {}
        scale_planes = {}
        pair_words = {}
        staged = {}
        subtracted = {}
        distance = {}
        cited_bank = {}
        diff_bank = {}
        own_copy = {}
        own_bank = {}
        h_sum = {}
        h_bf16, h_codes = {}, {}
        w1_codes = {}
        w4_tiles = {}

        def tiles_of(pair):
            return (2 * pair, 2 * pair + 1)


        def load_words(tile, words):
            nc.sync.dma_start(out=tile[:], in_=words.rearrange("p n i -> p (n i)").bitcast(I32))

        def load_table_planes(queue, q):
            rows = tab_scales.bitcast(I32)[:, 4 * q : 4 * q + 4, :]
            queue.dma_start(out=table_scales[32 * q : 32 * q + 8, :], in_=rows)

        def load_weight_planes(planes, scales, quadrants):
            for q in quadrants:
                rows = scales.bitcast(I32)[:, 4 * q : 4 * q + 4, :].rearrange("a r e -> r a e")
                nc.sync.dma_start(out=planes[32 * q : 32 * q + 4, :, :], in_=rows)

        def load_w1(part):
            a, first, count = w1_parts[part]
            rows = w1[P * PACK * a : P * PACK * (a + 1), first : first + count]
            nc.sync.dma_start(out=w1_raw[part][:], in_=rows.rearrange("(p j) r -> p j r", j=PACK))


        def gather_scales(name, start, count):
            plane = vector_tile([P, count], U8, "scales_" + name)
            window = table_scales[:].bitcast(U8)
            nc.vector.tensor_copy(plane[:], window.indirect(offsets[name][:, start // 16 : (start + count) // 16]))
            for k in range(count // TILE):
                picked_scales[name, start // TILE + k] = plane[:, k * TILE : (k + 1) * TILE]
            scale_planes[name, start] = plane
            return plane

        def gather_own_rows():
            rows = vector_tile([P, EARLY], U8, "own_rows")
            nc.vector.tensor_copy(rows[:], scale_rows[:].bitcast(U8).indirect(offsets[OWN][:, 0 : EARLY // 16]))
            return rows

        def move_own_rows(rows, runs):
            for run in runs:
                a, q = divmod(run, QUADS)
                first = ROWS_AT + 4 * run
                nc.sync.dma_start(
                    out=own_plane[32 * q + 4 * a : 32 * q + 4 * a + 4, :], in_=rows[first : first + 4, :].bitcast(I32)
                )

        def gather_first_scales(queue, start):
            plane = gather_scales(FIRST, start, HALF)
            queue.dma_start(
                out=first_scales_pass1[0:MOVED_ROWS, start // 4 : (start + HALF) // 4],
                in_=plane[4 : 4 + MOVED_ROWS, :].bitcast(I32),
            )

        def gather_tile(name, a, u):
            words = vector_tile([P, TILE], U32, "words_%s%d" % (name, a))
            columns = slice(u * TILE // 16, (u + 1) * TILE // 16)
            nc.vector.tensor_copy(words[:], table_words[a][:].bitcast(U32).indirect(offsets[name][:, columns]))
            picked_words[name, a, u] = words[:]

        def gather_words(name, a, pair, pairs=1):
            words = vector_tile([P, pairs * PAIR], U32, "words_%s%d" % (name, a))
            window = table_words[a][:].bitcast(U32)
            columns = slice(pair * PAIR // 16, (pair + pairs) * PAIR // 16)
            nc.vector.tensor_copy(words[:], window.indirect(offsets[name][:, columns]))
            for k in range(2 * pairs):
                picked_words[name, a, 2 * pair + k] = words[:, k * TILE : (k + 1) * TILE]
            for k in range(pairs):
                pair_words[name, a, pair + k] = words[:, k * PAIR : (k + 1) * PAIR]

        def gather_passes(name, pair, pairs=1):
            for a in range(PASSES):
                gather_words(name, a, pair, pairs)


        def round_on_gpsimd(dst, src):
            nc.gpsimd.tensor_scalar(out=dst, in0=src, scalar1=1.0, scalar2=0.0, op0=ALU.mult, op1=ALU.add)

        def rounded(part, place):
            a, first, count = w1_parts[part]
            blocks = w1_bf16[a, place][:].rearrange("p (t g c) -> p t g c", g=H // BLOCK, c=BLOCK)
            return blocks[:, :, first // BLOCK : (first + count) // BLOCK, :]

        def round_w1_on_gpsimd(part, places):
            src = w1_raw[part][:].rearrange("p j (g t i) -> p g t i j", t=PACK, i=RUN)[:, :, 0:places]
            round_on_gpsimd(rounded(part, 0).rearrange("p t g (i j) -> p g t i j", j=PACK), src)

        def round_w1_on_scalar(part, first):
            src = w1_raw[part][:].rearrange("p j (g t u i) -> p t g u j i", t=PACK, u=2, i=4)
            dst = rounded(part, first).rearrange("p t g (u i j) -> p t g u j i", u=2, j=PACK)
            for t in range(first, PACK):
                nc.scalar.copy(out=dst[:, t - first], in_=src[:, t])

        def quantize_w1(a, first):
            count = w1_bf16[a, first].shape[1] // H
            codes = vector_tile([P, count * P], U32, "w1_codes")
            nc.vector.quantize_mx(
                out=codes[:].bitcast(FP8X4), scales=w1_scales[:, a, first * P : (first + count) * P],
                in_=w1_bf16[a, first][:],
            )
            for k in range(count):
                w1_codes[a, first + k] = codes[:, k * P : (k + 1) * P]

        def round_w4():
            w4_tiles["bf16"] = gpsimd_tile([P, PACK * N], BF16, "w4_bf16")
            round_on_gpsimd(
                w4_tiles["bf16"][:].rearrange("p (e m t) -> p e m t", e=2, t=PACK),
                w4_raw[:].rearrange("p t (m e) -> p e m t", e=2),
            )

        def quantize_w4():
            w4_tiles["codes"] = vector_tile([P, N], U32, "w4_codes")
            nc.vector.quantize_mx(
                out=w4_tiles["codes"][:].bitcast(FP8X4), scales=w4_scales[:], in_=w4_tiles["bf16"][:]
            )


        def by_token(bank):
            return bank[:].rearrange("p t n -> p n t")

        def cited_pass(name, u, a, first=0):
            if a == first:
                cited_bank[name, u] = next_bank([P, H], "cited_bank")
            if name == LAST:
                weight, weight_plane = w3_codes[a][:].bitcast(FP8X4), w3_planes[:].bitcast(U8)[:, a, :]
                token_plane = picked_scales[LAST, u][4 * a :, :]
            else:
                weight, weight_plane = w2_codes[:, a, :].bitcast(U8).bitcast(FP4X4), w2_planes[:].bitcast(U8)[:, a, :]
                moved_plane = first_scales_pass1[:].bitcast(U8)[:, u * TILE : (u + 1) * TILE]
                token_plane = moved_plane if a else picked_scales[FIRST, u]
            nc.tensor.matmul_mx(
                out=cited_bank[name, u][:], lhsT=picked_words[name, a, u].bitcast(FP8X4), lhsT_scale=token_plane,
                rhs=weight, rhs_scale=weight_plane, start=(a == first), stop=(a != first),
            )

        def cited_products(name, pair, first=0):
            for u in tiles_of(pair):
                for a in (first, 1 - first):
                    cited_pass(name, u, a, first)

        def stage(name, *tiles):
            for u in tiles:
                staged[name, u] = scalar_tile([P, PACK, H // (PACK * RUN), RUN], F32, "staged_" + name)
                sums = cited_bank[name, u][:].rearrange("p (g t i) -> p t g i", t=PACK, i=RUN)
                nc.scalar.activation(
                    out=staged[name, u][:], in_=sums, func=ACT.Copy, scale=-1.0 if name == LAST else 1.0
                )

        def subtract_on_gpsimd(u):
            subtracted[u] = kept([P, PACK, H // (PACK * RUN), RUN], F32, "subtracted%d" % u)
            nc.gpsimd.tensor_tensor(out=subtracted[u][:], in0=staged[FIRST, u][:], in1=staged[LAST, u][:], op=ALU.add)

        def share(u):
            if u // 2 >= WOVEN:
                return range(PACK), u * TILE, TILE
            return range(2 * (u % 2), 2 * (u % 2) + 2), u // 2 * PAIR, PAIR

        def differences(*banks):
            for u in banks:
                places, start, count = share(u)
                bank = next_bank([P, len(places), count], "diff_bank")
                for k, t in enumerate(places):
                    for first in range(0, count, TILE):
                        tile = (start + first) // TILE
                        terms = [subtracted[tile]] if tile in subtracted else [staged[FIRST, tile], staged[LAST, tile]]
                        for n, term in enumerate(terms):
                            nc.tensor.matmul(
                                out=bank[:, k, first : first + TILE], lhsT=term[:, t].rearrange("p g i -> p (g i)"),
                                rhs=identity[:], start=(n == 0), stop=(n == len(terms) - 1), is_transpose=True,
                            )
                diff_bank[u] = bank

        def absolute_values(*banks):
            for u in banks:
                places, start, count = share(u)
                distance[u] = scalar_tile([P, count, len(places)], F32, "distance")
                nc.scalar.activation(out=distance[u][:], in_=by_token(diff_bank[u]), func=ACT.Abs)

        def own_product(u):
            places, start, count = share(u)
            own_bank[u] = next_bank([P, len(places), count], "own_bank")
            plane = own_plane[:].bitcast(U8) if start < EARLY else scale_planes[OWN, EARLY][:]
            for k, t in enumerate(places):
                for a in range(PASSES):
                    words = pair_words[OWN, a, u // 2][:, start % PAIR : start % PAIR + count]
                    nc.tensor.matmul_mx(
                        out=own_bank[u][:, k, :], lhsT=w1_codes[a, t].bitcast(FP8X4),
                        lhsT_scale=w1_scales[:, a, t * P : (t + 1) * P], rhs=words.bitcast(FP8X4),
                        rhs_scale=plane[4 * a :, start % EARLY : start % EARLY + count],
                        start=(a == 0), stop=(a == PASSES - 1),
                    )

        def own_pass(u, a):
            places, start, count = share(u)
            if a:
                own_bank[u] = next_bank([P, len(places), count], "own_bank")
            for k, t in enumerate(places):
                nc.tensor.matmul_mx(
                    out=own_bank[u][:, k, :], lhsT=w1_codes[a, t].bitcast(FP8X4),
                    lhsT_scale=w1_scales[:, a, t * P : (t + 1) * P], rhs=pair_words[OWN, a, u // 2].bitcast(FP8X4),
                    rhs_scale=own_plane[:].bitcast(U8)[4 * a :, start : start + count],
                    start=(a == 1 and k == 0), stop=(a == 0 and k == len(places) - 1),
                )

        def sum_of(u):
            if u // 2 < WOVEN:
                return h_sum[u // 2].rearrange("p u (n v t) -> p (u n) v t", v=2, t=2)[:, :, u % 2, :]
            return h_sum[u // 2][:, u % 2].rearrange("p (n t) -> p n t", t=PACK)

        def copy_own(u):
            own = scalar_tile(list(distance[u].shape), F32, "own")
            nc.scalar.activation(out=own[:], in_=by_token(own_bank[u]), func=ACT.Copy)
            own_copy[u] = own

        def add_on_gpsimd(u):
            if not h_sum:
                sums = gpsimd_tile([P, 2, 2, H], BF16, "h_sum_early")
                h_sum[0] = sums[:, 0]
                if GPSIMD_SUMS == 4:
                    h_sum[1] = sums[:, 1]
            nc.gpsimd.tensor_tensor(out=sum_of(u), in0=own_copy[u][:], in1=distance[u][:], op=ALU.add)

        def add_on_vector(u):
            if u // 2 not in h_sum:
                h_sum[u // 2] = vector_tile([P, 2, H], BF16, "h_sum")[:]
            nc.vector.tensor_tensor(out=sum_of(u), in0=by_token(own_bank[u]), in1=distance[u][:], op=ALU.add)

        def woven(pair):
            return h_sum[pair].rearrange("p u (n t) -> p n u t", t=2)

        def relu_on_scalar(pair):
            h_bf16[pair * PAIR] = scalar_tile([P, PACK * PAIR], BF16, "h_relu")
            nc.scalar.activation(
                out=h_bf16[pair * PAIR][:], in_=h_sum[pair].rearrange("p u c -> p (u c)"), func=ACT.Relu
            )

        def relu_on_gpsimd(pair):
            h_bf16[pair * PAIR] = kept([P, PACK * PAIR], BF16, "h_relu%d" % pair)
            nc.gpsimd.tensor_scalar(
                out=h_bf16[pair * PAIR][:].rearrange("p (n u t) -> p n u t", u=2, t=2), in0=woven(pair),
                scalar1=float("inf"), scalar2=0.0, op0=ALU.min, op1=ALU.max,
            )

        def relu_on_vector(start, count):
            h_bf16[start] = vector_tile([P, PACK * count], BF16, "h_bf16")
            if count == PAIR:
                result, sums = h_bf16[start][:], h_sum[start // PAIR].rearrange("p u c -> p (u c)")
            else:
                result, sums = h_bf16[start][:], h_sum[start // PAIR][:, start // TILE % 2]
            nc.vector.tensor_scalar(out=result, in0=sums, scalar1=0.0, scalar2=None, op0=ALU.max)

        def quantize_h(start, count):
            h_codes[start] = vector_tile([P, count], U32, "h_codes")
            nc.vector.quantize_mx(
                out=h_codes[start][:].bitcast(FP8X4), scales=h_scales[:, start : start + count], in_=h_bf16[start][:]
            )

        def score_product(sums, e, start, count):
            classes = slice(e * P, (e + 1) * P)
            nc.tensor.matmul_mx(
                out=sums, lhsT=w4_tiles["codes"][:, classes].bitcast(FP8X4), lhsT_scale=w4_scales[:, classes],
                rhs=h_codes[start][:].bitcast(FP8X4), rhs_scale=h_scales[:, start : start + count],
                start=True, stop=True,
            )

        def add_bias_on_scalar(result, sums, e):
            nc.scalar.activation(out=result, in_=sums, func=ACT.Identity, bias=bias[:, e : e + 1])

        def add_bias_on_vector(result, sums, e):
            nc.vector.tensor_scalar(out=result, in0=sums, scalar1=bias[:, e : e + 1], scalar2=None, op0=ALU.add)

        def store(start, count, result):
            nc.sync.dma_start(out=out.rearrange("(m e) s -> m e s", e=2)[:, :, start : start + count], in_=result[:])

        def finish_pair(pair):
            bank = next_bank([P, 2, PAIR], "score_bank")
            for e in range(2):
                score_product(bank[:, e, :], e, pair * PAIR, PAIR)
            result = scalar_tile([P, 2, PAIR], F32, "result")
            for e in range(2):
                add_bias_on_scalar(result[:, e, :], bank[:, e, :], e)
            store(pair * PAIR, PAIR, result)

        def finish_tile(u, second_adder):
            result = scalar_tile([P, 2, TILE], F32, "result")
            for e, adder in enumerate((add_bias_on_scalar, second_adder)):
                bank = next_bank([P, TILE], "score_bank")
                score_product(bank[:], e, u * TILE, TILE)
                adder(result[:, e, :], bank[:], e)
            store(u * TILE, TILE, result)


        nc.gpsimd.memset(table_scales[:], 0)
        nc.vector.memset(w3_planes[:], 0)
        nc.vector.memset(scale_rows[0:ROWS_AT, :], 0)
        nc.vector.memset(w2_planes[:], 0)
        nc.vector.memset(first_scales_pass1[:], 0)
        nc.vector.memset(own_plane[:], 0)

        nc.sync.dma_start(out=scale_rows[ROWS_AT:P, :], in_=tab_scales.rearrange("a q t -> (a q) t").bitcast(I32))
        nc.sync.dma_start(offsets[OWN][:], offs)
        nc.sync.dma_start(offsets[LAST][:], offs3)
        for q in range(QUADS):
            load_table_planes(nc.sync, q)
        load_words(table_words[0], tab_words[0])
        nc.sync.dma_start(offsets[FIRST][:], offs2)
        load_words(w3_codes[0], w3_words[0])
        load_weight_planes(w3_planes, w3_scales, range(QUADS))
        load_words(table_words[1], tab_words[1])
        load_words(w3_codes[1], w3_words[1])
        nc.sync.dma_start(out=w2_codes[:], in_=w2_words.rearrange("a p e -> p a e").bitcast(I32))
        load_weight_planes(w2_planes, w2_scales, range(QUADS))
        load_w1(0)

        own_rows = gather_own_rows()
        identity = kept([P, P], F32, "identity")
        make_identity(nc, identity[:])
        gather_scales(LAST, 0, EARLY)
        gather_words(LAST, 0, 0, pairs=2)
        gather_first_scales(nc.sync, 0)
        load_w1(1)
        load_w1(2)
        load_w1(3)
        move_own_rows(own_rows, range(5))
        gather_words(FIRST, 0, 0)
        gather_words(LAST, 1, 0)
        gather_words(LAST, 1, 1)
        gather_words(FIRST, 0, 1)
        gather_words(FIRST, 1, 0, pairs=2)
        for a in range(PASSES):
            for u in tiles_of(0) + tiles_of(1):
                cited_pass(LAST, u, a)
        stage(LAST, *tiles_of(0))
        stage(LAST, *tiles_of(1))
        for u in range(3):
            cited_pass(FIRST, u, 0)
        cited_pass(FIRST, 0, 1)
        cited_pass(FIRST, 1, 1)
        cited_pass(FIRST, 2, 1)
        cited_pass(FIRST, 3, 1, first=1)
        cited_pass(FIRST, 3, 0, first=1)
        stage(FIRST, 0, 1, 2, 3)

        gather_passes(LAST, 2)
        gather_first_scales(nc.sync, HALF)
        move_own_rows(own_rows, range(5, 8))
        for t in range(PACK):
            nc.sync.dma_start(out=w4_raw[:, t, :], in_=w4.rearrange("(g t i) n -> t g i n", t=PACK, i=RUN)[t])
        nc.sync.dma_start(out=bias[:], in_=b.rearrange("(m e) -> m e", e=2))
        gather_passes(FIRST, 2)
        gather_passes(OWN, 0)
        round_w1_on_gpsimd(0, PACK)
        round_w1_on_gpsimd(1, PACK)
        round_w1_on_gpsimd(2, SHARE)
        round_w1_on_gpsimd(3, SHARE)
        cited_products(LAST, 2)
        differences(0, 1)
        stage(LAST, 4, 5)
        w1_bf16[1, SHARE] = scalar_tile([P, (PACK - SHARE) * H], BF16, "w1_bf16_rest")
        round_w1_on_scalar(3, SHARE)
        round_w1_on_scalar(2, SHARE)
        gather_scales(LAST, EARLY, S - EARLY)
        quantize_w1(1, SHARE)
        quantize_w1(1, 0)
        quantize_w1(0, 0)
        round_w4()
        gather_passes(OWN, 1)
        gather_passes(LAST, 3)
        gather_passes(FIRST, 3)
        gather_passes(OWN, 2)
        gather_scales(OWN, EARLY, S - EARLY)
        gather_passes(OWN, 3)

        differences(2, 3)
        absolute_values(0, 1)
        cited_products(FIRST, 2, first=1)
        absolute_values(2, 3)
        for a in (1, 0):
            for u in tiles_of(0):
                own_pass(u, a)
        stage(FIRST, 4, 5)
        for u in tiles_of(0):
            copy_own(u)
            add_on_gpsimd(u)
        differences(4, 5)
        own_product(2)
        own_product(3)
        absolute_values(4, 5)
        for u in tiles_of(1):
            copy_own(u)
            add_on_gpsimd(u)
        cited_products(LAST, 3)
        cited_products(FIRST, 3, first=1)
        stage(LAST, 6, 7)
        stage(FIRST, 6, 7)
        relu_on_scalar(0)
        own_product(4)
        own_product(5)
        differences(6, 7)
        absolute_values(6, 7)

        second_last, last = tiles_of(PAIRS - 1)
        add_on_vector(4)
        add_on_vector(5)
        quantize_w4()
        relu_on_vector(PAIR, PAIR)
        quantize_h(0, PAIR)
        relu_on_vector(2 * PAIR, PAIR)
        own_product(second_last)
        finish_pair(0)
        own_product(last)
        quantize_h(PAIR, PAIR)
        quantize_h(2 * PAIR, PAIR)
        finish_pair(1)
        add_on_vector(second_last)
        finish_pair(2)
        add_on_vector(last)
        for u in tiles_of(PAIRS - 1):
            relu_on_vector(u * TILE, TILE)
        for u in tiles_of(PAIRS - 1):
            quantize_h(u * TILE, TILE)
        finish_tile(second_last, add_bias_on_scalar)
        finish_tile(last, add_bias_on_vector)
